import numpy as np, ml_dtypes
CORES = [16,18,20,22]
N = 4
BF = ml_dtypes.bfloat16
def gentries(a):
    return np.ascontiguousarray(a.reshape(8, 16, -1).transpose(0, 2, 1)).reshape(8, -1)
def gtable(e):
    e = np.asarray(e); return np.ascontiguousarray(e.reshape(8, -1, 16).transpose(0, 2, 1)).reshape(128, -1).astype(np.int32)
I, W, PL, RO, CNT, B, AS = 256, 4096, 4096, 6, 12, 64, 64
def records(x, s):
    return np.take_along_axis(x, s.transpose(0, 1, 3, 2).reshape(N, 8, 1, 16 * I), 3).reshape(N, 8, 16, I, 16)
def dist(xs, z):
    return np.sum(np.abs(xs - z[..., None]), axis=2).transpose(0, 1, 3, 2)
def parts(rng):
    x = (256 * rng.random((N, 8, 16, W)) * rng.choice(np.array([1.0, 1.0, 0.5, 0.25]), (N, 8, 1, W))).astype(np.int64)
    z = rng.integers(0, 256, (N, 8, 16, I)); f = rng.integers(0, 256, (N, 8, 16, I))
    s = rng.integers(0, W, (N, 8, 16, I)); pl = rng.integers(0, W, (N, 8, 16, PL)); p = rng.integers(0, PL, (N, 8, I))
    th = rng.integers(300, 1300, (N, 8, 1, I)) + rng.integers(0, 200, (N, 8, 16, I))
    return x, z, f, s, pl, p, th
def pack(x, z, f, s, pl, p, th):
    return {"x0": x.reshape(N, 128, W).astype(np.float32).astype(BF), "z0": z.reshape(N, 128, I).astype(np.float32).astype(BF), "f0": f.reshape(N, 128, I).astype(np.float32).astype(BF),
            "s0": s.reshape(N, 128, I).astype(np.int32), "pl": pl.reshape(N, 128, PL).astype(np.int32), "p0": np.stack([gtable(a) for a in p]), "th": th.reshape(N, 128, I).astype(np.int32)}
def setup_inputs(rng):
    return pack(*parts(rng))
def setup_inputs_spread(rng):
    x = (np.exp2(8 * rng.random((N, 8, 1, W))) * rng.random((N, 8, 16, W))).astype(np.int64)
    z = (np.exp2(8 * rng.random((N, 8, 1, I))) * rng.random((N, 8, 16, I))).astype(np.int64)
    f = (np.exp2(8 * rng.random((N, 8, 1, I))) * rng.random((N, 8, 16, I))).astype(np.int64)
    s = (W * rng.random((N, 8, 16, I)) ** 3).astype(np.int64); pl = (W * rng.random((N, 8, 16, PL)) ** 2).astype(np.int64); p = (PL * rng.random((N, 8, I)) ** 3).astype(np.int64)
    th = np.minimum((np.exp2(5 + 7 * rng.random((N, 8, 1, I))) * (0.5 + 0.5 * rng.random((N, 8, 16, I)))).astype(np.int64), 4080)
    return pack(np.minimum(x, 255), np.minimum(z, 255), np.minimum(f, 255), np.minimum(s, W - 1), np.minimum(pl, W - 1), np.minimum(p, PL - 1), th)
def setup_inputs_ends(rng):
    def mix(n):
        return np.where(rng.random((N, 8, 1, n)) < 0.5, rng.integers(0, 2, (N, 8, 16, n)), rng.integers(0, 2, (N, 8, 1, n)))
    x = 255 * mix(W); z = 255 * mix(I); f = 255 * mix(I); th = 4080 * mix(I)
    s = (W - 1) * rng.integers(0, 2, (N, 8, 16, I)); pl = (W - 1) * rng.integers(0, 2, (N, 8, 16, PL)); p = (PL - 1) * rng.integers(0, 2, (N, 8, I))
    x[:, 1::2, :, W - 1] = 255; x[:, 1::2, :, 0] = 0; x[:, 0:4:2, :, W - 1] = 0; x[:, 0:4:2, :, 0] = 255
    pl[:, 7, :, PL - 1] = W - 1; pl[:, 7, :, 0] = 0; pl[:, 7, 0, 768] = 0
    for i in (0, 1, I - 2, I - 1):
        z[:, 7, :, i] = 0; f[:, 7, :, i] = 0; s[:, 7, :, i] = W - 1; th[:, 7, :, i] = 4080; p[:, 7, i] = PL - 1
    for i in (2, 3, I - 4, I - 3):
        z[:, 7, :, i] = 255; f[:, 7, :, i] = 255; s[:, 7, :, i] = 0; th[:, 7, :, i] = 4080; p[:, 7, i] = 0
    return pack(x, z, f, s, pl, p, th)
def setup_inputs_ties(rng):
    x, z, f, s, pl, p, th = parts(rng)
    x = 64 * rng.integers(0, 4, (N, 8, 16, W)); z = 64 * rng.integers(0, 4, (N, 8, 16, I))
    few = np.take_along_axis(rng.integers(0, W, (N, 8, 3, I)), rng.integers(0, 3, (N, 8, 16, I)), 2)
    s = np.where(rng.random((N, 8, 1, I)) < 0.5, few, s)
    ds = dist(records(x, s), z); dp = dist(records(x, np.take_along_axis(pl, p[:, :, None, :], 3)), z)
    one = (rng.random((N, 8, 16, I)) < 0.08).astype(np.int64); k = rng.integers(0, 3, (N, 8, 1, I))
    th = np.where(k == 0, ds + one, np.where(k == 1, np.minimum(dp + one, ds), np.minimum(dp, ds)))
    return pack(x, z, f, s, pl, p, np.minimum(th, 4080))
def setup_inputs_odd(rng):
    x, z, f, s, pl, p, th = parts(rng); h = W // 2
    o = np.argsort(rng.random((N, 8, W)), axis=-1)
    hi = np.zeros((N, 8, W), np.int64); np.put_along_axis(hi, o[:, :, h:], 1, 2)
    x = rng.integers(0, 56, (N, 8, 16, W)) + 200 * hi[:, :, None, :]; x[:, :, 15] ^= np.sum(x, axis=2) & 1
    kz = rng.integers(0, 2, (N, 8, 1, I)); z = rng.integers(0, 56, (N, 8, 16, I)) + 200 * kz; z[:, :, 15] ^= (np.sum(z, axis=2) & 1) ^ 1
    s = np.take_along_axis(o, (rng.integers(0, h, (N, 8, 16, I)) + h * (1 - kz)).reshape(N, 8, 16 * I), 2).reshape(N, 8, 16, I)
    pl = np.take_along_axis(o, (rng.integers(0, h, (N, 8, 16, PL)) + h * (np.arange(PL) & 1)).reshape(N, 8, 16 * PL), 2).reshape(N, 8, 16, PL)
    p = 2 * rng.integers(0, PL // 2, (N, 8, I)) + 1 - kz[:, :, 0]
    x[:, :, :, W - 1] = 255; x[:, ::2, :, W - 3] = 0; x[:, 1::2, :, 1] = 0
    pl[:, :, 0, PL - 1] = W - 1; pl[:, ::2, 0, 0] = W - 3; pl[:, 1::2, 0, 0] = 1
    ds = dist(records(x, s), z); dp = dist(records(x, np.take_along_axis(pl, p[:, :, None, :], 3)), z)
    one = (rng.random((N, 8, 16, I)) < 0.08).astype(np.int64); k = rng.integers(0, 3, (N, 8, 1, I))
    th = np.where(k == 0, ds + one, np.where(k == 1, np.minimum(dp + one, ds), np.minimum(dp, ds)))
    th = np.minimum(th, 4080)
    for i in (0, 1, I - 2, I - 1):
        z[:, :, :, i] = 0; f[:, :, :, i] = 0; s[:, :, 0, i] = W - 1; p[:, :, i] = PL - 1; th[:, :, :, i] = 0; th[:, :, 0, i] = 4080
    return pack(x, z, f, s, pl, p, th)
def setup_inputs_corners(rng):
    x, z, f, s, pl, p, th = parts(rng)
    k = rng.integers(0, 8, (N, 8, I)); k[:, :, I - 8:] = np.arange(8); k = k[:, :, None, :]; row = np.arange(16)[:, None]
    th = 4080 * ((((k == 1) | (k == 4) | (k == 5)) & (row == 15)) | ((k == 2) & (row == 0)) | (k == 3)).astype(np.int64)
    th = np.where(k == 7, rng.integers(0, 4081, (N, 8, 16, I)), th)
    z = np.where(k == 4, 255, np.where((k == 5) | (k == 7) | ((k == 0) & (rng.random((N, 8, 1, I)) < 0.5)), 0, z))
    z = np.where(k == 6, np.where(row == 1, 100, 15), z)
    s = np.where(k == 2, (W - 1) * rng.integers(0, 2, s.shape), s); s = np.where(k == 3, rng.integers(0, W, (N, 8, 1, I)), s)
    s = np.where(k == 7, 16 * np.arange(I) + rng.integers(0, 16, s.shape), s); s = np.where((k == 5) & (row == 15), W - 1, s)
    x[:, :, :, W - 1] = 255
    pl[:, :, :, 0] = rng.integers(0, W - 1, (N, 8, 1)); pl[:, :, :, PL - 1] = W - 1; pl[:, :, 15, :] = rng.integers(0, W - 1, (N, 8, PL))
    e = rng.integers(0, 4, (N, 8, I)); p = np.where(e == 0, 0, np.where(e == 1, PL - 1, p))
    return pack(x, z, f, s, pl, p, th)
def check_inputs(d):
    bad = []
    for k, lo, hi in (("x0", 0, 255), ("z0", 0, 255), ("f0", 0, 255), ("s0", 0, W - 1), ("pl", 0, W - 1), ("p0", 0, PL - 1), ("th", 0, 4080)):
        v = np.asarray(d[k]).astype(np.float64)
        if not np.all((v >= lo) & (v <= hi) & (v == np.floor(v))): bad.append("range of " + k)
    return bad
def reference(x0, z0, f0, s0, pl, p0, th):
    X = x0.astype(np.float32).astype(np.int32).reshape(N, 8, 16, W); z = z0.astype(np.float32).astype(np.int32).reshape(N, 8, 16, I); f = f0.astype(np.float32).astype(np.int32).reshape(N, 8, 16, I)
    S = s0.astype(np.int32).reshape(N, 8, 16, I); plans = pl.astype(np.int32).reshape(N, 8, 16, PL); lim = th.astype(np.int32).reshape(N, 8, 16, I)
    P = np.stack([gentries(a) for a in p0]).astype(np.int32); A = np.zeros((N, 8, I), np.int32)
    row = np.arange(16)[:, None]; wt = (2 * np.arange(16) + 1)[:, None]
    for t in range(RO):
        e = np.take_along_axis(plans, P[:, :, None, :], 3)
        xs = records(X, S); xe = records(X, e); bound = lim + AS * A[:, :, None, :]
        rs = dist(xs, z) < bound; rp = dist(xe, z) < bound
        c1 = np.any(rs, axis=2); c2 = ~c1 & np.any(rp, axis=2); c3 = ~c1 & ~c2
        j = np.argmax(rs, axis=2); jp = np.argmax(rp, axis=2)
        u = np.sum(wt * z, axis=2) & 4095; A = A + c3; P = np.where(c3, ((u * u >> 5) + 37 * u) & (PL - 1), P).astype(np.int32)
        low = np.sum(xs <= z[..., None], axis=2).transpose(0, 1, 3, 2)
        R = np.where(c1[:, :, None, :] & (low >= CNT) & (row != j[:, :, None, :]), e, S)
        t1 = np.take_along_axis(S, j[:, :, None, :], 2)[:, :, 0]; t2 = np.take_along_axis(e, jp[:, :, None, :], 2)[:, :, 0]; t3 = np.take_along_axis(plans[:, :, 0], P, 2)
        top = np.where(c1, t1, np.where(c2, t2, t3)); last = np.where(c1, j, 15)
        S = np.where(row <= last[:, :, None, :], np.concatenate([top[:, :, None, :], R[:, :, :15]], axis=2), R).astype(np.int32)
        f = (f + z) >> 1
        y = np.abs(np.take_along_axis(X, S[:, :, :1, :], 3) - f)
        place = 16 * np.arange(I) + (np.sum(y, axis=2) & 15)
        np.put_along_axis(X, place[:, :, None, :], (y + z) >> 1, 3)
        if t < RO - 1:
            z = np.concatenate([np.roll(y[..., b * B:(b + 1) * B], b + t, axis=0) for b in range(N)], axis=3)
    yx = np.sum(X.reshape(N, 8, 16, I, 16) * np.arange(1, 17), axis=4)
    return {"ys": S.reshape(N, 128, I).astype(np.float32), "yp": np.stack([gtable(a) for a in P + PL * A]).astype(np.float32),
            "yf": f.reshape(N, 128, I).astype(np.float32).astype(BF), "yx": yx.reshape(N, 128, I).astype(np.float32)}

@@ -1,0 +1,721 @@
+from concourse.mybir import dt, AluOpType, ActivationFunctionType
+
+NT, NA, NR = 6, 256, 4096
+N = 64
+NP = NA // N
+
+SCRATCH = {}
+for _nm, _sh, _ty in (
+        ("X", 4096, "bfloat16"), ("PL", 4096, "int32"), ("Z", NT * NA, "bfloat16"), ("Y", NT * NA, "bfloat16"),
+        ("ZE", 2 * NR, "bfloat16"), ("DS", 2 * NR, "bfloat16"), ("DE", 2 * NR, "bfloat16"),
+        ("AS", 2 * NR, "bfloat16"), ("AE", 2 * NR, "bfloat16"), ("LW", 2 * NR, "bfloat16"),
+        ("TH", NA, "int32"), ("S0", NA, "int32"), ("P0", 16, "int32"), ("F0", NA, "bfloat16"),
+        ("S16", 7 * NA, "float16"), ("SU", 7 * NA, "uint16"), ("E16", 7 * NA, "float16"), ("EU", 7 * NA, "uint16"),
+        ("EH", NT * NA, "float16"), ("F16", 7 * NA, "float16"), ("RR", 4 * NA, "bfloat16"), ("WW", 8 * NA, "float16"),
+        ("TRT", 8 * 128, "float32"), ("TRY", 8 * 128, "float32"), ("LST", NT * 16, "uint16"), ("YD", NT * NA, "float32"),
+        ("PI1", NT * 16, "int32"), ("PI2", NT * 16, "int32"), ("PI3", NT * 16, "int32"), ("PLC", NT * 16, "uint16"),
+        ("XN", NT * NA, "int32"), ("HB", NT * NA, "bfloat16"), ("QB", NT * NA, "bfloat16"), ("SW", NT * NA, "bfloat16"), ("FM", NT * NA, "bfloat16"),
+        ("SE", 4 * NA, "float16"), ("MM", 4 * NA, "float16"),
+        ("U1", NT * 16, "int32"), ("U2", NT * 16, "int32"), ("U3", NT * 16, "int32"), ("U4", NT * 16, "int32"),
+        ("U5", NT * 16, "int32"), ("U6", NT * 16, "int32"), ("UH", NT * 16, "int32"), ("UU", NT * 16, "uint16"), ("PU", 16, "uint16"),
+        ("PF", 7 * 16, "float32"), ("PA", 7 * 16, "float32"), ("PD", 7 * 16, "float32"), ("PM", 7 * 16, "float32"), ("YPO", 16, "float32"),
+        ("YSO", NA, "float32"), ("YFO", NA, "bfloat16"), ("YXO", NA, "float32"),
+        ("IOC", 144, "float32"), ("PC", 1, "float32"), ("PI", 1, "int32"), ("IOB", 16, "int32"), ("BASE", 16, "int32"),
+        ("PG", 1, "int32"), ("PK", 1, "int32"), ("PH", 1, "int32"), ("PO", 1, "int32"), ("C0F", 1, "float32"), ("C15F", 1, "float32"), ("W2", 1, "float32"),
+        ("K16", 1, "float32"), ("R0", 1, "float32"), ("D0F", 1, "float32"), ("D31F", 1, "float32"), ("ODC", 1, "float32"), ("EVC", 1, "float32"),
+        ("CA", 128, "float32"), ("CB", 128, "float32"), ("OB", 128, "float32"), ("LF", 128, "float32"), ("IFF", 128, "float32"), ("PB", 128, "float32"),
+        ("T1", 128, "float32"), ("T2", 128, "float32"),
+        ("BIG", 144, "bfloat16"), ("BIGW", 144, "bfloat16"), ("BIG2", 144, "bfloat16"), ("BIGN", 144, "bfloat16"), ("BIG0B", 144, "bfloat16"), ("BIG16", 144, "float16"),
+        ("ONESB", 128, "bfloat16"), ("N4", 128, "bfloat16"), ("EV", 128, "float16"), ("OD", 128, "float16"), ("EV0", 128, "float16"), ("OD0", 128, "float16"),
+        ("EVB", 128, "bfloat16"), ("ODB", 128, "bfloat16"),
+        ("IB", 128, "bfloat16"), ("NIB", 128, "bfloat16"), ("I16", 128, "float16"), ("NI16", 128, "float16"), ("K4", 128, "bfloat16"), ("N64", 128, "bfloat16"),
+        ("A17", 128, "bfloat16"), ("N34", 128, "bfloat16"), ("PQ", 128, "bfloat16"), ("NQ", 128, "bfloat16"), ("G1", 128, "bfloat16"), ("NL", 128, "bfloat16"), ("NK4", 128, "bfloat16"),
+        ("SHI", 128, "float16"), ("R00", 128, "float16"), ("R0K", 128, "bfloat16"), ("ONE", N, "bfloat16"), ("CI", 2048, "bfloat16")):
+    SCRATCH[_nm] = ("sbuf", [128, _sh], _ty)
+for _k in range(8):
+    SCRATCH["ps%d" % _k] = ("psum", [128, 16, 32] if _k in (4, 5) else [128, 512], "float32")
+
+LOADS = ["lz", "lx", "ls", "lf", "lp", "lpl", "lt"]
+STORES = ["ost%d" % k for k in range(4)]
+SEMAPHORES = ["cv", "cs", "ct", "cg", "lsent"] + LOADS + STORES + ["za%d%d" % (t, b) for t in range(1, NT) for b in range(4)]
+
+A = AluOpType
+AF = ActivationFunctionType
+BYTES2 = {k for k, v in SCRATCH.items() if v[2] in ("bfloat16", "float16", "uint16")}
+QS = {"V": "cv", "S": "cs", "P": "ct", "G": "cg"}
+
+EST = dict(g=1.55, sc=3.0, v=0.00083 * 1.2, pe=0.00042 * 1.2, vo=0.0, so=0.06, lat=0.12, self_=0.08, net=2.6)
+OPT = dict(ep="SSVS", ea="SSSS", sa="SSSS", ep0="SVVV", gh=(1, 1, 1, 1), ah=(1, 1, 1, 1), ze0="SSSSSSSSGGGGVVVV", ze=("SSSSGGGGGGVVVVVV", "GG" + "V" * 14), lw="VVSV", up=(1, 1, 1, 0), s7=(7, 6, 7, 6), tops=((0, 1), (2,), (3,)), places=((0, 1), (2, 3)))
+
+
+PRIO = {'PI1': -0.1, 'U6': 1.6, 'psDs': 0.5, 'PA': -1.9, 'C0': 0.8, 'PF': 1.3, 'PK': 1.2, 'BIG': -1.0, 'EH': -1.3, 'D0': -1.2, 'MM': -0.0,
+        'PG': 1.0, 'PM': -1.8, 'ODC': 1.1, 'N34': 0.1, 'YP': 1.9, 'U2': 0.3, 'PU': 1.0, 'RP': 0.4, 'lf': 1.3, 'psS': 0.1, 'LST': -0.3,
+        'S16': 0.5, 'U4': -0.6, 'psE': -1.7, 'lz': 1.4, 'PI3': 0.5, 'OD': -0.2, 'BIGW': 0.4, 'SU': 0.3, 'SHI': -1.0, 'pi': 0.3,
+        'A17': -1.7, 'S160': -1.7, 'XN': -0.2, 'stys': -1.1, 'ioc': -1.2}
+
+
+def Rf(buf, lo, hi, st=1):
+    return (buf, lo, hi, st)
+
+
+def R3(buf, lo, hi, h=None):
+    return (buf, lo, hi, 1, h)
+
+
+def cnt(r):
+    k = (r[2] - r[1] + r[3] - 1) // r[3]
+    return k // 2 if len(r) == 5 and r[4] is not None else k
+
+
+def isref(x):
+    return isinstance(x, tuple)
+
+
+def ind(win, off):
+    return ("#", win, off)
+
+
+def duration(q, ins):
+    e = EST
+    d = 0.0
+    for m, kw in ins:
+        if m == "matmul":
+            d += max(64, cnt(kw["rhs"])) * e["pe"]
+            continue
+        if m == "iota":
+            d += 0.3
+            continue
+        if m == "affine":
+            d += 0.17 + 2 * cnt(kw["in_"]) * e["v"]
+            continue
+        refs = [v for v in kw.values() if isref(v)]
+        gat = [k for k, v in kw.items() if isref(v) and v[0] == "#"]
+        if gat:
+            n = 16 * cnt(kw[gat[0]][2])
+            d += 0.06 + n * e["v"] * (e["sc"] if gat[0] == "out" else e["g"])
+        elif q == "S":
+            d += e["so"] + cnt(kw["out"]) * e["v"]
+        else:
+            o = kw.get("out", kw.get("ap"))
+            n = cnt(o)
+            big = [v for v in refs if cnt(v) == n]
+            c = 1.0
+            if m in ("tensor_copy", "tensor_scalar", "memset") and all(v[0] in BYTES2 for v in big):
+                c = 0.5
+            if m == "tensor_tensor" and not any(v[0][:2] == "ps" for v in refs):
+                c = 2.0
+            d += e["vo"] + max(64, n * c) * e["v"]
+    return d
+
+
+def touches(ins):
+    rd, wr = [], []
+    for m, kw in ins:
+        for k, v in kw.items():
+            if not isref(v):
+                continue
+            if v[0] == "#":
+                (wr if k == "out" else rd).append(v[1])
+                rd.append(v[2])
+            elif k in ("out", "ap"):
+                wr.append(v)
+            else:
+                rd.append(v)
+    return rd, wr
+
+
+def meet(a, b):
+    if not (a[0] < b[1] and b[0] < a[1]):
+        return False
+    return not (a[2] == b[2] and a[2] > 1 and (a[0] - b[0]) % a[2])
+
+
+def add(P, q, name, ins, rd=None, wr=None, dur=None, sem=None, inc=1, extra=None, prio=0.0):
+    r, w = touches(ins)
+    r += rd or []
+    w += wr or []
+    T = {"i": len(P["tasks"]), "q": q, "name": name, "ins": ins, "sem": sem, "inc": inc, "prio": prio,
+         "dur": duration(q, ins) if dur is None else dur, "pre": {}, "banks": []}
+    hist = P["last"]
+
+    def dep(o, kind):
+        old = T["pre"].get(o)
+        if old is None or kind == "raw":
+            T["pre"][o] = kind
+    seen = {}
+    for a, lst in (("r", r), ("w", w)):
+        for ref in lst:
+            seen.setdefault((ref[0], ref[1], ref[2], ref[3]), set()).add(a)
+    for (buf, lo, hi, st), accs in seen.items():
+        if buf[:2] == "ps" and buf not in T["banks"]:
+            T["banks"].append(buf)
+        for (o, oq, oa, oset) in hist.get(buf, ()):
+            over = meet((lo, hi, st), oset)
+            if over and "w" in accs and "w" not in oa:
+                dep(o, "war")
+            elif over and ("w" in accs or "w" in oa):
+                dep(o, "raw")
+    for (buf, lo, hi, st), accs in seen.items():
+        h = hist.setdefault(buf, [])
+        if "w" in accs and st == 1:
+            h[:] = [e for e in h if not (lo <= e[3][0] and e[3][1] <= hi)]
+        h.append((T["i"], q, accs, (lo, hi, st)))
+    for o in extra or []:
+        dep(o, "time")
+    T["up"] = P.get("up", 0.0)
+    P["tasks"].append(T)
+    return T["i"]
+
+
+def mm(out, lhsT, rhs, start, stop):
+    return ("matmul", dict(out=out, lhsT=lhsT, rhs=rhs, start=start, stop=stop))
+
+
+def acc(out, pairs):
+    k = len(pairs)
+    return [mm(out, l, r, i == 0, i == k - 1) for i, (l, r) in enumerate(pairs)]
+
+
+def ts(out, in0, s1, op0, s2=None, op1=None):
+    kw = dict(out=out, in0=in0, scalar1=s1, scalar2=s2, op0=op0)
+    if op1 is not None:
+        kw["op1"] = op1
+    return [("tensor_scalar", kw)]
+
+
+def tt(out, in0, in1, op):
+    return [("tensor_tensor", dict(out=out, in0=in0, in1=in1, op=op))]
+
+
+def cp(out, in_):
+    return [("tensor_copy", dict(out=out, in_=in_))]
+
+
+def act(out, in_, f, bias=0.0, scale=1.0):
+    return [("activation", dict(out=out, in_=in_, func=f, bias=bias, scale=scale))]
+
+
+def tr(out, in_):
+    return [("vtranspose", dict(out=out, in_=in_))]
+
+
+def M(name):
+    return Rf(name, 0, 128)
+
+
+def sel(m, name="BIG"):
+    return Rf(name, 15 - m, 143 - m)
+
+
+ORDER = {0: (2, 3, 1, 0), 1: (2, 1, 0, 3), 2: (0, 1, 3, 2), 3: (0, 3, 2, 1), 4: (2, 3, 1, 0), 5: (2, 1, 0, 3)}
+
+
+def build():
+    P = {"tasks": [], "last": {}}
+    c1 = lambda n: Rf(n, 0, 1)
+    C = lambda n: Rf(n, 0, 128)
+    B = lambda n: Rf(n, 0, 144)
+    def load(q, sem, ref, dur, src):
+        return add(P, q, sem, [("dma", dict(out=ref, src=src + (1,)))], dur=0.1, sem=sem, inc=16, prio=dur)
+    load("Y", "ls", Rf("S0", 0, NA), 2.2, ("s0", 0, NA))
+    load("Y", "lz", Rf("Z", 0, NA), 2.2, ("z0", 0, NA))
+    load("Y", "lx", Rf("X", 0, NR), 7, ("x0", 0, NR))
+    load("S", "lp", Rf("P0", 0, 16), 2.5, ("p0", 0, 16))
+    load("S", "lf", Rf("F0", 0, NA), 2.5, ("f0", 0, NA))
+    load("Y", "lt", Rf("TH", 0, NA), 8, ("th", 0, NA))
+    load("Y", "lpl", Rf("PL", 0, NR), 17, ("pl", 0, NR))
+    io = lambda nm, ref, pat, ch: add(P, "G", nm, [("iota", dict(out=ref, pattern=pat, base=0, channel_multiplier=ch))])
+    io("ioc", B("IOC"), [[1, 144]], 0)
+    io("pc", c1("PC"), [[1, 1]], 1)
+    io("pi", c1("PI"), [[1, 1]], 1)
+    io("iob", Rf("IOB", 0, 16), [[0, 4], [256, 4]], 0)
+    V = lambda nm, ins, **k: add(P, "V", nm, ins, **k)
+    S = lambda nm, ins, **k: add(P, "S", nm, ins, **k)
+    PE = lambda nm, ins, **k: add(P, "P", nm, ins, **k)
+    V("PG", ts(c1("PG"), c1("PI"), 4, A.arith_shift_right))
+    V("PH", ts(c1("PH"), c1("PI"), 5, A.arith_shift_right))
+    V("PK", ts(c1("PK"), c1("PI"), 15, A.bitwise_and))
+    V("PO", ts(c1("PO"), c1("PG"), 1, A.bitwise_and))
+    V("C15", ts(c1("C15F"), c1("PG"), 16.0, A.mult, 15.0, A.add))
+    V("BIG", ts(B("BIG"), B("IOC"), c1("C15F"), A.is_equal))
+    V("C0", ts(c1("C0F"), c1("PG"), 16.0, A.mult))
+    V("D0", ts(c1("D0F"), c1("PH"), 32.0, A.mult))
+    V("D31", ts(c1("D31F"), c1("PH"), 32.0, A.mult, 31.0, A.add))
+    V("ODC", ts(c1("ODC"), c1("PO"), 1.0, A.mult))
+    V("EVC", ts(c1("EVC"), c1("PO"), 0.0, A.is_equal))
+    V("W2", ts(c1("W2"), c1("PK"), 2.0, A.mult, 1.0, A.add))
+    V("K16", ts(c1("K16"), c1("PK"), 16.0, A.mult))
+    V("R0", ts(c1("R0"), c1("PK"), 0.0, A.is_equal))
+    V("BASE", ts(Rf("BASE", 0, 16), Rf("IOB", 0, 16), c1("K16"), A.add))
+    V("BIGW", ts(B("BIGW"), B("BIG"), c1("W2"), A.mult))
+    V("BIG2", ts(B("BIG2"), B("BIG"), 2.0, A.mult))
+    V("BIGN", ts(B("BIGN"), B("BIG"), -1.0, A.mult))
+    V("BIG0B", ts(B("BIG0B"), B("BIG"), c1("R0"), A.mult))
+    V("BIG16", ts(B("BIG16"), B("BIG"), 1.0, A.mult))
+    V("CA", ts(C("CA"), C("IOC"), c1("C0F"), A.is_ge))
+    V("CB", ts(C("CB"), C("IOC"), c1("C15F"), A.is_le))
+    V("OB", tt(C("OB"), C("CA"), C("CB"), A.mult))
+    V("IFF", ts(C("IFF"), C("IOC"), c1("PC"), A.is_equal))
+    V("T1", ts(C("T1"), C("IOC"), c1("PC"), A.is_gt))
+    V("LF", tt(C("LF"), C("T1"), C("CB"), A.mult))
+    V("IB", ts(C("IB"), C("IFF"), 1.0, A.mult))
+    V("NIB", ts(C("NIB"), C("IFF"), -1.0, A.mult))
+    V("I16", ts(C("I16"), C("IFF"), 1.0, A.mult))
+    V("NI16", ts(C("NI16"), C("IFF"), -1.0, A.mult))
+    V("T2", tt(C("T2"), C("IFF"), C("LF"), A.subtract))
+    V("G1", ts(C("G1"), C("T2"), 4096.0, A.mult))
+    V("N4", ts(C("N4"), C("OB"), -4096.0, A.mult))
+    V("K4", ts(C("K4"), C("IFF"), 4096.0, A.mult))
+    V("ONESB", ts(C("ONESB"), C("OB"), 1.0, A.mult))
+    V("PBa", ts(C("T1"), C("IOC"), c1("D0F"), A.is_ge))
+    V("PBb", ts(C("T2"), C("IOC"), c1("D31F"), A.is_le))
+    V("PB", tt(C("PB"), C("T1"), C("T2"), A.mult))
+    V("EV", ts(C("EV"), C("PB"), c1("EVC"), A.mult))
+    V("OD", ts(C("OD"), C("PB"), c1("ODC"), A.mult))
+    V("EV0", ts(C("EV0"), C("PB"), c1("EVC"), A.mult, c1("R0"), A.mult))
+    V("OD0", ts(C("OD0"), C("PB"), c1("ODC"), A.mult, c1("R0"), A.mult))
+    V("EVB", ts(C("EVB"), C("PB"), c1("EVC"), A.mult))
+    V("ODB", ts(C("ODB"), C("PB"), c1("ODC"), A.mult))
+    V("ONE", [("memset", dict(ap=Rf("ONE", 0, N), constant=1.0))])
+    V("A17", ts(C("A17"), C("OB"), 17.0, A.mult))
+    V("N34", ts(C("N34"), C("OB"), -34.0, A.mult))
+    V("PQ", ts(C("PQ"), C("IFF"), 2048.0, A.mult))
+    V("NQ", ts(C("NQ"), C("IFF"), -2048.0, A.mult))
+    V("NL", ts(C("NL"), C("LF"), -4096.0, A.mult))
+    V("NK4", ts(C("NK4"), C("IFF"), -4096.0, A.mult))
+    V("SHa", ts(C("T1"), C("IOC"), -1.0, A.add, c1("PC"), A.is_equal))
+    V("SHb", tt(C("T2"), C("T1"), C("CB"), A.mult))
+    V("SHI", tt(C("SHI"), C("T2"), C("IFF"), A.subtract))
+    V("R00", ts(C("R00"), C("IFF"), c1("R0"), A.mult))
+    V("R0K", ts(C("R0K"), C("R00"), 65536.0, A.mult))
+    V("N64", ts(C("N64"), C("IFF"), -64.0, A.mult))
+    for p in range(NP):
+        a = p * N
+        V("SU0", cp(Rf("SU", a, a + N), Rf("S0", a, a + N)))
+    V("S160", ts(Rf("S16", 0, NA), Rf("S0", 0, NA), -2048.0, A.add))
+    V("F160", ts(Rf("F16", 0, NA), Rf("F0", 0, NA), 1024.0, A.add))
+    V("PU", cp(Rf("PU", 0, 16), Rf("P0", 0, 16)))
+    V("PF0", cp(Rf("PF", 0, 16), Rf("P0", 0, 16)))
+    V("PA0", [("memset", dict(ap=Rf("PA", 0, 16), constant=0.0))])
+    Xa = Rf("X", 0, NR)
+    I16, IB = M("I16"), M("IB")
+    for t in range(NT):
+        last = t == NT - 1
+        o = t * NA
+        par = t % 2
+        zc = lambda a, b, s=1, o=o: Rf("Z", o + a, o + b, s)
+        ordr = ORDER[t]
+        loc = (-t) % 4
+        k0, k1 = t * 16, t * 16 + 16
+        U = lambda nm: Rf(nm, t * 16, t * 16 + 16)
+
+        def hash_():
+            PE("psU", acc(Rf("ps6", 448, 464), [(sel(m, "BIGW"), zc(m, NA, 16)) for m in range(16)]))
+            V("U1", cp(U("U1"), Rf("ps6", 448, 464)))
+            V("U2", ts(U("U2"), U("U1"), 4095, A.bitwise_and))
+            V("U3", tt(U("U3"), U("U2"), U("U2"), A.mult))
+            V("U5", ts(U("U5"), U("U2"), 37.0, A.mult))
+            V("U4", ts(U("U4"), U("U3"), 5, A.arith_shift_right))
+            V("U6", tt(U("U6"), U("U4"), U("U5"), A.add))
+            V("UH", ts(U("UH"), U("U6"), 4095, A.bitwise_and))
+            V("UU", cp(U("UU"), U("UH")))
+            V("EH", ts(Rf("EH", o, o + NA), ind(Rf("PL", 0, NR), U("UU")), -2048.0, A.add))
+
+        pairs = []
+        for p in ordr:
+            if p // 2 not in pairs:
+                pairs.append(p // 2)
+        for h in pairs:
+            a = 2 * N * h
+            for k in range(16):
+                b0 = par * NR + 16 * a
+                ref = Rf("ZE", b0 + k, b0 + 32 * N, 16)
+                e = OPT["ze0"] if t == 0 else OPT["ze"][pairs.index(h)]
+                if e[k] == "S":
+                    S("ze", act(ref, zc(a, a + 2 * N), AF.Copy))
+                elif e[k] == "G":
+                    add(P, "G", "ze", [("affine", dict(out=ref, in_=zc(a, a + 2 * N)))])
+                else:
+                    V("ze", cp(ref, zc(a, a + 2 * N)))
+        if t == 0:
+            V("E160", ts(Rf("E16", 0, NA), ind(Rf("PL", 0, NR), Rf("PU", 0, 16)), -2048.0, A.add))
+            V("EU0", ts(Rf("EU", 0, NA), Rf("E16", 0, NA), 2048.0, A.add))
+        ep = OPT["ep0"] if t == 0 else OPT["ep"]
+        for ip, p in enumerate(ordr):
+            if ep[ip] == "S":
+                a = p * N
+                for h in range(2):
+                    x0 = par * NR + 16 * a + 8 * N * h
+                    x1 = x0 + 8 * N
+                    S("GEs", act(Rf("DE", x0, x1), ind(Xa, Rf("EU", o + a + N // 2 * h, o + a + N // 2 * (h + 1))), AF.Copy))
+                    PE("psZ", acc(Rf("ps7", 0, 512), [(IB, Rf("DE", x0, x1)), (M("NIB"), Rf("ZE", x0, x1))]))
+                    S("AE", act(Rf("AE", x0, x1), Rf("ps7", 0, 512), AF.Abs))
+        sub, later = [], []
+        for ip, p in enumerate(ordr):
+            a = p * N
+            b16 = par * NR + 16 * a
+            e16 = b16 + 16 * N
+            pq = ip % 2
+            z = zc(a, a + N)
+            big = lambda nm: Rf(nm, b16, e16)
+            D, K, L = "ps%d" % pq, "ps%d" % (2 + pq), "ps%d" % (4 + pq)
+            if ip == 0:
+                PE("psF", acc(Rf("ps2", 256, 512), [(I16, Rf("F16", o, o + NA)), (IB, zc(0, NA))]))
+                V("F16", ts(Rf("F16", o + NA, o + 2 * NA), Rf("ps2", 256, 512), 0.5, A.mult, 511.75, A.add))
+            eu = Rf("EU", o + a, o + a + N)
+            gh = OPT["gh"][ip]
+            for h in range(gh):
+                x0, x1 = b16 + 16 * N // gh * h, b16 + 16 * N // gh * (h + 1)
+                V("GS", tt(Rf("DS", x0, x1), ind(Xa, Rf("SU", o + a + N // gh * h, o + a + N // gh * (h + 1))), Rf("ZE", x0, x1), A.subtract))
+            wS = [(sel(k), Rf("AS", b16 + k, e16, 16)) for k in range(16)]
+            if OPT["sa"][ip] == "V":
+                V("RS", ts(big("AS"), big("DS"), 0.0, A.max))
+                wS = [(sel(k, "BIGN"), Rf("DS", b16 + k, e16, 16)) for k in range(16)] + [(sel(k, "BIG2"), Rf("AS", b16 + k, e16, 16)) for k in range(16)]
+            else:
+                ah = OPT["ah"][ip]
+                for h in range(ah):
+                    x0, x1 = b16 + 16 * N // ah * h, b16 + 16 * N // ah * (h + 1)
+                    S("AS", act(Rf("AS", x0, x1), Rf("DS", x0, x1), AF.Abs))
+            wE = [(sel(k), Rf("AE", b16 + k, e16, 16)) for k in range(16)]
+            wN = []
+            if ep[ip] == "V":
+                V("GE", tt(big("DE"), ind(Xa, eu), big("ZE"), A.subtract))
+                if OPT["ea"][ip] == "V":
+                    V("RE", ts(big("AE"), big("DE"), 0.0, A.max))
+                    wN = [(sel(k, "BIGN"), Rf("DE", b16 + k, e16, 16)) for k in range(16)]
+                    wE = [(sel(k, "BIG2"), Rf("AE", b16 + k, e16, 16)) for k in range(16)]
+                else:
+                    S("AE", act(big("AE"), big("DE"), AF.Abs))
+            if OPT["lw"][ip] == "V":
+                V("LW", ts(big("LW"), big("DS"), 0.0, A.is_le))
+            else:
+                S("LW", act(big("LW"), big("DS"), AF.Sign, bias=-0.5))
+            hist = [(M("N64"), Rf("SW", u * NA + a, u * NA + a + N)) for u in range(t)]
+            P["up"] = OPT["up"][ip]
+            xs = PE("psDs", acc(Rf(D, 0, N), hist + wS))
+            if wN:
+                both = acc(Rf(D, N, 2 * N), hist + wN + wE)
+                P["tasks"][PE("psDe", both[:-16], extra=[xs])]["opens"] = D
+                P["tasks"][PE("psDe", both[-16:])]["closes"] = D
+            else:
+                PE("psDe", acc(Rf(D, N, 2 * N), hist + wE))
+            rb = par * 2 * NA + 2 * a
+            r, rp = Rf("RR", rb, rb + N), Rf("RR", rb + N, rb + 2 * N)
+            V("RR", tt(r, Rf(D, 0, N), Rf("TH", a, a + N), A.is_lt))
+            V("RP", tt(rp, Rf(D, N, 2 * N), Rf("TH", a, a + N), A.is_lt))
+            if ip == 0:
+                hash_()
+            s16, e_16 = Rf("S16", o + a, o + a + N), Rf("E16", o + a, o + a + N)
+            eh = Rf("EH", o + a, o + a + N)
+            one = Rf("ONE", 0, N)
+            PE("psK", acc(Rf(K, 0, N), [(I16, s16), (M("G1"), r)]) +
+               acc(Rf(K, N, 2 * N), [(I16, e_16), (M("G1"), rp), (M("N4"), r)]) +
+               acc(Rf(K, 2 * N, 3 * N), [(I16, eh), (M("K4"), one), (M("N4"), r), (M("N4"), rp)]))
+            wb = par * 4 * NA + 4 * a
+            V("W", ts(Rf("WW", wb, wb + 3 * N), Rf(K, 0, 3 * N), -4096.0, A.add, -2048.0, A.max))
+            w = lambda j, wb=wb: Rf("WW", wb + j * N, wb + j * N + N)
+            PE("psT", acc(R3(L, 0, 2 * N, 0), [(M("EV"), w(0)), (M("EV"), w(1)), (M("EV0"), w(2))]) +
+               acc(R3(L, 0, 2 * N, 1), [(M("OD"), w(0)), (M("OD"), w(1)), (M("OD0"), w(2))]))
+            tb = (par * 4 + ip) * 128
+            V("TRT", tr(Rf("TRT", tb, tb + 2 * N), R3(L, 0, 2 * N)))
+
+            def top_and_y(ip=ip, p=p, a=a, K=K, L=L, z=z, tb=tb):
+                l0 = t * 16 + 4 * ip
+                yd = Rf("YD", o + a, o + a + N)
+                V("YD", tt(yd, ind(Xa, Rf("LST", l0, l0 + 4)), Rf("F16", o + NA + a, o + NA + a + N), A.subtract))
+                if p == loc and not last:
+                    y = Rf("Z", o + NA + a, o + NA + a + N)
+                else:
+                    y = Rf("Y", o + a, o + a + N)
+                S("Y", act(y, yd, AF.Abs, bias=1024.0))
+                if p != loc and not last:
+                    add(P, "G", "send", [("send", dict(src=y, t=t, b=p))], dur=0.3, sem="none")
+                    add(P, "N", "recv", [], wr=[Rf("Z", o + NA + a, o + NA + a + N)], dur=EST["net"], sem="za%d%d" % (t + 1, p), inc=0, extra=[len(P["tasks"]) - 1])
+                PE("psY", acc(R3(L, 2 * N, 4 * N, 0), [(M("EVB"), y)]) + acc(R3(L, 2 * N, 4 * N, 1), [(M("ODB"), y)]) +
+                   acc(Rf(K, 6 * N, 7 * N), [(IB, y), (IB, z)]))
+                V("TRY", tr(Rf("TRY", tb, tb + 2 * N), R3(L, 2 * N, 4 * N)))
+                V("XN", ts(Rf("XN", o + a, o + a + N), Rf(K, 6 * N, 7 * N), 0.5, A.mult, -0.25, A.add))
+            later.append(top_and_y)
+            for grp in OPT["tops"]:
+                if grp[-1] == ip:
+                    l0, l1 = t * 16 + 4 * grp[0], t * 16 + 4 * ip + 4
+                    V("LST", ts(Rf("LST", l0, l1), Rf("TRT", (par * 4 + grp[0]) * 128, tb + 2 * N, 32), 67584.0, A.add))
+                    for j in grp:
+                        later[j]()
+            for grp in OPT["places"]:
+                if grp[-1] == ip:
+                    l0, l1 = t * 16 + 4 * grp[0], t * 16 + 4 * ip + 4
+                    V("PI1", cp(Rf("PI1", l0, l1), Rf("TRY", (par * 4 + grp[0]) * 128, tb + 2 * N, 32)))
+                    V("PI2", ts(Rf("PI2", l0, l1), Rf("PI1", l0, l1), 15, A.bitwise_and))
+                    V("PI3", tt(Rf("PI3", l0, l1), Rf("PI2", l0, l1), Rf("BASE", 0, l1 - l0), A.add))
+                    V("PLC", cp(Rf("PLC", l0, l1), Rf("PI3", l0, l1)))
+            P["up"] = 0.0
+            qb, fm = Rf("QB", o + a, o + a + N), Rf("FM", o + a, o + a + N)
+            S7 = "ps%d" % OPT["s7"][ip]
+            PE("psJ", acc(Rf(D, 5 * N, 6 * N), [(M("G1"), r)]))
+            S("FM", act(fm, Rf(D, 5 * N, 6 * N), AF.Relu, scale=1.0 / 4096))
+            wL = [(sel(k), Rf("LW", b16 + k, e16, 16)) for k in range(16)]
+            if OPT["lw"][ip] == "V":
+                PE("psLo", acc(Rf(S7, 5 * N, 6 * N), wL + [(M("A17"), fm)]))
+                S("QB", act(qb, Rf(S7, 5 * N, 6 * N), AF.Sign, bias=-28.5))
+            else:
+                PE("psLo", acc(Rf(S7, 5 * N, 6 * N), wL + [(M("N34"), fm)]))
+                S("QB", act(qb, Rf(S7, 5 * N, 6 * N), AF.Sign, bias=-41.0, scale=-1.0))
+            PE("psW", acc(Rf(D, 2 * N, 3 * N), [(M("ONESB"), r), (M("ONESB"), rp)]) +
+               [])
+            S("SW", act(Rf("SW", o + a, o + a + N), Rf(D, 2 * N, 3 * N), AF.Relu, bias=1.0, scale=-1.0))
+            if not last:
+                en = Rf("E16", o + NA + a, o + NA + a + N)
+                PE("psE", acc(Rf(D, 3 * N, 4 * N), [(I16, e_16), (M("NK4"), Rf("SW", o + a, o + a + N))]))
+                V("E16", tt(en, w(2), Rf(D, 3 * N, 4 * N), A.max))
+                V("EU", ts(Rf("EU", o + NA + a, o + NA + a + N), en, 2048.0, A.add))
+            sub.append((p, a, OPT["s7"][ip], r, rp, s16, e_16, fm, qb, w))
+        for ip, (p, a, pq, r, rp, s16, e_16, fm, qb, w) in enumerate(sub):
+            l0, l1 = t * 16 + 4 * ip, t * 16 + 4 * ip + 4
+            V("SC", [("tensor_copy", dict(out=ind(Rf("X", 16 * a, 16 * (a + N)), Rf("PLC", l0, l1)), in_=Rf("XN", o + a, o + a + N)))])
+        for p, a, pq, r, rp, s16, e_16, fm, qb, w in sub:
+            S7 = "ps%d" % pq
+            PE("psX", acc(Rf(S7, 0, N), [(I16, s16), (M("NQ"), qb), (M("NK4"), fm)]) + acc(Rf(S7, N, 2 * N), [(I16, e_16), (M("PQ"), qb), (M("NK4"), fm)]))
+            sb = par * 2 * NA + 2 * a
+            V("SE", ts(Rf("SE", sb, sb + 2 * N), Rf(S7, 0, 2 * N), -2048.0, A.add, -2048.0, A.max))
+            sx, ex = Rf("SE", sb, sb + N), Rf("SE", sb + N, sb + 2 * N)
+            PE("psM", acc(Rf(S7, 2 * N, 3 * N), [(I16, sx), (I16, ex), (M("NL"), r)]))
+            m = Rf("MM", sb, sb + N)
+            V("MM", ts(m, Rf(S7, 2 * N, 3 * N), 2048.0, A.add, -2048.0, A.max))
+            row0 = sel(0, "BIG16")
+            PE("psS", acc(Rf(S7, 4 * N, 5 * N), [(I16, sx), (I16, ex), (row0, w(0)), (row0, w(1)), (M("R00"), w(2)), (M("R0K"), one), (M("SHI"), m)]))
+            if last:
+                V("YS", ts(Rf("YSO", a, a + N), Rf(S7, 4 * N, 5 * N), 4096.0, A.add))
+            else:
+                V("SU", ts(Rf("SU", o + NA + a, o + NA + a + N), Rf(S7, 4 * N, 5 * N), 4096.0, A.add))
+                V("S16", ts(Rf("S16", o + NA + a, o + NA + a + N), Rf(S7, 4 * N, 5 * N), 2048.0, A.add))
+        PE("psP", acc(Rf("ps6", 464, 480), [(sel(m, "BIG0B"), Rf("SW", o + m, o + NA, 16)) for m in range(16)]))
+        V("PA", tt(Rf("PA", k0 + 16, k1 + 16), Rf("PA", k0, k1), Rf("ps6", 464, 480), A.add))
+        V("PD", tt(Rf("PD", k0, k1), Rf("UH", k0, k1), Rf("PF", k0, k1), A.subtract))
+        V("PM", tt(Rf("PM", k0, k1), Rf("PD", k0, k1), Rf("ps6", 464, 480), A.mult))
+        V("PF", tt(Rf("PF", k0 + 16, k1 + 16), Rf("PF", k0, k1), Rf("PM", k0, k1), A.add))
+    k0 = NT * 16
+    V("YP1", ts(Rf("PM", k0, k0 + 16), Rf("PA", k0, k0 + 16), 4096.0, A.mult))
+    V("YP", tt(Rf("YPO", 0, 16), Rf("PM", k0, k0 + 16), Rf("PF", k0, k0 + 16), A.add))
+    V("YF", ts(Rf("YFO", 0, NA), Rf("F16", NT * NA, NT * NA + NA), -1024.0, A.add))
+    for c in range(16):
+        V("CI", ts(Rf("CI", c * 128, c * 128 + 128), C("IB"), float(c + 1), A.mult))
+    for p, a in [(x[0], x[1]) for x in sub]:
+        PE("psV", acc(Rf("ps%d" % (p % 2), a, a + N), [(Rf("CI", c * 128, c * 128 + 128), Rf("X", 16 * a + c, 16 * (a + N), 16)) for c in range(16)]))
+        S("YX", act(Rf("YXO", a, a + N), Rf("ps%d" % (p % 2), a, a + N), AF.Copy))
+    for k, (o_, b) in enumerate((("ys", "YSO"), ("yp", "YPO"), ("yf", "YFO"), ("yx", "YXO"))):
+        add(P, "Y", "st" + o_, [("store", dict(dst=o_, src=Rf(b, 0, SCRATCH[b][1][1])))], dur=0.1, sem="ost%d" % k, inc=16)
+    return P
+
+
+def schedule(P):
+    T = P["tasks"]
+    n = len(T)
+    succ = [[] for _ in range(n)]
+    for t in T:
+        for o, kind in t["pre"].items():
+            succ[o].append((t["i"], kind))
+
+    def lat(o, i, kind):
+        a, b = T[o], T[i]
+        if kind == "time":
+            return 0.0
+        if a["inc"] == 16:
+            return a["prio"]
+        if a["q"] == b["q"]:
+            return 0.0 if a["q"] == "P" else EST["self_"]
+        return EST["lat"]
+    far = [0.0] * n
+    for i in range(n - 1, -1, -1):
+        far[i] = T[i]["dur"] + max([lat(i, j, k) + far[j] for j, k in succ[i]] or [0.0])
+    for i in range(n):
+        far[i] += T[i]["up"] + PRIO.get(T[i]["name"], 0.0)
+    ready = [0.0] * n
+    left = [len(t["pre"]) for t in T]
+    free = {}
+    avail = {}
+    for t in T:
+        free.setdefault(t["q"], 0.0)
+        avail.setdefault(t["q"], [])
+    for i in range(n):
+        if left[i] == 0:
+            avail[T[i]["q"]].append(i)
+    order, start = [], [0.0] * n
+    held = {}
+
+    opened = set()
+
+    def er(i):
+        r = ready[i]
+        for b in T[i]["banks"]:
+            if b in opened and T[i]["q"] == "P" and T[i].get("closes") != b:
+                return 1e9
+            for q2, (e2, o2) in held.get(b, {}).items():
+                if q2 != T[i]["q"] and e2 + EST["lat"] > r:
+                    r = e2 + EST["lat"]
+        return r
+    while len(order) < n:
+        best = None
+        for q, lst in avail.items():
+            if not lst:
+                continue
+            s = min(er(i) for i in lst)
+            if q != "N":
+                s = max(free[q], s)
+            if best is None or s < best[0]:
+                best = (s, q)
+        s, q = best
+        if q == "N":
+            i = min(avail[q], key=lambda j: ready[j])
+            s = ready[i]
+        elif q == "Y":
+            i = min(avail[q])
+            s = max(free[q], ready[i])
+        else:
+            c = [j for j in avail[q] if er(j) <= s + 0.03]
+            d = [j for j in c if T[j]["inc"] == 16]
+            i = min(d) if d else max(c, key=lambda j: far[j])
+            s = max(free[q], er(i))
+        if "opens" in T[i]:
+            opened.add(T[i]["opens"])
+        if "closes" in T[i]:
+            opened.discard(T[i]["closes"])
+        avail[q].remove(i)
+        start[i] = s
+        end = s + T[i]["dur"]
+        for b in T[i]["banks"]:
+            for q2, (e2, o2) in held.get(b, {}).items():
+                if q2 != q:
+                    T[i]["pre"][o2] = "raw"
+            held.setdefault(b, {})[q] = (end, i)
+        if q != "N":
+            free[q] = end
+        order.append(i)
+        for j, kind in succ[i]:
+            x = end + lat(i, j, kind)
+            if x > ready[j]:
+                ready[j] = x
+            left[j] -= 1
+            if left[j] == 0:
+                avail[T[j]["q"]].append(j)
+    return order, start, max(free.values())
+
+
+CACHE = {}
+
+
+def plan():
+    if "p" not in CACHE:
+        P = build()
+        CACHE["p"] = (P, schedule(P))
+    return CACHE["p"]
+
+
+def rank_program(g, core, T, topo):
+    rank = T.rank_of(core)
+    if rank is None:
+        return
+    P, (order, start, length) = plan()
+    tasks = P["tasks"]
+    queues = {"V": g.vector, "S": g.scalar, "P": g.tensor, "G": g, "Y": g.sync}
+    clock = {q: {} for q in queues}
+    total = {}
+    info = {}
+
+    def ap(v):
+        if not isref(v):
+            return v
+        if v[0] == "#":
+            return ap(v[1]).indirect(ap(v[2]))
+        if len(v) == 5:
+            b = T[v[0]]
+            i, j = v[1] // 32, v[2] // 32
+            return b[:, i:j, :] if v[4] is None else b[:, i:j, 16 * v[4]:16 * v[4] + 16]
+        if v[3] == 1:
+            return T[v[0]][:, v[1]:v[2]]
+        return T[v[0]][:, v[1]:v[2]:v[3]]
+
+    def lanes(src, dst):
+        return topo.engines(src, dst)[::2]
+    nloc = 0
+    for i in order:
+        t = tasks[i]
+        q = t["q"]
+        if q == "N":
+            tt_, b = int(t["sem"][2]), int(t["sem"][3])
+            e = len(lanes(T.cores[(rank - b - (tt_ - 1)) % 4], core))
+            info[i] = (t["sem"], e, {t["sem"]: e})
+            total[t["sem"]] = e
+            continue
+        eng = queues[q]
+        ck = clock[q]
+        need = {}
+        for o, kind in t["pre"].items():
+            if kind == "time" or (tasks[o]["q"] == q and q == "P") or o not in info:
+                continue
+            sem, val, know = info[o]
+            if ck.get(sem, 0) < val and need.get(sem, (0,))[0] < val:
+                need[sem] = (val, know)
+        for sem in sorted(need):
+            val, know = need[sem]
+            if any(o2 != sem and k2.get(sem, 0) >= val for o2, (v2, k2) in need.items()):
+                continue
+            eng.wait_ge(T.sem[sem], val)
+        for sem, (val, know) in need.items():
+            for s2, v2 in know.items():
+                if ck.get(s2, 0) < v2:
+                    ck[s2] = v2
+        if t["name"] == "send":
+            kw = t["ins"][0][1]
+            dst = T.cores[(rank + kw["b"] + kw["t"]) % 4]
+            rid, pid, _s = topo.addr(dst)
+            e = lanes(core, dst)
+            src = kw["src"]
+            o = src[1] + NA
+            g.remote_dma(T.Z[:, o:o + N], ap(src), T.sem["za%d%d" % (kw["t"] + 1, kw["b"])], T.sem["lsent"], pid, rid, sum(1 << x for x in e))
+            nloc += len(e)
+            continue
+        if t["inc"] == 16:
+            m, kw = t["ins"][0]
+            if m == "dma":
+                s = kw["src"]
+                h = eng.dma_start(ap(kw["out"]), T[s[0]][:, s[1]:s[2]])
+            else:
+                h = eng.dma_start(T[kw["dst"]][:, 0:kw["src"][2]], ap(kw["src"]))
+            h.then_inc(T.sem[t["sem"]], 16)
+            know = dict(ck)
+            know[t["sem"]] = 16
+            total[t["sem"]] = 16
+            info[i] = (t["sem"], 16, know)
+            continue
+        sem = QS[q]
+        for j, (m, kw) in enumerate(t["ins"]):
+            a = {k: ap(v) for k, v in kw.items()}
+            if m == "matmul":
+                h = eng.matmul(a["out"], a["lhsT"], a["rhs"], a["start"], a["stop"])
+            elif m == "iota":
+                flag = {} if SCRATCH[kw["out"][0]][2] == "int32" else {"allow_small_or_imprecise_dtypes": True}
+                h = eng.iota(a["out"], a["pattern"], a["base"], a["channel_multiplier"], **flag)
+            elif m == "affine":
+                h = eng.affine_select(out=a["out"], in_=a["in_"], pattern=[[0, cnt(kw["in_"])]], compare_op=A.is_gt, fill=0.0, base=1, channel_multiplier=0)
+            elif m == "memset":
+                h = eng.memset(a["ap"], a["constant"])
+            elif m == "vtranspose":
+                h = eng.transpose(a["out"], a["in_"])
+            elif m == "tensor_copy":
+                h = eng.tensor_copy(**a)
+            elif m == "tensor_tensor":
+                h = eng.tensor_tensor(**a)
+            elif m == "tensor_scalar":
+                h = eng.tensor_scalar(**a)
+            else:
+                h = eng.activation(**a)
+            if j == len(t["ins"]) - 1:
+                h.then_inc(T.sem[sem], 1)
+        total[sem] = total.get(sem, 0) + 1
+        know = dict(ck)
+        know[sem] = total[sem]
+        info[i] = (sem, total[sem], know)
+    for sem in sorted(total):
+        g.wait_ge(T.sem[sem], total[sem])
+    g.wait_ge(T.sem.lsent, nloc)

@@ -1,39 +1,40 @@
 from concourse.mybir import dt, AluOpType, ActivationFunctionType
 
 NT, NA, NR = 6, 256, 4096
-N = 64
-NP = NA // N
+N = 128
+NB = 64
+L = 16 * N
 
 SCRATCH = {}
 for _nm, _sh, _ty in (
-        ("X", 4096, "bfloat16"), ("PL", 4096, "int32"), ("Z", NT * NA, "bfloat16"), ("Y", NT * NA, "bfloat16"),
-        ("ZE", 2 * NR, "bfloat16"), ("DS", 2 * NR, "bfloat16"), ("DE", 2 * NR, "bfloat16"),
-        ("AS", 2 * NR, "bfloat16"), ("AE", 2 * NR, "bfloat16"), ("LW", 2 * NR, "bfloat16"),
-        ("TH", NA, "int32"), ("S0", NA, "int32"), ("P0", 16, "int32"), ("F0", NA, "bfloat16"),
-        ("S16", 7 * NA, "float16"), ("SU", 7 * NA, "uint16"), ("E16", 7 * NA, "float16"), ("EU", 7 * NA, "uint16"),
-        ("EH", NT * NA, "float16"), ("F16", 7 * NA, "float16"), ("RR", 4 * NA, "bfloat16"), ("WW", 8 * NA, "float16"),
-        ("TRT", 8 * 128, "float32"), ("TRY", 8 * 128, "float32"), ("LST", NT * 16, "uint16"), ("YD", NT * NA, "float32"),
-        ("PI1", NT * 16, "int32"), ("PI2", NT * 16, "int32"), ("PI3", NT * 16, "int32"), ("PLC", NT * 16, "uint16"),
-        ("XN", NT * NA, "int32"), ("HB", NT * NA, "bfloat16"), ("QB", NT * NA, "bfloat16"), ("SW", NT * NA, "bfloat16"), ("FM", NT * NA, "bfloat16"),
-        ("SE", 4 * NA, "float16"), ("MM", 4 * NA, "float16"),
-        ("U1", NT * 16, "int32"), ("U2", NT * 16, "int32"), ("U3", NT * 16, "int32"), ("U4", NT * 16, "int32"),
-        ("U5", NT * 16, "int32"), ("U6", NT * 16, "int32"), ("UH", NT * 16, "int32"), ("UU", NT * 16, "uint16"), ("PU", 16, "uint16"),
-        ("PF", 7 * 16, "float32"), ("PA", 7 * 16, "float32"), ("PD", 7 * 16, "float32"), ("PM", 7 * 16, "float32"), ("YPO", 16, "float32"),
-        ("YSO", NA, "float32"), ("YFO", NA, "bfloat16"), ("YXO", NA, "float32"),
-        ("IOC", 144, "float32"), ("PC", 1, "float32"), ("PI", 1, "int32"), ("IOB", 16, "int32"), ("BASE", 16, "int32"),
-        ("PG", 1, "int32"), ("PK", 1, "int32"), ("PH", 1, "int32"), ("PO", 1, "int32"), ("C0F", 1, "float32"), ("C15F", 1, "float32"), ("W2", 1, "float32"),
-        ("K16", 1, "float32"), ("R0", 1, "float32"), ("D0F", 1, "float32"), ("D31F", 1, "float32"), ("ODC", 1, "float32"), ("EVC", 1, "float32"),
-        ("CA", 128, "float32"), ("CB", 128, "float32"), ("OB", 128, "float32"), ("LF", 128, "float32"), ("IFF", 128, "float32"), ("PB", 128, "float32"),
-        ("T1", 128, "float32"), ("T2", 128, "float32"),
-        ("BIG", 144, "bfloat16"), ("BIGW", 144, "bfloat16"), ("BIG2", 144, "bfloat16"), ("BIGN", 144, "bfloat16"), ("BIG0B", 144, "bfloat16"), ("BIG16", 144, "float16"),
-        ("ONESB", 128, "bfloat16"), ("N4", 128, "bfloat16"), ("EV", 128, "float16"), ("OD", 128, "float16"), ("EV0", 128, "float16"), ("OD0", 128, "float16"),
-        ("EVB", 128, "bfloat16"), ("ODB", 128, "bfloat16"),
-        ("IB", 128, "bfloat16"), ("NIB", 128, "bfloat16"), ("I16", 128, "float16"), ("NI16", 128, "float16"), ("K4", 128, "bfloat16"), ("N64", 128, "bfloat16"),
-        ("A17", 128, "bfloat16"), ("N34", 128, "bfloat16"), ("PQ", 128, "bfloat16"), ("NQ", 128, "bfloat16"), ("G1", 128, "bfloat16"), ("NL", 128, "bfloat16"), ("NK4", 128, "bfloat16"),
-        ("SHI", 128, "float16"), ("R00", 128, "float16"), ("R0K", 128, "bfloat16"), ("ONE", N, "bfloat16"), ("CI", 2048, "bfloat16")):
-    SCRATCH[_nm] = ("sbuf", [128, _sh], _ty)
+        ("X", [NR], "bfloat16"), ("PL", [NR], "int32"), ("Z4", [2 * NT, 512], "bfloat16"), ("Y", [NT * NA], "bfloat16"),
+        ("DS", [2 * L], "bfloat16"), ("HS", [2 * L], "float16"), ("DE", [2 * L], "bfloat16"), ("AE", [2 * L], "bfloat16"),
+        ("TH", [NA], "int32"), ("S0", [NA], "int32"), ("P0", [16], "int32"), ("F0", [NA], "bfloat16"),
+        ("KT", [3 * NA], "float16"), ("TT", [3 * NA], "float16"), ("THA", [NA], "float16"),
+        ("EK", [NT * NA], "float16"), ("ET", [NT * NA], "float16"),
+        ("S16", [7 * NA], "float16"), ("SU", [7 * NA], "uint16"), ("E16", [7 * NA], "float16"), ("EU", [7 * NA], "uint16"),
+        ("F16", [7 * NA], "float16"), ("NI", [NA], "int32"), ("RR", [2 * NA], "bfloat16"), ("RP", [2 * NA], "bfloat16"), ("QQ", [2 * NA], "bfloat16"),
+        ("WF", [2 * NA], "float32"), ("WH", [2 * NA], "float16"), ("W2", [NA], "float16"), ("MS", [NA], "bfloat16"),
+        ("SE", [2 * NA], "float16"), ("MM", [NA], "float16"), ("SW", [2 * NT, N], "bfloat16"),
+        ("YD", [NT * NA], "float32"), ("XN", [NT * NA], "int32"),
+        ("PI1", [NT * 16], "int32"), ("PI2", [NT * 16], "int32"), ("PI3", [NT * 16], "int32"), ("PLC", [NT * 16], "uint16"),
+        ("U1", [NT * 16], "int32"), ("U2", [NT * 16], "int32"), ("U3", [NT * 16], "int32"), ("U4", [NT * 16], "int32"),
+        ("U5", [NT * 16], "int32"), ("U6", [NT * 16], "int32"), ("UH", [NT * 16], "int32"), ("UU", [NT * 16], "uint16"), ("PU", [16], "uint16"),
+        ("PT", [NT * 16], "int32"), ("PV", [NT * 16], "int32"), ("PW", [7 * 16], "int32"), ("YPO", [16], "float32"),
+        ("YSO", [NA], "float32"), ("YFO", [NA], "bfloat16"), ("YXO", [NA], "float32"),
+        ("IOC", [160], "float32"), ("PC", [1], "float32"), ("PI", [1], "int32"), ("IO8", [N], "int32"), ("BASE", [16], "int32"), ("TC", [NT * 16], "int32"),
+        ("IOB", [16], "int32"), ("PG", [1], "int32"), ("PK", [1], "int32"), ("PO", [1], "int32"), ("C15F", [1], "float32"), ("PGF", [1], "float32"),
+        ("WK", [1], "float32"), ("K16", [1], "float32"), ("ODC", [1], "float32"), ("EVC", [1], "float32"), ("A8", [N], "int32"),
+        ("WI", [160], "bfloat16"), ("EVW", [160], "bfloat16"), ("ODW", [160], "bfloat16"), ("BIG", [144], "bfloat16"), ("BIGW", [144], "bfloat16"),
+        ("GS", [8], "bfloat16"), ("GN", [8], "bfloat16"), ("GH", [8], "bfloat16"), ("O8", [N], "bfloat16"), ("GT", [N], "bfloat16"), ("LT", [N], "bfloat16"),
+        ("T1", [N], "bfloat16"), ("T2", [N], "bfloat16"), ("ONE", [N], "bfloat16"), ("NIB", [N], "bfloat16"), ("HI", [N], "bfloat16"), ("I32", [N], "bfloat16"),
+        ("N64", [N], "bfloat16"), ("PQ", [N], "bfloat16"), ("NQ", [N], "bfloat16"), ("NK4", [N], "bfloat16"), ("K4", [N], "bfloat16"), ("Q256", [N], "bfloat16"),
+        ("G1", [N], "bfloat16"), ("G1H", [N], "bfloat16"), ("N4", [N], "bfloat16"), ("N2", [N], "bfloat16"), ("SM", [N], "bfloat16"),
+        ("NLI", [N], "bfloat16"), ("SHI", [N], "bfloat16"), ("CT", [N], "bfloat16"), ("KS32", [8], "float32"), ("NI32", [N], "float32"),
+        ("CI", [2048], "bfloat16")):
+    SCRATCH[_nm] = ("sbuf", [128] + _sh, _ty)
 for _k in range(8):
-    SCRATCH["ps%d" % _k] = ("psum", [128, 16, 32] if _k in (4, 5) else [128, 512], "float32")
+    SCRATCH["ps%d" % _k] = ("psum", [128, 4, N], "float32")
 
 LOADS = ["lz", "lx", "ls", "lf", "lp", "lpl", "lt"]
 STORES = ["ost%d" % k for k in range(4)]
@@ -44,27 +45,28 @@ AF = ActivationFunctionType
 BYTES2 = {k for k, v in SCRATCH.items() if v[2] in ("bfloat16", "float16", "uint16")}
 QS = {"V": "cv", "S": "cs", "P": "ct", "G": "cg"}
 
-EST = dict(g=1.55, sc=3.0, v=0.00083 * 1.2, pe=0.00042 * 1.2, vo=0.0, so=0.06, lat=0.12, self_=0.08, net=2.6)
-OPT = dict(ep="SSVS", ea="SSSS", sa="SSSS", ep0="SVVV", gh=(1, 1, 1, 1), ah=(1, 1, 1, 1), ze0="SSSSSSSSGGGGVVVV", ze=("SSSSGGGGGGVVVVVV", "GG" + "V" * 14), lw="VVSV", up=(1, 1, 1, 0), s7=(7, 6, 7, 6), tops=((0, 1), (2,), (3,)), places=((0, 1), (2, 3)))
-
-
-PRIO = {'PI1': -0.1, 'U6': 1.6, 'psDs': 0.5, 'PA': -1.9, 'C0': 0.8, 'PF': 1.3, 'PK': 1.2, 'BIG': -1.0, 'EH': -1.3, 'D0': -1.2, 'MM': -0.0,
-        'PG': 1.0, 'PM': -1.8, 'ODC': 1.1, 'N34': 0.1, 'YP': 1.9, 'U2': 0.3, 'PU': 1.0, 'RP': 0.4, 'lf': 1.3, 'psS': 0.1, 'LST': -0.3,
-        'S16': 0.5, 'U4': -0.6, 'psE': -1.7, 'lz': 1.4, 'PI3': 0.5, 'OD': -0.2, 'BIGW': 0.4, 'SU': 0.3, 'SHI': -1.0, 'pi': 0.3,
-        'A17': -1.7, 'S160': -1.7, 'XN': -0.2, 'stys': -1.1, 'ioc': -1.2}
+EST = dict(g=1.55, sc=3.8, v=0.00083, pe=0.00042, vo=0.045, so=0.08, po=0.0, lat=0.15, self_=0.1, net=2.6, lx=7.0, lpl=16.0)
+OPT = dict(ep=("SSSS", "SSSS"), ep0=("SVSV", "SVSV"), w="SS", rho="SS", hh=(1, 1), ge=(512, 512), split=False, up=(2.0, 0.0))
+HASH = ("psU", "U1", "U2", "U3", "U4", "U5", "U6", "UH", "UU", "EK", "ET")
 
 
 def Rf(buf, lo, hi, st=1):
     return (buf, lo, hi, st)
 
 
-def R3(buf, lo, hi, h=None):
-    return (buf, lo, hi, 1, h)
+def R2(buf, o0, o1, lo, hi, st=1):
+    return (buf, lo, hi, st, o0, o1)
+
+
+def spans(r):
+    if len(r) == 4:
+        return [r[1:4]]
+    w = SCRATCH[r[0]][1][2]
+    return [(o * w + r[1], o * w + r[2], r[3]) for o in range(r[4], r[5])]
 
 
 def cnt(r):
-    k = (r[2] - r[1] + r[3] - 1) // r[3]
-    return k // 2 if len(r) == 5 and r[4] is not None else k
+    return sum((hi - lo + st - 1) // st for lo, hi, st in spans(r))
 
 
 def isref(x):
@@ -75,15 +77,14 @@ def ind(win, off):
     return ("#", win, off)
 
 
-def duration(q, ins):
-    e = EST
+def duration(q, ins, e):
     d = 0.0
     for m, kw in ins:
         if m == "matmul":
-            d += max(64, cnt(kw["rhs"])) * e["pe"]
+            d += e["po"] + max(min(64, cnt(kw["lhsT"])), cnt(kw["rhs"])) * e["pe"] * (1 if kw["rhs"][0] in BYTES2 else 4)
             continue
         if m == "iota":
-            d += 0.3
+            d += 0.13 + 2 * cnt(kw["out"]) * e["v"]
             continue
         if m == "affine":
             d += 0.17 + 2 * cnt(kw["in_"]) * e["v"]
@@ -96,11 +97,9 @@ def duration(q, ins):
         elif q == "S":
             d += e["so"] + cnt(kw["out"]) * e["v"]
         else:
-            o = kw.get("out", kw.get("ap"))
-            n = cnt(o)
-            big = [v for v in refs if cnt(v) == n]
+            n = cnt(kw.get("out", kw.get("ap")))
             c = 1.0
-            if m in ("tensor_copy", "tensor_scalar", "memset") and all(v[0] in BYTES2 for v in big):
+            if m != "tensor_tensor" and all(v[0] in BYTES2 for v in refs if cnt(v) == n):
                 c = 0.5
             if m == "tensor_tensor" and not any(v[0][:2] == "ps" for v in refs):
                 c = 2.0
@@ -112,13 +111,15 @@ def touches(ins):
     rd, wr = [], []
     for m, kw in ins:
         for k, v in kw.items():
-            if not isref(v):
+            if not isref(v) or k == "src":
                 continue
             if v[0] == "#":
                 (wr if k == "out" else rd).append(v[1])
                 rd.append(v[2])
             elif k in ("out", "ap"):
                 wr.append(v)
+                if m == "matmul" and not kw["start"]:
+                    rd.append(v)
             else:
                 rd.append(v)
     return rd, wr
@@ -130,50 +131,38 @@ def meet(a, b):
     return not (a[2] == b[2] and a[2] > 1 and (a[0] - b[0]) % a[2])
 
 
-def add(P, q, name, ins, rd=None, wr=None, dur=None, sem=None, inc=1, extra=None, prio=0.0):
+def add(P, q, name, ins, wr=None, dur=None, sem=None, inc=1, extra=None, prio=0.0):
     r, w = touches(ins)
-    r += rd or []
     w += wr or []
     T = {"i": len(P["tasks"]), "q": q, "name": name, "ins": ins, "sem": sem, "inc": inc, "prio": prio,
-         "dur": duration(q, ins) if dur is None else dur, "pre": {}, "banks": []}
+         "fix": dur, "pre": {}, "banks": [], "up": P.get("up", 0.0)}
     hist = P["last"]
-
-    def dep(o, kind):
-        old = T["pre"].get(o)
-        if old is None or kind == "raw":
-            T["pre"][o] = kind
     seen = {}
     for a, lst in (("r", r), ("w", w)):
         for ref in lst:
-            seen.setdefault((ref[0], ref[1], ref[2], ref[3]), set()).add(a)
+            for sp in spans(ref):
+                seen.setdefault((ref[0],) + tuple(sp), set()).add(a)
     for (buf, lo, hi, st), accs in seen.items():
         if buf[:2] == "ps" and buf not in T["banks"]:
             T["banks"].append(buf)
-        for (o, oq, oa, oset) in hist.get(buf, ()):
-            over = meet((lo, hi, st), oset)
-            if over and "w" in accs and "w" not in oa:
-                dep(o, "war")
-            elif over and ("w" in accs or "w" in oa):
-                dep(o, "raw")
+        for (o, oa, oset) in hist.get(buf, ()):
+            if ("w" in accs or "w" in oa) and meet((lo, hi, st), oset):
+                T["pre"][o] = "raw"
     for (buf, lo, hi, st), accs in seen.items():
         h = hist.setdefault(buf, [])
         if "w" in accs and st == 1:
-            h[:] = [e for e in h if not (lo <= e[3][0] and e[3][1] <= hi)]
-        h.append((T["i"], q, accs, (lo, hi, st)))
+            h[:] = [e for e in h if not (lo <= e[2][0] and e[2][1] <= hi)]
+    for (buf, lo, hi, st), accs in seen.items():
+        hist[buf].append((T["i"], accs, (lo, hi, st)))
     for o in extra or []:
-        dep(o, "time")
-    T["up"] = P.get("up", 0.0)
+        T["pre"].setdefault(o, "time")
     P["tasks"].append(T)
     return T["i"]
 
 
-def mm(out, lhsT, rhs, start, stop):
-    return ("matmul", dict(out=out, lhsT=lhsT, rhs=rhs, start=start, stop=stop))
-
-
-def acc(out, pairs):
-    k = len(pairs)
-    return [mm(out, l, r, i == 0, i == k - 1) for i, (l, r) in enumerate(pairs)]
+def acc(items, start=True, stop=True):
+    k = len(items)
+    return [("matmul", dict(out=o, lhsT=l, rhs=r, start=start and i == 0, stop=stop and i == k - 1)) for i, (o, l, r) in enumerate(items)]
 
 
 def ts(out, in0, s1, op0, s2=None, op1=None):
@@ -200,319 +189,317 @@ def tr(out, in_):
 
 
 def M(name):
-    return Rf(name, 0, 128)
+    return Rf(name, 0, N)
 
 
 def sel(m, name="BIG"):
     return Rf(name, 15 - m, 143 - m)
 
 
-ORDER = {0: (2, 3, 1, 0), 1: (2, 1, 0, 3), 2: (0, 1, 3, 2), 3: (0, 3, 2, 1), 4: (2, 3, 1, 0), 5: (2, 1, 0, 3)}
+def half(frm, to):
+    o = 16 - 16 * (to - frm)
+    return Rf("ODW" if frm else "EVW", o, o + N)
 
 
-def build():
+def reg(bank, j, n=1):
+    return Rf("ps%d" % bank, N * j, N * (j + n))
+
+
+def build(opt=None):
+    opt = opt or OPT
     P = {"tasks": [], "last": {}}
     c1 = lambda n: Rf(n, 0, 1)
-    C = lambda n: Rf(n, 0, 128)
-    B = lambda n: Rf(n, 0, 144)
-    def load(q, sem, ref, dur, src):
-        return add(P, q, sem, [("dma", dict(out=ref, src=src + (1,)))], dur=0.1, sem=sem, inc=16, prio=dur)
-    load("Y", "ls", Rf("S0", 0, NA), 2.2, ("s0", 0, NA))
-    load("Y", "lz", Rf("Z", 0, NA), 2.2, ("z0", 0, NA))
-    load("Y", "lx", Rf("X", 0, NR), 7, ("x0", 0, NR))
-    load("S", "lp", Rf("P0", 0, 16), 2.5, ("p0", 0, 16))
-    load("S", "lf", Rf("F0", 0, NA), 2.5, ("f0", 0, NA))
-    load("Y", "lt", Rf("TH", 0, NA), 8, ("th", 0, NA))
-    load("Y", "lpl", Rf("PL", 0, NR), 17, ("pl", 0, NR))
-    io = lambda nm, ref, pat, ch: add(P, "G", nm, [("iota", dict(out=ref, pattern=pat, base=0, channel_multiplier=ch))])
-    io("ioc", B("IOC"), [[1, 144]], 0)
-    io("pc", c1("PC"), [[1, 1]], 1)
-    io("pi", c1("PI"), [[1, 1]], 1)
-    io("iob", Rf("IOB", 0, 16), [[0, 4], [256, 4]], 0)
     V = lambda nm, ins, **k: add(P, "V", nm, ins, **k)
     S = lambda nm, ins, **k: add(P, "S", nm, ins, **k)
-    PE = lambda nm, ins, **k: add(P, "P", nm, ins, **k)
+    G = lambda nm, ins, **k: add(P, "G", nm, ins, **k)
+
+    def PE(nm, ins, opens=None, closes=None, **k):
+        i = add(P, "P", nm, ins, **k)
+        if opens:
+            P["tasks"][i]["opens"] = opens
+        if closes:
+            P["tasks"][i]["closes"] = closes
+        return i
+
+    def load(q, sem, ref, dur, src):
+        return add(P, q, sem, [("dma", dict(out=ref, src=src))], dur=0.1, sem=sem, inc=16, prio=dur)
+    load("Y", "ls", Rf("S0", 0, NA), 2.2, ("s0", 0, NA))
+    load("Y", "lz", R2("Z4", 0, 2, 0, N), 2.2, ("z0", 0, NA))
+    load("Y", "lx", Rf("X", 0, NR), EST["lx"], ("x0", 0, NR))
+    load("S", "lt", Rf("TH", 0, NA), 2.5, ("th", 0, NA))
+    load("S", "lp", Rf("P0", 0, 16), 2.5, ("p0", 0, 16))
+    load("S", "lf", Rf("F0", 0, NA), 2.5, ("f0", 0, NA))
+    load("Y", "lpl", Rf("PL", 0, NR), EST["lpl"], ("pl", 0, NR))
+    io = lambda nm, ref, pat, ch, base=0: G(nm, [("iota", dict(out=ref, pattern=pat, base=base, channel_multiplier=ch))])
+    io("pc", c1("PC"), [[1, 1]], 1)
+    io("ioc", Rf("IOC", 0, 160), [[1, 160]], 0)
+    io("pi", c1("PI"), [[1, 1]], 1)
+    io("io8", M("IO8"), [[1, N]], -1, N)
+    io("iob", Rf("IOB", 0, 16), [[256, 16]], 0)
+    io("tc", Rf("TC", 0, NT * 16), [[4096, NT], [0, 16]], 0, 4096)
+    I = Rf("WI", 16, 16 + N)
+    ONE = M("ONE")
+    V("WI", ts(Rf("WI", 0, 160), Rf("IOC", 0, 160), -16.0, A.add, c1("PC"), A.is_equal))
     V("PG", ts(c1("PG"), c1("PI"), 4, A.arith_shift_right))
-    V("PH", ts(c1("PH"), c1("PI"), 5, A.arith_shift_right))
     V("PK", ts(c1("PK"), c1("PI"), 15, A.bitwise_and))
     V("PO", ts(c1("PO"), c1("PG"), 1, A.bitwise_and))
-    V("C15", ts(c1("C15F"), c1("PG"), 16.0, A.mult, 15.0, A.add))
-    V("BIG", ts(B("BIG"), B("IOC"), c1("C15F"), A.is_equal))
-    V("C0", ts(c1("C0F"), c1("PG"), 16.0, A.mult))
-    V("D0", ts(c1("D0F"), c1("PH"), 32.0, A.mult))
-    V("D31", ts(c1("D31F"), c1("PH"), 32.0, A.mult, 31.0, A.add))
     V("ODC", ts(c1("ODC"), c1("PO"), 1.0, A.mult))
     V("EVC", ts(c1("EVC"), c1("PO"), 0.0, A.is_equal))
-    V("W2", ts(c1("W2"), c1("PK"), 2.0, A.mult, 1.0, A.add))
+    V("EVW", ts(Rf("EVW", 0, 160), Rf("WI", 0, 160), c1("EVC"), A.mult))
+    V("ODW", ts(Rf("ODW", 0, 160), Rf("WI", 0, 160), c1("ODC"), A.mult))
+    V("PGF", ts(c1("PGF"), c1("PG"), 1.0, A.mult))
+    V("C15", ts(c1("C15F"), c1("PG"), 16.0, A.mult, 15.0, A.add))
+    V("WK", ts(c1("WK"), c1("PK"), 2.0, A.mult, 1.0, A.add))
     V("K16", ts(c1("K16"), c1("PK"), 16.0, A.mult))
-    V("R0", ts(c1("R0"), c1("PK"), 0.0, A.is_equal))
     V("BASE", ts(Rf("BASE", 0, 16), Rf("IOB", 0, 16), c1("K16"), A.add))
-    V("BIGW", ts(B("BIGW"), B("BIG"), c1("W2"), A.mult))
-    V("BIG2", ts(B("BIG2"), B("BIG"), 2.0, A.mult))
-    V("BIGN", ts(B("BIGN"), B("BIG"), -1.0, A.mult))
-    V("BIG0B", ts(B("BIG0B"), B("BIG"), c1("R0"), A.mult))
-    V("BIG16", ts(B("BIG16"), B("BIG"), 1.0, A.mult))
-    V("CA", ts(C("CA"), C("IOC"), c1("C0F"), A.is_ge))
-    V("CB", ts(C("CB"), C("IOC"), c1("C15F"), A.is_le))
-    V("OB", tt(C("OB"), C("CA"), C("CB"), A.mult))
-    V("IFF", ts(C("IFF"), C("IOC"), c1("PC"), A.is_equal))
-    V("T1", ts(C("T1"), C("IOC"), c1("PC"), A.is_gt))
-    V("LF", tt(C("LF"), C("T1"), C("CB"), A.mult))
-    V("IB", ts(C("IB"), C("IFF"), 1.0, A.mult))
-    V("NIB", ts(C("NIB"), C("IFF"), -1.0, A.mult))
-    V("I16", ts(C("I16"), C("IFF"), 1.0, A.mult))
-    V("NI16", ts(C("NI16"), C("IFF"), -1.0, A.mult))
-    V("T2", tt(C("T2"), C("IFF"), C("LF"), A.subtract))
-    V("G1", ts(C("G1"), C("T2"), 4096.0, A.mult))
-    V("N4", ts(C("N4"), C("OB"), -4096.0, A.mult))
-    V("K4", ts(C("K4"), C("IFF"), 4096.0, A.mult))
-    V("ONESB", ts(C("ONESB"), C("OB"), 1.0, A.mult))
-    V("PBa", ts(C("T1"), C("IOC"), c1("D0F"), A.is_ge))
-    V("PBb", ts(C("T2"), C("IOC"), c1("D31F"), A.is_le))
-    V("PB", tt(C("PB"), C("T1"), C("T2"), A.mult))
-    V("EV", ts(C("EV"), C("PB"), c1("EVC"), A.mult))
-    V("OD", ts(C("OD"), C("PB"), c1("ODC"), A.mult))
-    V("EV0", ts(C("EV0"), C("PB"), c1("EVC"), A.mult, c1("R0"), A.mult))
-    V("OD0", ts(C("OD0"), C("PB"), c1("ODC"), A.mult, c1("R0"), A.mult))
-    V("EVB", ts(C("EVB"), C("PB"), c1("EVC"), A.mult))
-    V("ODB", ts(C("ODB"), C("PB"), c1("ODC"), A.mult))
-    V("ONE", [("memset", dict(ap=Rf("ONE", 0, N), constant=1.0))])
-    V("A17", ts(C("A17"), C("OB"), 17.0, A.mult))
-    V("N34", ts(C("N34"), C("OB"), -34.0, A.mult))
-    V("PQ", ts(C("PQ"), C("IFF"), 2048.0, A.mult))
-    V("NQ", ts(C("NQ"), C("IFF"), -2048.0, A.mult))
-    V("NL", ts(C("NL"), C("LF"), -4096.0, A.mult))
-    V("NK4", ts(C("NK4"), C("IFF"), -4096.0, A.mult))
-    V("SHa", ts(C("T1"), C("IOC"), -1.0, A.add, c1("PC"), A.is_equal))
-    V("SHb", tt(C("T2"), C("T1"), C("CB"), A.mult))
-    V("SHI", tt(C("SHI"), C("T2"), C("IFF"), A.subtract))
-    V("R00", ts(C("R00"), C("IFF"), c1("R0"), A.mult))
-    V("R0K", ts(C("R0K"), C("R00"), 65536.0, A.mult))
-    V("N64", ts(C("N64"), C("IFF"), -64.0, A.mult))
-    for p in range(NP):
-        a = p * N
-        V("SU0", cp(Rf("SU", a, a + N), Rf("S0", a, a + N)))
-    V("S160", ts(Rf("S16", 0, NA), Rf("S0", 0, NA), -2048.0, A.add))
+    V("BIG", ts(Rf("BIG", 0, 144), Rf("IOC", 0, 144), c1("C15F"), A.is_equal))
+    V("BIGW", ts(Rf("BIGW", 0, 144), Rf("BIG", 0, 144), c1("WK"), A.mult))
+    V("GS", ts(Rf("GS", 0, 8), Rf("IOC", 0, 8), c1("PGF"), A.is_equal))
+    V("GN", ts(Rf("GN", 0, 8), Rf("IOC", 0, 8), c1("PGF"), A.is_equal, -1.0, A.mult))
+    V("GH", ts(Rf("GH", 0, 8), Rf("IOC", 0, 8), c1("PGF"), A.is_equal, -0.5, A.mult))
+    V("ONE", [("memset", dict(ap=ONE, constant=1.0))])
+    V("A8", ts(M("A8"), M("IO8"), 7, A.bitwise_and))
+    V("O8", ts(M("O8"), M("A8"), 0.0, A.is_equal))
+    V("GT", ts(M("GT"), M("IOC"), c1("PC"), A.is_gt))
+    V("LT", tt(M("LT"), M("O8"), M("GT"), A.mult))
+    for nm, k in (("NIB", -1.0), ("HI", 0.5), ("I32", 32.0), ("N64", -64.0), ("PQ", 2048.0), ("NQ", -2048.0), ("NK4", -4096.0), ("K4", 4096.0),
+                  ("Q256", 256.0)):
+        V(nm, ts(M(nm), I, k, A.mult))
+    V("CT", ts(M("CT"), I, -0.6875, A.mult, 8.0, A.add))
+    V("N4", ts(M("N4"), M("O8"), -4096.0, A.mult))
+    V("N2", ts(M("N2"), M("O8"), -2048.0, A.mult))
+    V("T1", tt(M("T1"), I, M("LT"), A.subtract))
+    V("G1", ts(M("G1"), M("T1"), 4096.0, A.mult))
+    V("G1H", ts(M("G1H"), M("T1"), 2048.0, A.mult))
+    V("T2", tt(M("T2"), I, M("LT"), A.add))
+    V("NLI", ts(M("NLI"), M("T2"), -4096.0, A.mult))
+    V("T1b", ts(M("T1"), M("T1"), -16.0, A.mult))
+    V("T2b", tt(M("T2"), M("O8"), I, A.subtract))
+    V("SM", tt(M("SM"), M("T1"), M("T2"), A.add))
+    V("SHI", tt(M("SHI"), Rf("WI", 8, 8 + N), I, A.subtract))
+    if "S" in opt["w"]:
+        V("KS32", cp(Rf("KS32", 0, 8), Rf("O8", 0, 8)))
+        V("NI32", ts(M("NI32"), I, -1.0, A.mult))
+
+    def turned(j, bank):
+        V("TT", tr(Rf("TT", j * NA, j * NA + NA), Rf("KT", j * NA, j * NA + NA)))
+        ins = []
+        for c in range(2):
+            it = [(reg(bank, c), M("PQ"), ONE)]
+            for h in range(4):
+                for b in range(2):
+                    for gl in range(2):
+                        a = (2 * j + c) * N + 32 * h + 16 * gl
+                        it.append((Rf("ps%d" % bank, c * N + 2 * h + b, c * N + N, 8), half(b, gl), Rf("TT", a, a + 16)))
+            ins += acc(it)
+        PE("psA", ins)
+        return reg(bank, 0, 2)
+    V("KS", ts(Rf("KT", 0, NA), Rf("S0", 0, NA), -2048.0, A.add))
+    V("SU0", cp(Rf("SU", 0, NA), turned(0, 7)))
+    V("S160", ts(Rf("S16", 0, NA), Rf("SU", 0, NA), -2048.0, A.add))
+    V("KH", ts(Rf("KT", NA, 2 * NA), Rf("TH", 0, NA), -2048.0, A.add))
+    V("THA", ts(Rf("THA", 0, NA), turned(1, 5), -2048.0, A.add))
     V("F160", ts(Rf("F16", 0, NA), Rf("F0", 0, NA), 1024.0, A.add))
     V("PU", cp(Rf("PU", 0, 16), Rf("P0", 0, 16)))
-    V("PF0", cp(Rf("PF", 0, 16), Rf("P0", 0, 16)))
-    V("PA0", [("memset", dict(ap=Rf("PA", 0, 16), constant=0.0))])
+    V("KE", ts(Rf("KT", 2 * NA, 3 * NA), ind(Rf("PL", 0, NR), Rf("PU", 0, 16)), -2048.0, A.add))
+    V("EU0", cp(Rf("EU", 0, NA), turned(2, 6)))
+    V("E160", ts(Rf("E16", 0, NA), Rf("EU", 0, NA), -2048.0, A.add))
     Xa = Rf("X", 0, NR)
-    I16, IB = M("I16"), M("IB")
+    KS = Rf("O8", 0, 8)
+    shut = None
     for t in range(NT):
         last = t == NT - 1
         o = t * NA
-        par = t % 2
-        zc = lambda a, b, s=1, o=o: Rf("Z", o + a, o + b, s)
-        ordr = ORDER[t]
-        loc = (-t) % 4
-        k0, k1 = t * 16, t * 16 + 16
         U = lambda nm: Rf(nm, t * 16, t * 16 + 16)
-
-        def hash_():
-            PE("psU", acc(Rf("ps6", 448, 464), [(sel(m, "BIGW"), zc(m, NA, 16)) for m in range(16)]))
-            V("U1", cp(U("U1"), Rf("ps6", 448, 464)))
-            V("U2", ts(U("U2"), U("U1"), 4095, A.bitwise_and))
-            V("U3", tt(U("U3"), U("U2"), U("U2"), A.mult))
-            V("U5", ts(U("U5"), U("U2"), 37.0, A.mult))
-            V("U4", ts(U("U4"), U("U3"), 5, A.arith_shift_right))
-            V("U6", tt(U("U6"), U("U4"), U("U5"), A.add))
-            V("UH", ts(U("UH"), U("U6"), 4095, A.bitwise_and))
-            V("UU", cp(U("UU"), U("UH")))
-            V("EH", ts(Rf("EH", o, o + NA), ind(Rf("PL", 0, NR), U("UU")), -2048.0, A.add))
-
-        pairs = []
-        for p in ordr:
-            if p // 2 not in pairs:
-                pairs.append(p // 2)
-        for h in pairs:
-            a = 2 * N * h
-            for k in range(16):
-                b0 = par * NR + 16 * a
-                ref = Rf("ZE", b0 + k, b0 + 32 * N, 16)
-                e = OPT["ze0"] if t == 0 else OPT["ze"][pairs.index(h)]
-                if e[k] == "S":
-                    S("ze", act(ref, zc(a, a + 2 * N), AF.Copy))
-                elif e[k] == "G":
-                    add(P, "G", "ze", [("affine", dict(out=ref, in_=zc(a, a + 2 * N)))])
+        zb = R2("Z4", 2 * t, 2 * t + 2, 0, N)
+        for c in range(2):
+            z0 = (2 * t + c) * 512
+            G("zx", [("affine", dict(out=Rf("Z4", z0 + N, z0 + 2 * N), in_=Rf("Z4", z0, z0 + N)))])
+            G("zx", [("affine", dict(out=Rf("Z4", z0 + 2 * N, z0 + 4 * N), in_=Rf("Z4", z0, z0 + 2 * N)))])
+        PE("psF", acc([(reg(2, 2, 2), I, Rf("F16", o, o + NA)), (reg(2, 2, 2), I, zb)]))
+        V("F16", ts(Rf("F16", o + NA, o + 2 * NA), reg(2, 2, 2), 0.5, A.mult, 511.75, A.add))
+        pu = Rf("ps6", 2 * N + 16, 2 * N + 32)
+        PE("psU", acc([(pu, sel(m, "BIGW"), R2("Z4", 2 * t, 2 * t + 2, m, N, 16)) for m in range(16)]))
+        V("U1", cp(U("U1"), pu))
+        V("U2", ts(U("U2"), U("U1"), 4095, A.bitwise_and))
+        V("U3", tt(U("U3"), U("U2"), U("U2"), A.mult))
+        V("U5", ts(U("U5"), U("U2"), 37.0, A.mult))
+        V("U4", ts(U("U4"), U("U3"), 5, A.arith_shift_right))
+        V("U6", tt(U("U6"), U("U4"), U("U5"), A.add))
+        V("UH", ts(U("UH"), U("U6"), 4095, A.bitwise_and))
+        V("UU", cp(U("UU"), U("UH")))
+        V("EK", ts(Rf("EK", o, o + NA), ind(Rf("PL", 0, NR), U("UU")), -2048.0, A.add))
+        V("ET", tr(Rf("ET", o, o + NA), Rf("EK", o, o + NA)))
+        ep = opt["ep0"] if t == 0 else opt["ep"]
+        zturn = 0
+        for c in range(2):
+            P["up"] = opt["up"][c]
+            a, d0 = o + c * N, c * L
+            z4 = Rf("Z4", (2 * t + c) * 512, (2 * t + c + 1) * 512)
+            z = Rf("Z4", (2 * t + c) * 512, (2 * t + c) * 512 + N)
+            lane = lambda nm, ii: Rf(nm, d0 + ii, d0 + L, 16)
+            pc = lambda nm, k=1: Rf(nm, k * c * N, k * c * N + k * N)
+            th = pc("THA")
+            hist = lambda out, m: [(out, Rf("SW", (2 * u + c) * N, (2 * u + c + 1) * N), M(m)) for u in range(t)]
+            sums = lambda bank, j, nm, g8: [(Rf("ps%d" % bank, N * j + ii, N * j + N, 16), lane(nm, ii), Rf(g8, 0, 8)) for ii in range(16)]
+            for j in range(4):
+                V("GS", tt(Rf("DS", d0 + 512 * j, d0 + 512 * j + 512), ind(Xa, Rf("SU", a + 32 * j, a + 32 * j + 32)), z4, A.subtract))
+            hh = opt["hh"][c]
+            for j in range(hh):
+                x0, x1 = d0 + L // hh * j, d0 + L // hh * (j + 1)
+                V("H", ts(Rf("HS", x0, x1), Rf("DS", x0, x1), 127.9375, A.add, 128.0, A.min))
+            bw = 2 + c
+            PE("psW", acc([(reg(bw, 0), th, M("HI"))] + hist(reg(bw, 0), "I32") + sums(bw, 0, "DS", "GH")))
+            PE("psH", acc([(reg(bw, 1), M("CT"), ONE)] + sums(bw, 1, "HS", "GN")))
+            ni = pc("NI")
+            par = (t % 2) * NA + c * N
+            r, rho, q = Rf("RR", par, par + N), Rf("RP", par, par + N), Rf("QQ", par, par + N)
+            V("NI", ts(ni, reg(bw, 1), 0.15625, A.add, -1024.0, A.max))
+            V("RR", tt(r, ni, reg(bw, 0), A.is_lt))
+            V("QQ", tt(q, ni, reg(bw, 1), A.is_lt))
+            ge = opt["ge"][c]
+            for j in range(4):
+                x0, x1 = d0 + 512 * j, d0 + 512 * j + 512
+                eu = Rf("EU", a + 32 * j, a + 32 * j + 32)
+                if ep[c][j] == "S":
+                    if ge == 512:
+                        S("GE", act(Rf("DE", x0, x1), ind(Xa, eu), AF.Copy))
+                    elif j % 2 == 0:
+                        S("GE", act(Rf("DE", x0, x1 + 512), ind(Xa, Rf("EU", a + 32 * j, a + 32 * j + 64)), AF.Copy))
+                    zk = reg(zturn % 2, 0, 4)
+                    zturn += 1
+                    PE("psZ", acc([(zk, M("NIB"), z4), (zk, I, Rf("DE", x0, x1))]))
+                    S("AE", act(Rf("AE", x0, x1), zk, AF.Abs))
                 else:
-                    V("ze", cp(ref, zc(a, a + 2 * N)))
-        if t == 0:
-            V("E160", ts(Rf("E16", 0, NA), ind(Rf("PL", 0, NR), Rf("PU", 0, 16)), -2048.0, A.add))
-            V("EU0", ts(Rf("EU", 0, NA), Rf("E16", 0, NA), 2048.0, A.add))
-        ep = OPT["ep0"] if t == 0 else OPT["ep"]
-        for ip, p in enumerate(ordr):
-            if ep[ip] == "S":
-                a = p * N
-                for h in range(2):
-                    x0 = par * NR + 16 * a + 8 * N * h
-                    x1 = x0 + 8 * N
-                    S("GEs", act(Rf("DE", x0, x1), ind(Xa, Rf("EU", o + a + N // 2 * h, o + a + N // 2 * (h + 1))), AF.Copy))
-                    PE("psZ", acc(Rf("ps7", 0, 512), [(IB, Rf("DE", x0, x1)), (M("NIB"), Rf("ZE", x0, x1))]))
-                    S("AE", act(Rf("AE", x0, x1), Rf("ps7", 0, 512), AF.Abs))
-        sub, later = [], []
-        for ip, p in enumerate(ordr):
-            a = p * N
-            b16 = par * NR + 16 * a
-            e16 = b16 + 16 * N
-            pq = ip % 2
-            z = zc(a, a + N)
-            big = lambda nm: Rf(nm, b16, e16)
-            D, K, L = "ps%d" % pq, "ps%d" % (2 + pq), "ps%d" % (4 + pq)
-            if ip == 0:
-                PE("psF", acc(Rf("ps2", 256, 512), [(I16, Rf("F16", o, o + NA)), (IB, zc(0, NA))]))
-                V("F16", ts(Rf("F16", o + NA, o + 2 * NA), Rf("ps2", 256, 512), 0.5, A.mult, 511.75, A.add))
-            eu = Rf("EU", o + a, o + a + N)
-            gh = OPT["gh"][ip]
-            for h in range(gh):
-                x0, x1 = b16 + 16 * N // gh * h, b16 + 16 * N // gh * (h + 1)
-                V("GS", tt(Rf("DS", x0, x1), ind(Xa, Rf("SU", o + a + N // gh * h, o + a + N // gh * (h + 1))), Rf("ZE", x0, x1), A.subtract))
-            wS = [(sel(k), Rf("AS", b16 + k, e16, 16)) for k in range(16)]
-            if OPT["sa"][ip] == "V":
-                V("RS", ts(big("AS"), big("DS"), 0.0, A.max))
-                wS = [(sel(k, "BIGN"), Rf("DS", b16 + k, e16, 16)) for k in range(16)] + [(sel(k, "BIG2"), Rf("AS", b16 + k, e16, 16)) for k in range(16)]
+                    V("GE", tt(Rf("DE", x0, x1), ind(Xa, eu), z4, A.subtract))
+                    S("AE", act(Rf("AE", x0, x1), Rf("DE", x0, x1), AF.Abs))
+            de = reg(4, c)
+            PE("psD", acc([(de, th, M("NIB"))] + hist(de, "N64") + sums(4, c, "AE", "GS")))
+            if opt["rho"][c] == "S":
+                S("RP", act(rho, de, AF.Sign, bias=2047.5, scale=-1.0))
+                g1r, n4r = M("G1H"), M("N2")
             else:
-                ah = OPT["ah"][ip]
-                for h in range(ah):
-                    x0, x1 = b16 + 16 * N // ah * h, b16 + 16 * N // ah * (h + 1)
-                    S("AS", act(Rf("AS", x0, x1), Rf("DS", x0, x1), AF.Abs))
-            wE = [(sel(k), Rf("AE", b16 + k, e16, 16)) for k in range(16)]
-            wN = []
-            if ep[ip] == "V":
-                V("GE", tt(big("DE"), ind(Xa, eu), big("ZE"), A.subtract))
-                if OPT["ea"][ip] == "V":
-                    V("RE", ts(big("AE"), big("DE"), 0.0, A.max))
-                    wN = [(sel(k, "BIGN"), Rf("DE", b16 + k, e16, 16)) for k in range(16)]
-                    wE = [(sel(k, "BIG2"), Rf("AE", b16 + k, e16, 16)) for k in range(16)]
-                else:
-                    S("AE", act(big("AE"), big("DE"), AF.Abs))
-            if OPT["lw"][ip] == "V":
-                V("LW", ts(big("LW"), big("DS"), 0.0, A.is_le))
+                V("RP", ts(rho, de, 2047.5, A.is_lt, -0.5, A.add))
+                g1r, n4r = M("G1"), M("N4")
+            s16, e16 = Rf("S16", a, a + N), Rf("E16", a, a + N)
+            k0, k1, k2 = reg(5, 2 * c), reg(5, 2 * c + 1), reg(6, c)
+            PE("psK0", acc([(k0, s16, I), (k0, M("G1"), r)]))
+            PE("psK1", acc([(k1, e16, I), (k1, M("G1H"), ONE), (k1, M("N4"), r), (k1, g1r, rho)]))
+            it = [(k2, ONE, M("N2"))]
+            for h in range(4):
+                for b in range(2):
+                    for gl in range(2):
+                        x0 = a + 32 * h + 16 * gl
+                        it.append((Rf("ps6", c * N + 2 * h + b, c * N + N, 8), half(b, gl), Rf("ET", x0, x0 + 16)))
+            PE("psK2", acc(it, stop=False), opens="ps6", extra=[shut] if shut is not None else None)
+            PE("psK2", acc([(k2, r, M("N4")), (k2, rho, n4r)], start=False), closes="ps6")
+            w2 = pc("W2")
+            V("W2", ts(w2, k2, -2048.0, A.max))
+            pt = Rf("ps6", 2 * N + 8 * c, 2 * N + 8 * c + 8)
+            w20 = Rf("W2", c * N, c * N + 8)
+            if opt["w"][c] == "S":
+                S("W", act(pc("WF", 2), reg(5, 2 * c, 2), AF.Relu, bias=-2048.0))
+                w0, w1 = Rf("WF", 2 * c * N, 2 * c * N + N), Rf("WF", 2 * c * N + N, 2 * c * N + 2 * N)
+                shut = PE("psT", acc([(pt, I, w20), (pt, w0, Rf("KS32", 0, 8)), (pt, w1, Rf("KS32", 0, 8))]))
+                top, rest, nw = 2048.0, 4096.0, "NI32"
             else:
-                S("LW", act(big("LW"), big("DS"), AF.Sign, bias=-0.5))
-            hist = [(M("N64"), Rf("SW", u * NA + a, u * NA + a + N)) for u in range(t)]
-            P["up"] = OPT["up"][ip]
-            xs = PE("psDs", acc(Rf(D, 0, N), hist + wS))
-            if wN:
-                both = acc(Rf(D, N, 2 * N), hist + wN + wE)
-                P["tasks"][PE("psDe", both[:-16], extra=[xs])]["opens"] = D
-                P["tasks"][PE("psDe", both[-16:])]["closes"] = D
-            else:
-                PE("psDe", acc(Rf(D, N, 2 * N), hist + wE))
-            rb = par * 2 * NA + 2 * a
-            r, rp = Rf("RR", rb, rb + N), Rf("RR", rb + N, rb + 2 * N)
-            V("RR", tt(r, Rf(D, 0, N), Rf("TH", a, a + N), A.is_lt))
-            V("RP", tt(rp, Rf(D, N, 2 * N), Rf("TH", a, a + N), A.is_lt))
-            if ip == 0:
-                hash_()
-            s16, e_16 = Rf("S16", o + a, o + a + N), Rf("E16", o + a, o + a + N)
-            eh = Rf("EH", o + a, o + a + N)
-            one = Rf("ONE", 0, N)
-            PE("psK", acc(Rf(K, 0, N), [(I16, s16), (M("G1"), r)]) +
-               acc(Rf(K, N, 2 * N), [(I16, e_16), (M("G1"), rp), (M("N4"), r)]) +
-               acc(Rf(K, 2 * N, 3 * N), [(I16, eh), (M("K4"), one), (M("N4"), r), (M("N4"), rp)]))
-            wb = par * 4 * NA + 4 * a
-            V("W", ts(Rf("WW", wb, wb + 3 * N), Rf(K, 0, 3 * N), -4096.0, A.add, -2048.0, A.max))
-            w = lambda j, wb=wb: Rf("WW", wb + j * N, wb + j * N + N)
-            PE("psT", acc(R3(L, 0, 2 * N, 0), [(M("EV"), w(0)), (M("EV"), w(1)), (M("EV0"), w(2))]) +
-               acc(R3(L, 0, 2 * N, 1), [(M("OD"), w(0)), (M("OD"), w(1)), (M("OD0"), w(2))]))
-            tb = (par * 4 + ip) * 128
-            V("TRT", tr(Rf("TRT", tb, tb + 2 * N), R3(L, 0, 2 * N)))
-
-            def top_and_y(ip=ip, p=p, a=a, K=K, L=L, z=z, tb=tb):
-                l0 = t * 16 + 4 * ip
-                yd = Rf("YD", o + a, o + a + N)
-                V("YD", tt(yd, ind(Xa, Rf("LST", l0, l0 + 4)), Rf("F16", o + NA + a, o + NA + a + N), A.subtract))
-                if p == loc and not last:
-                    y = Rf("Z", o + NA + a, o + NA + a + N)
-                else:
-                    y = Rf("Y", o + a, o + a + N)
-                S("Y", act(y, yd, AF.Abs, bias=1024.0))
-                if p != loc and not last:
-                    add(P, "G", "send", [("send", dict(src=y, t=t, b=p))], dur=0.3, sem="none")
-                    add(P, "N", "recv", [], wr=[Rf("Z", o + NA + a, o + NA + a + N)], dur=EST["net"], sem="za%d%d" % (t + 1, p), inc=0, extra=[len(P["tasks"]) - 1])
-                PE("psY", acc(R3(L, 2 * N, 4 * N, 0), [(M("EVB"), y)]) + acc(R3(L, 2 * N, 4 * N, 1), [(M("ODB"), y)]) +
-                   acc(Rf(K, 6 * N, 7 * N), [(IB, y), (IB, z)]))
-                V("TRY", tr(Rf("TRY", tb, tb + 2 * N), R3(L, 2 * N, 4 * N)))
-                V("XN", ts(Rf("XN", o + a, o + a + N), Rf(K, 6 * N, 7 * N), 0.5, A.mult, -0.25, A.add))
-            later.append(top_and_y)
-            for grp in OPT["tops"]:
-                if grp[-1] == ip:
-                    l0, l1 = t * 16 + 4 * grp[0], t * 16 + 4 * ip + 4
-                    V("LST", ts(Rf("LST", l0, l1), Rf("TRT", (par * 4 + grp[0]) * 128, tb + 2 * N, 32), 67584.0, A.add))
-                    for j in grp:
-                        later[j]()
-            for grp in OPT["places"]:
-                if grp[-1] == ip:
-                    l0, l1 = t * 16 + 4 * grp[0], t * 16 + 4 * ip + 4
-                    V("PI1", cp(Rf("PI1", l0, l1), Rf("TRY", (par * 4 + grp[0]) * 128, tb + 2 * N, 32)))
-                    V("PI2", ts(Rf("PI2", l0, l1), Rf("PI1", l0, l1), 15, A.bitwise_and))
-                    V("PI3", tt(Rf("PI3", l0, l1), Rf("PI2", l0, l1), Rf("BASE", 0, l1 - l0), A.add))
-                    V("PLC", cp(Rf("PLC", l0, l1), Rf("PI3", l0, l1)))
-            P["up"] = 0.0
-            qb, fm = Rf("QB", o + a, o + a + N), Rf("FM", o + a, o + a + N)
-            S7 = "ps%d" % OPT["s7"][ip]
-            PE("psJ", acc(Rf(D, 5 * N, 6 * N), [(M("G1"), r)]))
-            S("FM", act(fm, Rf(D, 5 * N, 6 * N), AF.Relu, scale=1.0 / 4096))
-            wL = [(sel(k), Rf("LW", b16 + k, e16, 16)) for k in range(16)]
-            if OPT["lw"][ip] == "V":
-                PE("psLo", acc(Rf(S7, 5 * N, 6 * N), wL + [(M("A17"), fm)]))
-                S("QB", act(qb, Rf(S7, 5 * N, 6 * N), AF.Sign, bias=-28.5))
-            else:
-                PE("psLo", acc(Rf(S7, 5 * N, 6 * N), wL + [(M("N34"), fm)]))
-                S("QB", act(qb, Rf(S7, 5 * N, 6 * N), AF.Sign, bias=-41.0, scale=-1.0))
-            PE("psW", acc(Rf(D, 2 * N, 3 * N), [(M("ONESB"), r), (M("ONESB"), rp)]) +
-               [])
-            S("SW", act(Rf("SW", o + a, o + a + N), Rf(D, 2 * N, 3 * N), AF.Relu, bias=1.0, scale=-1.0))
+                V("W", ts(pc("WH", 2), reg(5, 2 * c, 2), -4096.0, A.add, -2048.0, A.max))
+                w0, w1 = Rf("WH", 2 * c * N, 2 * c * N + N), Rf("WH", 2 * c * N + N, 2 * c * N + 2 * N)
+                shut = PE("psT", acc([(pt, I, w20), (pt, w0, KS), (pt, w1, KS)]))
+                top, rest, nw = 2048.0 * 33, 2048.0, "NIB"
+            lst = Rf("SU", a + NA, a + NA + 8)
+            V("LST", ts(lst, pt, top, A.add))
+            yd, y = Rf("YD", a, a + N), Rf("Y", a, a + N)
+            V("YD", tt(yd, ind(Xa, lst), Rf("F16", a + NA, a + NA + N), A.subtract))
+            S("Y", act(y, yd, AF.Abs, bias=1024.0))
             if not last:
-                en = Rf("E16", o + NA + a, o + NA + a + N)
-                PE("psE", acc(Rf(D, 3 * N, 4 * N), [(I16, e_16), (M("NK4"), Rf("SW", o + a, o + a + N))]))
-                V("E16", tt(en, w(2), Rf(D, 3 * N, 4 * N), A.max))
-                V("EU", ts(Rf("EU", o + NA + a, o + NA + a + N), en, 2048.0, A.add))
-            sub.append((p, a, OPT["s7"][ip], r, rp, s16, e_16, fm, qb, w))
-        for ip, (p, a, pq, r, rp, s16, e_16, fm, qb, w) in enumerate(sub):
-            l0, l1 = t * 16 + 4 * ip, t * 16 + 4 * ip + 4
-            V("SC", [("tensor_copy", dict(out=ind(Rf("X", 16 * a, 16 * (a + N)), Rf("PLC", l0, l1)), in_=Rf("XN", o + a, o + a + N)))])
-        for p, a, pq, r, rp, s16, e_16, fm, qb, w in sub:
-            S7 = "ps%d" % pq
-            PE("psX", acc(Rf(S7, 0, N), [(I16, s16), (M("NQ"), qb), (M("NK4"), fm)]) + acc(Rf(S7, N, 2 * N), [(I16, e_16), (M("PQ"), qb), (M("NK4"), fm)]))
-            sb = par * 2 * NA + 2 * a
-            V("SE", ts(Rf("SE", sb, sb + 2 * N), Rf(S7, 0, 2 * N), -2048.0, A.add, -2048.0, A.max))
-            sx, ex = Rf("SE", sb, sb + N), Rf("SE", sb + N, sb + 2 * N)
-            PE("psM", acc(Rf(S7, 2 * N, 3 * N), [(I16, sx), (I16, ex), (M("NL"), r)]))
-            m = Rf("MM", sb, sb + N)
-            V("MM", ts(m, Rf(S7, 2 * N, 3 * N), 2048.0, A.add, -2048.0, A.max))
-            row0 = sel(0, "BIG16")
-            PE("psS", acc(Rf(S7, 4 * N, 5 * N), [(I16, sx), (I16, ex), (row0, w(0)), (row0, w(1)), (M("R00"), w(2)), (M("R0K"), one), (M("SHI"), m)]))
+                for b in (2 * c, 2 * c + 1):
+                    src = Rf("Y", o + NB * b, o + NB * b + NB)
+                    x0 = (2 * t + 2 + c) * 512 + NB * (b % 2)
+                    dst = Rf("Z4", x0, x0 + NB)
+                    if (b + t) % 4:
+                        i = G("send", [("send", dict(in_=src, to=["Z4", x0], t=t, b=b))], dur=0.3, sem="none")
+                        add(P, "N", "recv", [], wr=[dst], dur=EST["net"], sem="za%d%d" % (t + 1, b), inc=0, extra=[i])
+                    else:
+                        add(P, "Y", "stay", [("copy", dict(out=dst, in_=src))], dur=0.1, sem="za%d%d" % (t + 1, b), inc=16, prio=2.2)
+            xn = reg(3, 2 + c)
+            PE("psN", acc([(xn, I, z), (xn, I, y)]))
+            V("XN", ts(Rf("XN", a, a + N), xn, 0.5, A.mult, -0.25, A.add))
+            if opt["split"] or c == 1:
+                c0 = c if opt["split"] else 0
+                l0, l1 = 16 * t + 8 * c0, 16 * t + 8 * c + 8
+                py = Rf("ps6", 3 * N + 8 * c0, 3 * N + 8 * c + 8)
+                PE("psY", acc([(py, sel(m), Rf("Y", o + c0 * N + m, a + N, 16)) for m in range(16)]))
+                W = lambda nm: Rf(nm, l0, l1)
+                V("PI1", cp(W("PI1"), py))
+                V("PI2", ts(W("PI2"), W("PI1"), 15, A.bitwise_and))
+                V("PI3", tt(W("PI3"), W("PI2"), Rf("BASE", 0, l1 - l0), A.add))
+                V("PLC", cp(W("PLC"), W("PI3")))
+            P["up"] = 0.0
+            sw = Rf("SW", (2 * t + c) * N, (2 * t + c + 1) * N)
+            cn = reg(4, 2 + c)
+            PE("psC", acc([(cn, r, M("N4")), (cn, rho, n4r)]))
+            S("SW", act(sw, cn, AF.Relu, bias=-7.0, scale=1.0 / 4096))
+            if not last:
+                en = Rf("E16", a + NA, a + NA + N)
+                PE("psE", acc([(cn, I, e16), (cn, M("NK4"), sw)]))
+                V("E16", tt(en, w2, cn, A.max))
+                V("EU", ts(Rf("EU", a + NA, a + NA + N), en, 2048.0, A.add))
+            ms = pc("MS")
+            PE("psQ", acc([(reg(7, 0), M("SM"), r), (reg(7, 0), M("Q256"), q)]))
+            S("MS", act(ms, reg(7, 0), AF.Sign, bias=-256.5))
+            PE("psX", acc([(reg(7, 1), s16, I), (reg(7, 1), M("NQ"), ms)]) + acc([(reg(7, 2), e16, I), (reg(7, 2), M("PQ"), ms)]))
+            V("SE", ts(pc("SE", 2), reg(7, 1, 2), -2048.0, A.add, -2048.0, A.max))
+            sx, ex = Rf("SE", 2 * c * N, 2 * c * N + N), Rf("SE", 2 * c * N + N, 2 * c * N + 2 * N)
+            PE("psM", acc([(reg(7, 3), I, sx), (reg(7, 3), I, ex), (reg(7, 3), M("NLI"), r)]))
+            mm_ = pc("MM")
+            V("MM", ts(mm_, reg(7, 3), 2048.0, A.add, -2048.0, A.max))
+            sn, i8 = Rf("ps7", 8, N), Rf("WI", 24, 16 + N)
+            PE("psS", acc([(sn, sx, i8), (sn, ex, i8), (sn, w0, Rf(nw, 8, N)), (sn, mm_, Rf("SHI", 8, N))]))
+            V("SU", ts(Rf("SU", a + NA + 8, a + NA + N), sn, rest, A.add))
+            V("S16", ts(Rf("S16", a + NA, a + NA + N), Rf("SU", a + NA, a + NA + N), -2048.0, A.add))
             if last:
-                V("YS", ts(Rf("YSO", a, a + N), Rf(S7, 4 * N, 5 * N), 4096.0, A.add))
-            else:
-                V("SU", ts(Rf("SU", o + NA + a, o + NA + a + N), Rf(S7, 4 * N, 5 * N), 4096.0, A.add))
-                V("S16", ts(Rf("S16", o + NA + a, o + NA + a + N), Rf(S7, 4 * N, 5 * N), 2048.0, A.add))
-        PE("psP", acc(Rf("ps6", 464, 480), [(sel(m, "BIG0B"), Rf("SW", o + m, o + NA, 16)) for m in range(16)]))
-        V("PA", tt(Rf("PA", k0 + 16, k1 + 16), Rf("PA", k0, k1), Rf("ps6", 464, 480), A.add))
-        V("PD", tt(Rf("PD", k0, k1), Rf("UH", k0, k1), Rf("PF", k0, k1), A.subtract))
-        V("PM", tt(Rf("PM", k0, k1), Rf("PD", k0, k1), Rf("ps6", 464, 480), A.mult))
-        V("PF", tt(Rf("PF", k0 + 16, k1 + 16), Rf("PF", k0, k1), Rf("PM", k0, k1), A.add))
-    k0 = NT * 16
-    V("YP1", ts(Rf("PM", k0, k0 + 16), Rf("PA", k0, k0 + 16), 4096.0, A.mult))
-    V("YP", tt(Rf("YPO", 0, 16), Rf("PM", k0, k0 + 16), Rf("PF", k0, k0 + 16), A.add))
+                bk = 2 + c
+                it = [(reg(bk, 0), M("PQ"), ONE)]
+                for h in range(4):
+                    for gl in range(2):
+                        for b in range(2):
+                            it.append((Rf("ps%d" % bk, 32 * h + 16 * gl, 32 * h + 16 * gl + 16), half(gl, b), Rf("S16", a + NA + 2 * h + b, a + NA + N, 8)))
+                PE("psO", acc(it))
+                V("YS", tr(pc("YSO"), reg(bk, 0)))
+        for c in range(2) if opt["split"] else (None,):
+            lo, hi = (0, 2) if c is None else (c, c + 1)
+            V("SC", cp(ind(Rf("X", lo * L, hi * L), Rf("PLC", 16 * t + 8 * lo, 16 * t + 8 * hi)), Rf("XN", o + lo * N, o + hi * N)))
+    for lo, hi in ((0, NT - 1), (NT - 1, NT)):
+        V("PT", tt(Rf("PT", 16 * lo, 16 * hi), Rf("UH", 16 * lo, 16 * hi), Rf("TC", 16 * lo, 16 * hi), A.add))
+        V("PV", tt(Rf("PV", 16 * lo, 16 * hi), Rf("PT", 16 * lo, 16 * hi), R2("SW", 2 * lo, 2 * hi, 0, 8), A.mult))
+    V("PW", tt(Rf("PW", 0, 32), Rf("PV", 0, 32), Rf("PV", 32, 64), A.max))
+    V("PW", tt(Rf("PW", 32, 48), Rf("PV", 64, 80), Rf("P0", 0, 16), A.max))
+    V("PW", tt(Rf("PW", 48, 64), Rf("PW", 0, 16), Rf("PW", 16, 32), A.max))
+    V("PW", tt(Rf("PW", 64, 80), Rf("PW", 32, 48), Rf("PW", 48, 64), A.max))
+    V("PW", tt(Rf("PW", 80, 96), Rf("PW", 64, 80), Rf("PV", 80, 96), A.max))
+    V("PW", ts(Rf("PW", 96, 112), Rf("PW", 80, 96), 4095, A.bitwise_and))
+    pa = Rf("ps4", 0, 16)
+    PE("psP", acc([(pa, M("K4"), R2("SW", 2 * t, 2 * t + 2, 0, 8)) for t in range(NT)]))
+    V("YP", tt(Rf("YPO", 0, 16), Rf("PW", 96, 112), pa, A.add))
     V("YF", ts(Rf("YFO", 0, NA), Rf("F16", NT * NA, NT * NA + NA), -1024.0, A.add))
     for c in range(16):
-        V("CI", ts(Rf("CI", c * 128, c * 128 + 128), C("IB"), float(c + 1), A.mult))
-    for p, a in [(x[0], x[1]) for x in sub]:
-        PE("psV", acc(Rf("ps%d" % (p % 2), a, a + N), [(Rf("CI", c * 128, c * 128 + 128), Rf("X", 16 * a + c, 16 * (a + N), 16)) for c in range(16)]))
-        S("YX", act(Rf("YXO", a, a + N), Rf("ps%d" % (p % 2), a, a + N), AF.Copy))
-    for k, (o_, b) in enumerate((("ys", "YSO"), ("yp", "YPO"), ("yf", "YFO"), ("yx", "YXO"))):
-        add(P, "Y", "st" + o_, [("store", dict(dst=o_, src=Rf(b, 0, SCRATCH[b][1][1])))], dur=0.1, sem="ost%d" % k, inc=16)
+        V("CI", ts(Rf("CI", c * N, c * N + N), I, float(c + 1), A.mult))
+    for c in range(2):
+        PE("psV", acc([(reg(c, 0), Rf("CI", k * N, k * N + N), Rf("X", c * L + k, c * L + L, 16)) for k in range(16)]))
+        S("YX", act(Rf("YXO", c * N, c * N + N), reg(c, 0), AF.Copy))
+    for k, (o_, b) in enumerate((("yf", "YFO"), ("yp", "YPO"), ("ys", "YSO"), ("yx", "YXO"))):
+        add(P, "Y", "st" + o_, [("store", dict(dst=o_, in_=Rf(b, 0, SCRATCH[b][1][1])))], dur=0.1, sem="ost%d" % k, inc=16, prio=2.0)
     return P
 
 
-def schedule(P):
+def schedule(P, e=None):
+    e = e or EST
     T = P["tasks"]
     n = len(T)
     succ = [[] for _ in range(n)]
     for t in T:
+        t["dur"] = duration(t["q"], t["ins"], e) if t["fix"] is None else t["fix"]
         for o, kind in t["pre"].items():
             succ[o].append((t["i"], kind))
 
@@ -523,13 +510,13 @@ def schedule(P):
         if a["inc"] == 16:
             return a["prio"]
         if a["q"] == b["q"]:
-            return 0.0 if a["q"] == "P" else EST["self_"]
-        return EST["lat"]
+            return 0.0 if a["q"] == "P" else e["self_"]
+        return e["lat"]
     far = [0.0] * n
     for i in range(n - 1, -1, -1):
-        far[i] = T[i]["dur"] + max([lat(i, j, k) + far[j] for j, k in succ[i]] or [0.0])
+        far[i] = T[i]["dur"] + max([lat(i, j, k) + far[j] for j, k in succ[i]] or [T[i]["prio"]])
     for i in range(n):
-        far[i] += T[i]["up"] + PRIO.get(T[i]["name"], 0.0)
+        far[i] += 4.0 if T[i]["name"] in HASH else T[i]["up"]
     ready = [0.0] * n
     left = [len(t["pre"]) for t in T]
     free = {}
@@ -542,7 +529,6 @@ def schedule(P):
             avail[T[i]["q"]].append(i)
     order, start = [], [0.0] * n
     held = {}
-
     opened = set()
 
     def er(i):
@@ -551,8 +537,8 @@ def schedule(P):
             if b in opened and T[i]["q"] == "P" and T[i].get("closes") != b:
                 return 1e9
             for q2, (e2, o2) in held.get(b, {}).items():
-                if q2 != T[i]["q"] and e2 + EST["lat"] > r:
-                    r = e2 + EST["lat"]
+                if q2 != T[i]["q"] and e2 + e["lat"] > r:
+                    r = e2 + e["lat"]
         return r
     while len(order) < n:
         best = None
@@ -568,9 +554,6 @@ def schedule(P):
         if q == "N":
             i = min(avail[q], key=lambda j: ready[j])
             s = ready[i]
-        elif q == "Y":
-            i = min(avail[q])
-            s = max(free[q], ready[i])
         else:
             c = [j for j in avail[q] if er(j) <= s + 0.03]
             d = [j for j in c if T[j]["inc"] == 16]
@@ -598,7 +581,7 @@ def schedule(P):
             left[j] -= 1
             if left[j] == 0:
                 avail[T[j]["q"]].append(j)
-    return order, start, max(free.values())
+    return order, start, max(start[i] + T[i]["dur"] + T[i]["prio"] for i in range(n))
 
 
 CACHE = {}
@@ -627,13 +610,17 @@ def rank_program(g, core, T, topo):
             return v
         if v[0] == "#":
             return ap(v[1]).indirect(ap(v[2]))
-        if len(v) == 5:
-            b = T[v[0]]
-            i, j = v[1] // 32, v[2] // 32
-            return b[:, i:j, :] if v[4] is None else b[:, i:j, 16 * v[4]:16 * v[4] + 16]
-        if v[3] == 1:
-            return T[v[0]][:, v[1]:v[2]]
-        return T[v[0]][:, v[1]:v[2]:v[3]]
+        b = T[v[0]]
+        if len(v) == 6:
+            return b[:, v[4]:v[5], v[1]:v[2]:v[3]]
+        sh = SCRATCH[v[0]][1]
+        if len(sh) == 2:
+            return b[:, v[1]:v[2]:v[3]]
+        w = sh[2]
+        o = v[1] // w
+        if v[2] <= o * w + w:
+            return b[:, o, v[1] - o * w:v[2] - o * w:v[3]]
+        return b[:, o:v[2] // w, :]
 
     def lanes(src, dst):
         return topo.engines(src, dst)[::2]
@@ -670,9 +657,8 @@ def rank_program(g, core, T, topo):
             dst = T.cores[(rank + kw["b"] + kw["t"]) % 4]
             rid, pid, _s = topo.addr(dst)
             e = lanes(core, dst)
-            src = kw["src"]
-            o = src[1] + NA
-            g.remote_dma(T.Z[:, o:o + N], ap(src), T.sem["za%d%d" % (kw["t"] + 1, kw["b"])], T.sem["lsent"], pid, rid, sum(1 << x for x in e))
+            o = kw["to"][1]
+            g.remote_dma(ap(Rf("Z4", o, o + NB)), ap(kw["in_"]), T.sem["za%d%d" % (kw["t"] + 1, kw["b"])], T.sem["lsent"], pid, rid, sum(1 << x for x in e))
             nloc += len(e)
             continue
         if t["inc"] == 16:
@@ -680,8 +666,10 @@ def rank_program(g, core, T, topo):
             if m == "dma":
                 s = kw["src"]
                 h = eng.dma_start(ap(kw["out"]), T[s[0]][:, s[1]:s[2]])
+            elif m == "copy":
+                h = eng.dma_start(ap(kw["out"]), ap(kw["in_"]))
             else:
-                h = eng.dma_start(T[kw["dst"]][:, 0:kw["src"][2]], ap(kw["src"]))
+                h = eng.dma_start(T[kw["dst"]][:, 0:kw["in_"][2]], ap(kw["in_"]))
             h.then_inc(T.sem[t["sem"]], 16)
             know = dict(ck)
             know[t["sem"]] = 16

@@ -3,35 +3,38 @@ from concourse.mybir import dt, AluOpType, ActivationFunctionType
 NT, NA, NR = 6, 256, 4096
 N = 128
 NB = 64
+ZW = 8 * N
 L = 16 * N
 
 SCRATCH = {}
 for _nm, _sh, _ty in (
-        ("X", [NR], "bfloat16"), ("PL", [NR], "int32"), ("Z4", [2 * NT, 512], "bfloat16"), ("Y", [NT * NA], "bfloat16"),
+        ("X", [NR], "bfloat16"), ("PL", [NR], "int32"), ("Z4", [2 * NT, ZW], "bfloat16"), ("Y", [NT * NA], "bfloat16"),
         ("DS", [2 * L], "bfloat16"), ("HS", [2 * L], "float16"), ("DE", [2 * L], "bfloat16"), ("AE", [2 * L], "bfloat16"),
-        ("TH", [NA], "int32"), ("S0", [NA], "int32"), ("P0", [16], "int32"), ("F0", [NA], "bfloat16"),
-        ("KT", [3 * NA], "float16"), ("TT", [3 * NA], "float16"), ("THA", [NA], "float16"),
-        ("EK", [NT * NA], "float16"), ("ET", [NT * NA], "float16"),
-        ("S16", [7 * NA], "float16"), ("SU", [7 * NA], "uint16"), ("E16", [7 * NA], "float16"), ("EU", [7 * NA], "uint16"),
+        ("TH", [NA], "int32"), ("S0", [NA], "int32"), ("P0", [16], "int32"), ("FB", [7 * NA], "bfloat16"), ("FM", [NA], "float32"),
+        ("UB", [NT * 16], "bfloat16"), ("UF", [NT * 16], "float32"),
+        ("KT", [3 * NA], "float16"), ("TT", [6, N], "float16"), ("THA", [NA], "float16"),
+        ("EK", [NT * NA], "float16"), ("ET", [2 * NT, N], "float16"),
+        ("S16", [14, N], "float16"), ("SU", [14, N], "uint16"), ("E16", [7 * NA], "float16"), ("EU", [7 * NA], "uint16"),
         ("F16", [7 * NA], "float16"), ("NI", [NA], "int32"), ("RR", [2 * NA], "bfloat16"), ("RP", [2 * NA], "bfloat16"), ("QQ", [2 * NA], "bfloat16"),
         ("WF", [2 * NA], "float32"), ("WH", [2 * NA], "float16"), ("W2", [NA], "float16"), ("MS", [NA], "bfloat16"),
         ("SE", [2 * NA], "float16"), ("MM", [NA], "float16"), ("SW", [2 * NT, N], "bfloat16"),
         ("YD", [NT * NA], "float32"), ("XN", [NT * NA], "int32"),
         ("PI1", [NT * 16], "int32"), ("PI2", [NT * 16], "int32"), ("PI3", [NT * 16], "int32"), ("PLC", [NT * 16], "uint16"),
-        ("U1", [NT * 16], "int32"), ("U2", [NT * 16], "int32"), ("U3", [NT * 16], "int32"), ("U4", [NT * 16], "int32"),
-        ("U5", [NT * 16], "int32"), ("U6", [NT * 16], "int32"), ("UH", [NT * 16], "int32"), ("UU", [NT * 16], "uint16"), ("PU", [16], "uint16"),
+        ("PH", [NT * 16], "float16"), ("BH", [16], "float16"), ("XT", [NA], "bfloat16"), ("XM", [NA], "float32"), ("XB", [NT * NA], "bfloat16"),
+        ("U1", [NT * 16], "int32"), ("U2", [NT * 16], "int32"), ("U3", [NT * 16], "int32"),
+        ("U5", [NT * 16], "int32"), ("UH", [NT * 16], "int32"), ("UU", [NT * 16], "uint16"), ("PU", [16], "uint16"),
         ("PT", [NT * 16], "int32"), ("PV", [NT * 16], "int32"), ("PW", [7 * 16], "int32"), ("YPO", [16], "float32"),
         ("YSO", [NA], "float32"), ("YFO", [NA], "bfloat16"), ("YXO", [NA], "float32"),
         ("IOC", [160], "float32"), ("PC", [1], "float32"), ("PI", [1], "int32"), ("IO8", [N], "int32"), ("BASE", [16], "int32"), ("TC", [NT * 16], "int32"),
         ("IOB", [16], "int32"), ("PG", [1], "int32"), ("PK", [1], "int32"), ("PO", [1], "int32"), ("C15F", [1], "float32"), ("PGF", [1], "float32"),
         ("WK", [1], "float32"), ("K16", [1], "float32"), ("ODC", [1], "float32"), ("EVC", [1], "float32"), ("A8", [N], "int32"),
         ("WI", [160], "bfloat16"), ("EVW", [160], "bfloat16"), ("ODW", [160], "bfloat16"), ("BIG", [144], "bfloat16"), ("BIGW", [144], "bfloat16"),
-        ("GS", [8], "bfloat16"), ("GN", [8], "bfloat16"), ("GH", [8], "bfloat16"), ("O8", [N], "bfloat16"), ("GT", [N], "bfloat16"), ("LT", [N], "bfloat16"),
-        ("T1", [N], "bfloat16"), ("T2", [N], "bfloat16"), ("ONE", [N], "bfloat16"), ("NIB", [N], "bfloat16"), ("HI", [N], "bfloat16"), ("I32", [N], "bfloat16"),
+        ("GS", [8], "bfloat16"), ("GN", [8], "bfloat16"), ("GH", [8], "bfloat16"), ("O8", [N], "bfloat16"), ("T3", [N], "bfloat16"), ("T4", [N], "bfloat16"),
+        ("T1", [N], "bfloat16"), ("T2", [N], "bfloat16"), ("ONE", [NA], "bfloat16"), ("NIB", [N], "bfloat16"), ("HI", [N], "bfloat16"), ("I32", [N], "bfloat16"),
         ("N64", [N], "bfloat16"), ("PQ", [N], "bfloat16"), ("NQ", [N], "bfloat16"), ("NK4", [N], "bfloat16"), ("K4", [N], "bfloat16"), ("Q256", [N], "bfloat16"),
         ("G1", [N], "bfloat16"), ("G1H", [N], "bfloat16"), ("N4", [N], "bfloat16"), ("N2", [N], "bfloat16"), ("SM", [N], "bfloat16"),
         ("NLI", [N], "bfloat16"), ("SHI", [N], "bfloat16"), ("CT", [N], "bfloat16"), ("KS32", [8], "float32"), ("NI32", [N], "float32"),
-        ("CI", [2048], "bfloat16")):
+        ("CI", [L], "bfloat16"), ("CJ", [L], "bfloat16")):
     SCRATCH[_nm] = ("sbuf", [128] + _sh, _ty)
 for _k in range(8):
     SCRATCH["ps%d" % _k] = ("psum", [128, 4, N], "float32")
@@ -45,9 +48,54 @@ AF = ActivationFunctionType
 BYTES2 = {k for k, v in SCRATCH.items() if v[2] in ("bfloat16", "float16", "uint16")}
 QS = {"V": "cv", "S": "cs", "P": "ct", "G": "cg"}
 
-EST = dict(g=1.55, sc=3.8, v=0.00083, pe=0.00042, vo=0.045, so=0.08, po=0.0, lat=0.15, self_=0.1, net=2.6, lx=7.0, lpl=16.0)
-OPT = dict(ep=("SSSS", "SSSS"), ep0=("SVSV", "SVSV"), w="SS", rho="SS", hh=(1, 1), ge=(512, 512), split=False, up=(2.0, 0.0))
-HASH = ("psU", "U1", "U2", "U3", "U4", "U5", "U6", "UH", "UU", "EK", "ET")
+EST = dict(g=1.55, sc=3.8, v=0.00083, pe=0.00042, vo=0.035, so=0.06, po=0.0, lat=0.13, self_=0.08, net=2.6, lx=7.0, lpl=16.0)
+OPT = dict(ep=("SSSS", "SSSS"), ep0=("SVSR", "SRSV"), w=("VS", "VV"), rho="SS", yd="VV", hh=(1, 1), ge=(512, 512), dd=(0, 0), pi=2, yb=2,
+           split=(False, True), cut=dict(psW=16, psD=16), xn="SS", cn=((2, 1), (1, 0)), sb=(7, 0))
+UP = {}
+TURN0 = dict(
+    V="ONE WI PG PO ODC EVC EVW ODW PQ A8 O8 N4 N2 T1 KS TT KH TT PK PGF C15 WK BIG BIGW SUs GH HI THA GN CT GS PU U1 SM U2 F160 U5 K16 U3 BASE UH S16s UU BH F16 KS32 NI32 "
+      "GS0 GS0 GS0 GS0 H0 GS1 GS1 NI0 GS1 RR0 QQ0 GS1 Wa0 H1 NI1 RR1 QQ1 KE TT EK ET Wa1 EUs GV0 E16s GV0 AV0 GV1 AV1 GV1 SE0 W20 SE1 MM0 LST0 MM1 YD0 SU0 W21 Wb1 S160 "
+      "E160 LST1 YD1 EU0 SU1 E161 S161 EU1 PI11 PLC1 SC1",
+    S="lt lp lf MS0 MS1 GE0 GE0 AE0 AE0 GE1 AE0 GE1 RP0 AE1 Wb0 AE1 AE1 SW0 Y0 RP1 XM0 XN0 SW1 Y1 XM1 XN1",
+    P="psA psA psU psF psW0 psW0 psH0 psK00 psQ0 psW1 psW1 psH1 psA psK01 psQ1 psJ psZ0 psZ0 psD0 psX0 psX1 psZ1 psD0 psK10 psK20 psZ1 psM0 psT0 psM1 psD1 psC0 psS0 psD1 "
+      "psK11 psK21 psE0 psN0 psT1 psC1 psS1 psE1 psY1 psN1 psL1",
+    G="pc ioc pi io8 iob zx0 zx0 zx1 zx1 SM G1 G1 SM Q256 Q256 NIB NIB G1H G1H NQ NQ NLI SHI NK4 NK4 I32 I32 N64 N64 K4 K4 tc CI CI send0 send1 send1")
+LAST = {}
+TURN = dict(
+    V="-SU1 GS0 -S161 GS0 GS0 U1 GS0 U2 H0 GS1 U5 GS1 U3 NI0 UH UU RR0 EK GS1 ET GS1 F16 W20 Wa0 H1 LST0 YD0 QQ0 PT NI1 RR1 QQ1 Wa1 PV SE0 Wb1 W21 E160 MM0 LST1 YD1 "
+      "PI10 EU0 SU0 PLC0 SE1 S160 SC0 E161 EU1 PI11 MM1 PLC1 SC1 YF PW PW PW PW PT PV PW PW YS0 YP",
+    S="GE0 GE0 AE0 GE0 AE0 GE0 AE0 GE1 AE0 GE1 AE1 RP0 GE1 Wb0 AE1 GE1 AE1 AE1 Y0 MS0 RP1 SW0 XM0 XN0 MS1 SW1 Y1 XM1 XN1 YX0 YX1",
+    P="psD0 psZ0 psU psZ0 psF psZ0 psW0 psW0 psZ0 psH0 psZ1 psW1 psD0 psD1 psZ1 psK00 psK10 psJ psK20 psZ1 psW1 psT0 psZ1 psH1 psQ0 psD1 psK01 psC0 psN0 psX0 psK11 psK21 "
+      "psE0 psM0 psQ1 psT1 psY0 psC1 psS0 psL0 psX1 psE1 psY1 psN1 psM1 psL1 psS1 psP psO0 psV0 psV1 -psO1",
+    G="zx0 zx0 zx1 zx1 send0 send0 send1 send1")
+
+
+OPT.update(bk=dict(w=(2, 3), z=(0, 1), k=((5, 0), (5, 2)), k2=((6, 0), (6, 1)), xn=((3, 2), (3, 3)), pu=3, o=(2, 3)), gs=((1, 1, 1, 1), (1, 1, 1, 1)), pi=4, xn="JI", cut=dict(psW=16, psD=16, psK1=1), ep0=("SRSR", "SRVR"))
+TURN0 = {'V': 'WI PG A8 PO EVC HI O8 PQ ONE KS N2 KH EVW PK ODC ODW TT WK PGF TT C15 N4 CT BIG K16 GS PU GN BIGW T1 F160 KS32 BASE SUs GH U1 BH THA U2 NI32 U5 SM U3 F16 UH UU S16s GS0 GS0 GS0 GS0 GS1 GS1 H0 GS1 NI0 GS1 RR0 QQ0 H1 Wa0 KE TT NI1 EK RR1 ET EUs Wa1 GV0 QQ1 GV0 AV0 E16s AV0 GV1 GV1 GV1 AV1 W20 AV1 SE0 LST0 YD0 MM0 W21 Wb1 SE1 LST1 YD1 E160 MM1 SU0 EU0 E161 S160 XN0 PI11 XN1 EU1 PLC1 SC1', 'S': 'lt lp lf GE0 GE0 GE1 AE0 AE0 MS0 AE1 RP0 AE1 Wb0 MS1 Y0 RP1 SW1 SW0 Y1 XM0', 'P': 'psA psA psU psF psW0 psW0 psW1 psH0 psW1 psK00 psH1 psA psK01 psJ psZ0 psQ0 psZ0 psD0 psZ1 psD0 psK10 psQ1 psK20 psK10 psX0 psD1 psT0 psD1 psX1 psM0 psK11 psK21 psK11 psC1 psC0 psT1 psE0 psM1 psE1 psS0 psN0 psY1 psN1 psL1 psS1', 'G': 'ioc pi pc io8 iob zx0 zx0 zx1 zx1 SM G1 G1 SM Q256 Q256 NIB NIB G1H G1H NQ NQ NLI SHI NK4 NK4 I32 I32 N64 N64 K4 K4 tc CI CI send0 send1 send1'}
+TURN = {'V': '-SU1 -S161 GS0 GS0 GS0 U1 GS0 U2 U5 H0 U3 GS1 UH GS1 UU NI0 EK RR0 ET GS1 GS1 Wa0 W20 H1 F16 QQ0 LST0 YD0 NI1 RR1 QQ1 Wa1 W21 Wb1 SE0 E160 LST1 YD1 MM0 E161 XN0 SE1 SU0 EU0 S160 PI11 XN1 MM1 PLC1 EU1 SC1', 'S': 'GE0 GE0 GE0 AE0 GE0 AE0 GE1 AE0 AE0 GE1 AE1 RP0 GE1 Wb0 AE1 GE1 AE1 AE1 Y0 SW0 MS0 RP1 SW1 MS1 XM0 Y1', 'P': 'psZ0 psD0 psU psZ0 psF psZ0 psW0 psW0 psZ0 psH0 psZ1 psD0 psD1 psW1 psZ1 psK00 psK10 psK10 psJ psK20 psZ1 psW1 psT0 psZ1 psH1 psQ0 psC0 psD1 psK01 psK11 psX0 psK21 psK11 psC1 psN0 psE0 psQ1 psT1 psE1 psM0 psX1 psS0 psY1 psN1 psM1 psL1 psS1', 'G': 'zx0 zx0 zx1 zx1 send0 send0 send1 send1'}
+LAST = {'V': '-SU1 GS0 GS0 GS0 -S161 U1 GS0 U2 U5 H0 GS1 U3 UH NI0 UU EK RR0 GS1 ET GS1 GS1 W20 Wa0 H1 LST0 F16 QQ0 YD0 NI1 RR1 QQ1 SE0 W21 Wb1 Wa1 PI10 XN0 LST1 YD1 PLC0 SE1 MM0 SC0 PI11 XN1 PLC1 SC1 PT SU0 S160 PV MM1 PW SU1 PW PT PW PV S161 PW YS0 YF PW PW YP YS1', 'S': 'GE0 GE0 GE0 AE0 GE0 AE0 GE1 AE0 AE0 GE1 AE1 RP0 GE1 Wb0 AE1 GE1 AE1 AE1 MS0 Y0 RP1 XM0 MS1 SW0 Y1 SW1 YX0 YX1', 'P': 'psD0 psZ0 psU psZ0 psF psZ0 psW0 psW0 psZ0 psH0 psZ1 psD0 psD1 psK00 psZ1 psK10 psK10 psJ psK20 psZ1 psW1 psW1 psT0 psZ1 psH1 psQ0 psD1 psK01 psX0 psK11 psN0 psK21 psK11 psC0 psY0 psQ1 psT1 psL0 psX1 psM0 psY1 psN1 psS0 psL1 psM1 psC1 psP psV1 psS1 psO0 psV0 psO1', 'G': 'zx0 zx0 zx1 zx1'}
+
+
+OPT.update(xn="SS", u="V", f="V", me=0, ms=0, sb=(((7, 0), (7, 1), (7, 3), (7, 0)), ((0, 0), (0, 1), (0, 3), (0, 0))))
+EST.update(pe=0.00036, vo=0.062, so=0.08, self_=0.1)
+TURN0 = {'V': 'WI PG PGF A8 O8 C15 PO PQ HI PK EVC ONE KS N4 PU ODC K16 WK TT BASE KH EVW ODW N2 BIG F160 BIGW GH GS TT U1 CT KS32 U2 T1 U5 F16 U3 SUs SM UH UU BH GN S16s THA GS1 GS0 GS0 GS0 GS1 GS0 H0 GS1 GS1 NI0 H1 QQ0 RR0 NI32 Wa0 NI1 KE TT QQ1 EK RR1 ET EUs E16s GV0 GV0 AV0 GV1 AV0 GV1 GV1 AV1 W20 AV1 LST0 Wa1 SE0 YD0 W21 MM0 Wb1 SE1 LST1 YD1 E160 MM1 E161 EU0 PI11 EU1 PI21 SU0 PI31 S160 PLC1 SC1', 'S': 'lf lt lp GE0 GE0 GE1 AE0 AE0 MS0 AE1 RP0 Wb0 AE1 RP1 Y0 MS1 SW0 XM0 SW1 Y1 XM1 XN0 XN1', 'P': 'psU psF psA psA psH0 psW0 psW1 psW0 psW1 psK00 psH1 psA psQ0 psJ0 psK01 psZ0 psZ0 psD0 psK10 psZ1 psD0 psX0 psQ1 psK10 psK20 psD1 psT0 psD1 psK11 psJ1 psK11 psK21 psM0 psX1 psC0 psT1 psC1 psN0 psS0 psE0 psM1 psE1 psY1 psN1 psS1', 'G': 'pc pi ioc io8 zx1 iob zx1 SM zx0 zx0 G1 SM Q256 G1 CI NLI Q256 G1H NQ NQ NIB G1H NIB NK4 NK4 I32 I32 N64 CI SHI N64 tc K4 send0 send1 send1 K4'}
+TURN = {'V': '-SU1 GS0 GS0 -S161 GS0 U1 GS0 U2 H0 U5 GS1 U3 GS1 UH NI0 UU EK RR0 ET GS1 GS1 QQ0 W20 H1 Wa0 F16 LST0 YD0 NI1 RR1 QQ1 Wa1 SE0 W21 Wb1 LST1 YD1 MM0 E160 SE1 E161 SU0 EU0 S160 PI11 PI21 EU1 PI31 MM1 PLC1 SC1', 'S': 'GE0 GE0 GE0 AE0 GE0 AE0 AE0 GE1 AE0 GE1 AE1 RP0 GE1 Wb0 GE1 AE1 AE1 AE1 Y0 MS0 RP1 SW0 MS1 SW1 XM0 XN0 Y1 XM1 XN1', 'P': 'psD0 psZ0 psU psZ0 psW0 psZ0 psW0 psF psZ0 psH0 psZ1 psW1 psD0 psD1 psZ1 psK00 psK10 psK10 psJ0 psK20 psZ1 psW1 psJ1 psZ1 psT0 psH1 psQ0 psD1 psK01 psX0 psC0 psK21 psK11 psK11 psQ1 psC1 psN0 psT1 psM0 psE0 psX1 psE1 psS0 psY1 psN1 psM1 psS1', 'G': 'zx0 zx0 zx1 zx1 send0 send0 send1 send1'}
+LAST = {'V': 'GS0 -SU1 GS0 GS0 GS0 H0 GS1 U1 U2 U5 -S161 U3 NI0 UH QQ0 UU EK RR0 ET GS1 GS1 W20 GS1 H1 Wa0 F16 LST0 YD0 NI1 RR1 QQ1 SE0 W21 Wb1 Wa1 PI10 PI20 LST1 PI30 YD1 PLC0 SE1 PT SC0 PI11 MM0 PI21 PI31 MM1 PLC1 SC1 PV PW SU0 YF S160 PT PW PV SU1 PW PW PW S161 PW YS0 YP YS1', 'S': 'GE0 GE0 GE0 AE0 GE0 AE0 GE1 AE0 AE0 GE1 AE1 RP0 GE1 GE1 AE1 MS0 Wb0 AE1 AE1 SW0 RP1 Y0 MS1 XM0 XN0 Y1 XM1 XN1 SW1 YX1 YX0', 'P': 'psD0 psZ0 psW0 psU psZ0 psZ0 psW0 psZ0 psF psH0 psZ1 psD0 psD1 psZ1 psK00 psJ0 psQ0 psK20 psW1 psK10 psZ1 psJ1 psK10 psZ1 psC0 psW1 psT0 psH1 psD1 psX0 psK01 psK11 psK21 psK11 psY0 psQ1 psN0 psT1 psM0 psX1 psC1 psY1 psN1 psM1 psS1 psP psS0 psV1 psO0 psV0 psO1', 'G': 'zx0 zx0 zx1 zx1'}
+
+
+OPT.update(w=("SS+", "SS"), pi=3, u="S", gs=((1, 1, 2), (2, 2)), me=1, cn=(None, (7, 2)), ms=1, sb=(None, ((1, 0), (0, 0), (1, 2), (7, 0))))
+TURN0 = {'V': 'ONE WI PG A8 O8 N4 PO PGF PK C15 HI KS EVC PU BIG EVW ODC PQ KH GH K16 WK TT ODW N2 BASE TT T1 KS32 GS BIGW CT F160 SUs GN BH THA F16 SM S16s GS0 GS0 GS1 GS0 GS1 H0 H1 NI32 U3 NI0 UH QQ0 UU RR0 NI1 KE TT EK QQ1 RR1 EUs ET GV0 GV1 GV0 AV0 AV0 E16s GV1 GV1 AV1 W20 AV1 LST0 YD0 W21 SE1 LST1 YD1 E161 EU1 PI11 MM1 PLC1 SC1', 'S': 'lp lf lt U1 U2 GE0 GE0 GE1 AE0 AE0 AE1 RP0 AE1 Wa0 MS1 Wa1 RP1 Y0 Wb1 SW1 XM0 Y1 XM1 XN1 XN0', 'P': 'psA psA psU psG psG psF psW0 psW0 psW1 psW1 psH0 psH1 psA psZ0 psJ0 psZ0 psD0 psZ1 psK00 psD0 psQ1 psK01 psK10 psK10 psK20 psD1 psT0 psD1 psJ1 psK11 psK11 psK21 psX1 psT1 psC1 psN0 psM1 psE1 psN1 psY1 psL1 psL1 psS1', 'G': 'pc ioc pi io8 iob NIB NIB zx0 zx0 SM zx1 zx1 zx0 zx1 G1 G1 SM Q256 Q256 G1H G1H NQ NQ NLI SHI NK4 NK4 I32 I32 N64 N64 K4 K4 tc CI CI send0 send1 send1'}
+TURN = {'V': '-SU1 GS0 GS0 GS0 H0 GS1 U3 NI0 UH RR0 -S161 UU EK ET GS1 W20 F16 H1 QQ0 LST0 YD0 NI1 RR1 QQ1 W21 LST1 YD1 SE1 E161 EU1 PI11 MM1 PLC1 SC1', 'S': 'GE0 GE0 GE0 GE0 AE0 AE0 U1 GE1 AE0 U2 AE0 GE1 AE1 GE1 RP0 GE1 AE1 Wa0 AE1 AE1 Y0 RP1 Wa1 Wb1 MS1 XM0 SW1 Y1 XM1 XN0 XN1', 'P': 'psZ0 psD0 psU psW0 psZ0 psG psZ0 psW0 psZ0 psF psG psH0 psZ1 psD0 psK00 psK10 psZ1 psD1 psJ0 psZ1 psK10 psK20 psW1 psW1 psJ1 psZ1 psT0 psH1 psD1 psK01 psK11 psK11 psK21 psC1 psQ1 psN0 psT1 psX1 psE1 psY1 psN1 psM1 psL1 psL1 psS1', 'G': 'zx0 zx0 zx0 zx1 zx1 zx1 send0 send0 send1 send1'}
+LAST = {'V': '-SU1 GS0 GS0 GS0 H0 GS1 U3 PT UH -S161 UU NI0 EK RR0 ET GS1 H1 W20 QQ0 F16 NI1 QQ1 RR1 LST0 YD0 W21 LST1 YD1 PI10 SE1 PLC0 PT SC0 PI11 PV MM1 PV PLC1 PW SC1 PW PW SU1 S161 PW YF PW PW YS1 YP', 'S': 'GE0 GE0 GE0 AE0 U1 AE0 GE0 GE1 AE0 U2 AE0 GE1 RP0 GE1 AE1 GE1 AE1 Wa0 AE1 AE1 RP1 Y0 Wb1 Wa1 MS1 XM0 Y1 XN0 SW1 XM1 XN1 YX1 YX0', 'P': 'psZ0 psZ0 psU psD0 psW0 psW0 psG psG psZ0 psZ0 psF psH0 psZ1 psD0 psZ1 psK00 psK10 psJ0 psK20 psD1 psZ1 psW1 psK10 psW1 psZ1 psH1 psJ1 psT0 psD1 psQ1 psK01 psK11 psK11 psK21 psY0 psN0 psT1 psC1 psX1 psL0 psL0 psY1 psN1 psM1 psL1 psL1 psV0 psS1 psV1 psO1 psP', 'G': 'zx0 zx0 zx0 zx1 zx1 zx1'}
+
+
+OPT.update(ep0=("SSSR", "SSSR"), mc=0, gs=((4, 4, 8), (8, 8)))
+EST.update(lx=4.5, lpl=9.5)
+TURN0 = {'V': 'ONE PG C15 PK BIG PO WK WI ODC A8 BIGW PQ ODW CT EVC O8 KS KH EVW N4 TT PU U3 PGF TT N2 GH SUs HI S16s THA T1 GN GS0 GS0 GS0 GS1 H0 KE TT UH GS NI0 EUs GS1 RR0 GV0 F160 UU H1 EK ET AV0 NI1 SM KS32 GV1 RR1 E16s NI32 K16 AV1 QQ0 W20 F16 QQ1 LST0 YD0 W21 SE1 LST1 YD1 BASE BH MM1 E161 PI11 EU1 PLC1 SC1', 'S': 'lt lp U1 U2 lf GE1 GE0 GE0 GE0 AE0 AE0 GE1 AE0 GE1 RP0 AE1 AE1 Wa0 AE1 RP1 MS1 Y0 Wa1 Wb1 SW1 XM0 Y1 XM1 XN0 XN1', 'P': 'psU psG psG psA psA psH0 psA psW0 psW0 psW1 psW1 psZ0 psD0 psZ0 psH1 psZ0 psJ0 psZ1 psK00 psF psD0 psZ1 psD1 psK10 psK10 psK01 psK20 psZ1 psJ1 psT0 psK11 psD1 psQ1 psK11 psK21 psX1 psC1 psN0 psT1 psE1 psM1 psN1 psY1 psL1 psL1 psS1', 'G': 'pi ioc pc NIB io8 NIB iob zx1 Q256 zx0 G1 zx0 zx1 G1 zx0 zx1 Q256 NQ NQ SHI NK4 G1H NK4 SM NLI G1H I32 I32 N64 N64 CI K4 SM CI tc send0 K4 send1 send1'}
+
+
+OPT.update(ep0=("SSSR", "SSRR"))
+TURN0 = {'V': 'PG ONE PO ODC EVC WI PK C15 BIG WK PGF KS A8 TT G8 KH TT O8 SUs PU F160 S16s THA GS0 GS0 U3 GS0 GS1 UH H0 KE TT GS1 EUs UU H1 EK NI0 K16 ET GV0 SM AV0 E16s RR0 NI1 F16 RR1 GV1 QQ0 GV1 QQ1 AV1 W20 BH AV1 LST0 YD0 W21 SE1 LST1 YD1 MM1 E161 PI11 EU1 PLC1 SC1', 'S': 'lp lt lf EVW NIB CT PQ ODW BIGW N2 U1 GH U2 NK4 T1 N4 HI GN K4 N64 NQ I32 NI32 Q256 KS32 GE0 GE0 GE0 AE0 AE0 GE1 AE0 GE1 RP0 AE1 Wa0 AE1 MS1 RP1 Y0 Wb1 Wa1 SW1 Y1 XM1 XM0 XN1 XN0', 'P': 'psA psA psU psG psG psH0 psA psW0 psW0 psF psW1 psW1 psZ0 psH1 psZ0 psZ0 psJ0 psK00 psD0 psZ1 psD0 psK01 psK10 psZ1 psK10 psK20 psD1 psQ1 psT0 psK11 psD1 psJ1 psK11 psK21 psX1 psC1 psT1 psN0 psE1 psM1 psN1 psY1 psL1 psL1 psS1', 'G': 'pi pc iob ioc io8 zx0 zx0 zx0 zx1 zx1 G1 zx1 tc G1 G1H G1H SM NLI SHI SM CI CI send0 send1 send1'}
 
 
 def Rf(buf, lo, hi, st=1):
@@ -135,7 +183,7 @@ def add(P, q, name, ins, wr=None, dur=None, sem=None, inc=1, extra=None, prio=0.
     r, w = touches(ins)
     w += wr or []
     T = {"i": len(P["tasks"]), "q": q, "name": name, "ins": ins, "sem": sem, "inc": inc, "prio": prio,
-         "fix": dur, "pre": {}, "banks": [], "up": P.get("up", 0.0)}
+         "fix": dur, "pre": {}, "banks": [], "label": name + P.get("c", ""), "t": P.get("t", 0)}
     hist = P["last"]
     seen = {}
     for a, lst in (("r", r), ("w", w)):
@@ -162,7 +210,8 @@ def add(P, q, name, ins, wr=None, dur=None, sem=None, inc=1, extra=None, prio=0.
 
 def acc(items, start=True, stop=True):
     k = len(items)
-    return [("matmul", dict(out=o, lhsT=l, rhs=r, start=start and i == 0, stop=stop and i == k - 1)) for i, (o, l, r) in enumerate(items)]
+    return [("matmul", dict(out=x[0], lhsT=x[1], rhs=x[2], start=start and i == 0, stop=stop and i == k - 1, part=(x + ([0, 128],))[3]))
+            for i, x in enumerate(items)]
 
 
 def ts(out, in0, s1, op0, s2=None, op1=None):
@@ -213,13 +262,22 @@ def build(opt=None):
     S = lambda nm, ins, **k: add(P, "S", nm, ins, **k)
     G = lambda nm, ins, **k: add(P, "G", nm, ins, **k)
 
-    def PE(nm, ins, opens=None, closes=None, **k):
+    def PE(nm, ins, opens=None, closes=None, inside=None, **k):
         i = add(P, "P", nm, ins, **k)
+        if inside:
+            opens = closes = inside
         if opens:
             P["tasks"][i]["opens"] = opens
         if closes:
             P["tasks"][i]["closes"] = closes
         return i
+
+    def PE2(nm, items, after):
+        k = opt["cut"].get(nm)
+        if not k:
+            return PE(nm, acc(items))
+        PE(nm, acc(items[:-k], stop=False), opens=items[0][0][0], extra=after)
+        return PE(nm, acc(items[-k:], start=False), closes=items[0][0][0])
 
     def load(q, sem, ref, dur, src):
         return add(P, q, sem, [("dma", dict(out=ref, src=src))], dur=0.1, sem=sem, inc=16, prio=dur)
@@ -228,7 +286,7 @@ def build(opt=None):
     load("Y", "lx", Rf("X", 0, NR), EST["lx"], ("x0", 0, NR))
     load("S", "lt", Rf("TH", 0, NA), 2.5, ("th", 0, NA))
     load("S", "lp", Rf("P0", 0, 16), 2.5, ("p0", 0, 16))
-    load("S", "lf", Rf("F0", 0, NA), 2.5, ("f0", 0, NA))
+    load("S", "lf", Rf("FB", 0, NA), 2.5, ("f0", 0, NA))
     load("Y", "lpl", Rf("PL", 0, NR), EST["lpl"], ("pl", 0, NR))
     io = lambda nm, ref, pat, ch, base=0: G(nm, [("iota", dict(out=ref, pattern=pat, base=base, channel_multiplier=ch))])
     io("pc", c1("PC"), [[1, 1]], 1)
@@ -245,111 +303,132 @@ def build(opt=None):
     V("PO", ts(c1("PO"), c1("PG"), 1, A.bitwise_and))
     V("ODC", ts(c1("ODC"), c1("PO"), 1.0, A.mult))
     V("EVC", ts(c1("EVC"), c1("PO"), 0.0, A.is_equal))
-    V("EVW", ts(Rf("EVW", 0, 160), Rf("WI", 0, 160), c1("EVC"), A.mult))
-    V("ODW", ts(Rf("ODW", 0, 160), Rf("WI", 0, 160), c1("ODC"), A.mult))
+    times = lambda nm, out, in_, k, b=0.0: S(nm, act(out, in_, AF.Identity, bias=b, scale=k))
+    times("EVW", Rf("EVW", 0, 160), Rf("WI", 0, 160), c1("EVC"))
+    times("ODW", Rf("ODW", 0, 160), Rf("WI", 0, 160), c1("ODC"))
     V("PGF", ts(c1("PGF"), c1("PG"), 1.0, A.mult))
     V("C15", ts(c1("C15F"), c1("PG"), 16.0, A.mult, 15.0, A.add))
     V("WK", ts(c1("WK"), c1("PK"), 2.0, A.mult, 1.0, A.add))
     V("K16", ts(c1("K16"), c1("PK"), 16.0, A.mult))
-    V("BASE", ts(Rf("BASE", 0, 16), Rf("IOB", 0, 16), c1("K16"), A.add))
+    if opt["pi"] == 4:
+        V("BASE", ts(Rf("BASE", 0, 16), Rf("IOB", 0, 16), c1("K16"), A.add))
     V("BIG", ts(Rf("BIG", 0, 144), Rf("IOC", 0, 144), c1("C15F"), A.is_equal))
-    V("BIGW", ts(Rf("BIGW", 0, 144), Rf("BIG", 0, 144), c1("WK"), A.mult))
-    V("GS", ts(Rf("GS", 0, 8), Rf("IOC", 0, 8), c1("PGF"), A.is_equal))
-    V("GN", ts(Rf("GN", 0, 8), Rf("IOC", 0, 8), c1("PGF"), A.is_equal, -1.0, A.mult))
-    V("GH", ts(Rf("GH", 0, 8), Rf("IOC", 0, 8), c1("PGF"), A.is_equal, -0.5, A.mult))
-    V("ONE", [("memset", dict(ap=ONE, constant=1.0))])
+    times("BIGW", Rf("BIGW", 0, 144), Rf("BIG", 0, 144), c1("WK"))
+    V("G8", ts(Rf("GS", 0, 8), Rf("IOC", 0, 8), c1("PGF"), A.is_equal))
+    times("GN", Rf("GN", 0, 8), Rf("GS", 0, 8), -1.0)
+    times("GH", Rf("GH", 0, 8), Rf("GS", 0, 8), -0.5)
+    V("ONE", [("memset", dict(ap=Rf("ONE", 0, NA), constant=1.0))])
     V("A8", ts(M("A8"), M("IO8"), 7, A.bitwise_and))
     V("O8", ts(M("O8"), M("A8"), 0.0, A.is_equal))
-    V("GT", ts(M("GT"), M("IOC"), c1("PC"), A.is_gt))
-    V("LT", tt(M("LT"), M("O8"), M("GT"), A.mult))
-    for nm, k in (("NIB", -1.0), ("HI", 0.5), ("I32", 32.0), ("N64", -64.0), ("PQ", 2048.0), ("NQ", -2048.0), ("NK4", -4096.0), ("K4", 4096.0),
-                  ("Q256", 256.0)):
-        V(nm, ts(M(nm), I, k, A.mult))
-    V("CT", ts(M("CT"), I, -0.6875, A.mult, 8.0, A.add))
-    V("N4", ts(M("N4"), M("O8"), -4096.0, A.mult))
-    V("N2", ts(M("N2"), M("O8"), -2048.0, A.mult))
-    V("T1", tt(M("T1"), I, M("LT"), A.subtract))
-    V("G1", ts(M("G1"), M("T1"), 4096.0, A.mult))
-    V("G1H", ts(M("G1H"), M("T1"), 2048.0, A.mult))
-    V("T2", tt(M("T2"), I, M("LT"), A.add))
-    V("NLI", ts(M("NLI"), M("T2"), -4096.0, A.mult))
-    V("T1b", ts(M("T1"), M("T1"), -16.0, A.mult))
-    V("T2b", tt(M("T2"), M("O8"), I, A.subtract))
-    V("SM", tt(M("SM"), M("T1"), M("T2"), A.add))
-    V("SHI", tt(M("SHI"), Rf("WI", 8, 8 + N), I, A.subtract))
-    if "S" in opt["w"]:
-        V("KS32", cp(Rf("KS32", 0, 8), Rf("O8", 0, 8)))
-        V("NI32", ts(M("NI32"), I, -1.0, A.mult))
+    for nm, k in (("PQ", 2048.0), ("NIB", -1.0), ("HI", 0.5), ("Q256", 256.0), ("NQ", -2048.0), ("NK4", -4096.0), ("I32", 32.0), ("N64", -64.0), ("K4", 4096.0)):
+        times(nm, M(nm), I, k)
+    times("CT", M("CT"), I, -0.6875, 8.0)
+    for nm, k in (("N4", -4096.0), ("N2", -2048.0), ("T1", 17.0)):
+        times(nm, M(nm), M("O8"), k)
+    V("BH", ts(Rf("BH", 0, 16), Rf("IOB", 0, 16), c1("K16"), A.add, 16400.0, A.add))
+    cut = lambda nm, out, in_, op, fill, k=1: G(nm, [("affine", dict(out=out, in_=in_, op=op, fill=fill, pattern=[[0, k], [1, N]]))])
+    cut("G1", M("T2"), M("N4"), A.is_gt, 0.0)
+    cut("G1", M("G1"), M("T2"), A.not_equal, 4096.0)
+    cut("SM", M("T4"), M("T1"), A.is_gt, 0.0)
+    V("SM", tt(M("T1"), M("T4"), M("O8"), A.max))
+    cut("SM", M("SM"), M("T1"), A.not_equal, -16.0)
+    cut("G1H", M("T2"), M("N2"), A.is_gt, 0.0)
+    cut("G1H", M("G1H"), M("T2"), A.not_equal, 2048.0)
+    cut("NLI", M("NLI"), M("N4"), A.is_ge, 0.0)
+    cut("SHI", M("SHI"), Rf("WI", 8, 8 + N), A.not_equal, -1.0)
+    io("CI", Rf("CJ", 0, L), [[1, 16], [0, N]], 0, 1)
+    cut("CI", Rf("CI", 0, L), Rf("CJ", 0, L), A.is_equal, 0.0, 16)
+    if "S" in "".join(opt["w"]):
+        times("KS32", Rf("KS32", 0, 8), Rf("O8", 0, 8), 1.0)
+        times("NI32", M("NI32"), I, -1.0)
 
     def turned(j, bank):
         V("TT", tr(Rf("TT", j * NA, j * NA + NA), Rf("KT", j * NA, j * NA + NA)))
-        ins = []
-        for c in range(2):
-            it = [(reg(bank, c), M("PQ"), ONE)]
-            for h in range(4):
-                for b in range(2):
-                    for gl in range(2):
-                        a = (2 * j + c) * N + 32 * h + 16 * gl
-                        it.append((Rf("ps%d" % bank, c * N + 2 * h + b, c * N + N, 8), half(b, gl), Rf("TT", a, a + 16)))
-            ins += acc(it)
-        PE("psA", ins)
+        it = [(reg(bank, 0, 2), M("PQ"), Rf("ONE", 0, NA))]
+        for h in range(4):
+            for b in range(2):
+                for gl in range(2):
+                    x0 = 32 * h + 16 * gl
+                    it.append((R2("ps%d" % bank, 0, 2, 2 * h + b, N, 8), half(b, gl), R2("TT", 2 * j, 2 * j + 2, x0, x0 + 16)))
+        PE("psA", acc(it))
         return reg(bank, 0, 2)
     V("KS", ts(Rf("KT", 0, NA), Rf("S0", 0, NA), -2048.0, A.add))
-    V("SU0", cp(Rf("SU", 0, NA), turned(0, 7)))
-    V("S160", ts(Rf("S16", 0, NA), Rf("SU", 0, NA), -2048.0, A.add))
+    V("SUs", cp(Rf("SU", 0, NA), turned(0, 7)))
+    V("S16s", ts(Rf("S16", 0, NA), Rf("SU", 0, NA), -2048.0, A.add))
     V("KH", ts(Rf("KT", NA, 2 * NA), Rf("TH", 0, NA), -2048.0, A.add))
     V("THA", ts(Rf("THA", 0, NA), turned(1, 5), -2048.0, A.add))
-    V("F160", ts(Rf("F16", 0, NA), Rf("F0", 0, NA), 1024.0, A.add))
+    fb, fo = ("F16", 1024.0) if opt["f"] == "V" else ("FB", 0.0)
+    if fo:
+        V("F160", ts(Rf("F16", 0, NA), Rf("FB", 0, NA), 1024.0, A.add))
     V("PU", cp(Rf("PU", 0, 16), Rf("P0", 0, 16)))
     V("KE", ts(Rf("KT", 2 * NA, 3 * NA), ind(Rf("PL", 0, NR), Rf("PU", 0, 16)), -2048.0, A.add))
-    V("EU0", cp(Rf("EU", 0, NA), turned(2, 6)))
-    V("E160", ts(Rf("E16", 0, NA), Rf("EU", 0, NA), -2048.0, A.add))
+    V("EUs", cp(Rf("EU", 0, NA), turned(2, 1)))
+    V("E16s", ts(Rf("E16", 0, NA), Rf("EU", 0, NA), -2048.0, A.add))
     Xa = Rf("X", 0, NR)
     KS = Rf("O8", 0, 8)
     shut = None
+    bk_ = opt["bk"]
     for t in range(NT):
         last = t == NT - 1
         o = t * NA
         U = lambda nm: Rf(nm, t * 16, t * 16 + 16)
         zb = R2("Z4", 2 * t, 2 * t + 2, 0, N)
+        split = opt["split"][last]
+        P["t"] = t
         for c in range(2):
-            z0 = (2 * t + c) * 512
-            G("zx", [("affine", dict(out=Rf("Z4", z0 + N, z0 + 2 * N), in_=Rf("Z4", z0, z0 + N)))])
-            G("zx", [("affine", dict(out=Rf("Z4", z0 + 2 * N, z0 + 4 * N), in_=Rf("Z4", z0, z0 + 2 * N)))])
-        PE("psF", acc([(reg(2, 2, 2), I, Rf("F16", o, o + NA)), (reg(2, 2, 2), I, zb)]))
-        V("F16", ts(Rf("F16", o + NA, o + 2 * NA), reg(2, 2, 2), 0.5, A.mult, 511.75, A.add))
-        pu = Rf("ps6", 2 * N + 16, 2 * N + 32)
-        PE("psU", acc([(pu, sel(m, "BIGW"), R2("Z4", 2 * t, 2 * t + 2, m, N, 16)) for m in range(16)]))
-        V("U1", cp(U("U1"), pu))
-        V("U2", ts(U("U2"), U("U1"), 4095, A.bitwise_and))
-        V("U3", tt(U("U3"), U("U2"), U("U2"), A.mult))
-        V("U5", ts(U("U5"), U("U2"), 37.0, A.mult))
-        V("U4", ts(U("U4"), U("U3"), 5, A.arith_shift_right))
-        V("U6", tt(U("U6"), U("U4"), U("U5"), A.add))
-        V("UH", ts(U("UH"), U("U6"), 4095, A.bitwise_and))
+            P["c"] = str(c)
+            z0 = (2 * t + c) * ZW
+            for n in (1, 2, 4)[:2 + (max(opt["gs"][c]) > 4)]:
+                G("zx", [("affine", dict(out=Rf("Z4", z0 + n * N, z0 + 2 * n * N), in_=Rf("Z4", z0, z0 + n * N)))])
+        P["c"] = ""
+        PE("psF", acc([(reg(2, 2, 2), I, Rf(fb, o, o + NA)), (reg(2, 2, 2), I, zb)]))
+        if opt["f"] == "V":
+            V("F16", ts(Rf("F16", o + NA, o + 2 * NA), reg(2, 2, 2), 0.5, A.mult, 511.75, A.add))
+        else:
+            S("FM", act(Rf("FM", 0, NA), reg(2, 2, 2), AF.Identity, bias=12582912.0, scale=0.4995))
+            S("F16", act(Rf("FB", o + NA, o + 2 * NA), Rf("FM", 0, NA), AF.Identity, bias=-12582912.0))
+        pu = Rf("ps%d" % bk_["pu"], 2 * N, 2 * N + 16)
+        it = [(pu, sel(m, "BIGW"), R2("Z4", 2 * t, 2 * t + 2, m, N, 16)) for m in range(16)]
+        i = PE("psU", acc(it))
+        if opt["u"] == "V":
+            V("U1", cp(U("U1"), pu))
+            V("U2", ts(U("U2"), U("U1"), 4095, A.bitwise_and))
+            V("U5", ts(U("U5"), U("U2"), 1184.0, A.add))
+            V("U3", tt(U("U3"), U("U2"), U("U5"), A.mult))
+        else:
+            pz = Rf("ps7", 3 * N, 3 * N + 16)
+            S("U1", act(U("UB"), pu, AF.Identity, bias=786432.0 - 2047.5))
+            PE("psG", acc([(pz,) + x[1:] for x in it], stop=False), opens="ps7", extra=[i])
+            PE("psG", acc([(pz, M("NIB"), U("UB"))], start=False), closes="ps7")
+            S("U2", act(U("UF"), pz, AF.Square, bias=786432.0 + 592))
+            V("U3", ts(U("U3"), U("UF"), -350464.0, A.add))
+        V("UH", ts(U("UH"), U("U3"), 5, A.arith_shift_right, 4095, A.bitwise_and))
         V("UU", cp(U("UU"), U("UH")))
         V("EK", ts(Rf("EK", o, o + NA), ind(Rf("PL", 0, NR), U("UU")), -2048.0, A.add))
         V("ET", tr(Rf("ET", o, o + NA), Rf("EK", o, o + NA)))
         ep = opt["ep0"] if t == 0 else opt["ep"]
-        zturn = 0
+        zturn, kept = 0, []
         for c in range(2):
-            P["up"] = opt["up"][c]
+            P["c"] = str(c)
             a, d0 = o + c * N, c * L
-            z4 = Rf("Z4", (2 * t + c) * 512, (2 * t + c + 1) * 512)
-            z = Rf("Z4", (2 * t + c) * 512, (2 * t + c) * 512 + N)
+            z4 = Rf("Z4", (2 * t + c) * ZW, (2 * t + c) * ZW + 512)
+            z = Rf("Z4", (2 * t + c) * ZW, (2 * t + c) * ZW + N)
             lane = lambda nm, ii: Rf(nm, d0 + ii, d0 + L, 16)
             pc = lambda nm, k=1: Rf(nm, k * c * N, k * c * N + k * N)
             th = pc("THA")
             hist = lambda out, m: [(out, Rf("SW", (2 * u + c) * N, (2 * u + c + 1) * N), M(m)) for u in range(t)]
             sums = lambda bank, j, nm, g8: [(Rf("ps%d" % bank, N * j + ii, N * j + N, 16), lane(nm, ii), Rf(g8, 0, 8)) for ii in range(16)]
-            for j in range(4):
-                V("GS", tt(Rf("DS", d0 + 512 * j, d0 + 512 * j + 512), ind(Xa, Rf("SU", a + 32 * j, a + 32 * j + 32)), z4, A.subtract))
+            first = [len(P["tasks"]) + 1]
+            j = 0
+            for n in opt["gs"][c]:
+                V("GS", tt(Rf("DS", d0 + N * j, d0 + N * (j + n)), ind(Xa, Rf("SU", a + 8 * j, a + 8 * (j + n))), Rf("Z4", z[1], z[1] + N * n), A.subtract))
+                j += n
             hh = opt["hh"][c]
             for j in range(hh):
                 x0, x1 = d0 + L // hh * j, d0 + L // hh * (j + 1)
                 V("H", ts(Rf("HS", x0, x1), Rf("DS", x0, x1), 127.9375, A.add, 128.0, A.min))
-            bw = 2 + c
-            PE("psW", acc([(reg(bw, 0), th, M("HI"))] + hist(reg(bw, 0), "I32") + sums(bw, 0, "DS", "GH")))
+            bw = bk_["w"][c]
+            PE2("psW", [(reg(bw, 0), th, M("HI"))] + hist(reg(bw, 0), "I32") + sums(bw, 0, "DS", "GH"), first)
             PE("psH", acc([(reg(bw, 1), M("CT"), ONE)] + sums(bw, 1, "HS", "GN")))
             ni = pc("NI")
             par = (t % 2) * NA + c * N
@@ -358,23 +437,38 @@ def build(opt=None):
             V("RR", tt(r, ni, reg(bw, 0), A.is_lt))
             V("QQ", tt(q, ni, reg(bw, 1), A.is_lt))
             ge = opt["ge"][c]
+            first = [len(P["tasks"])]
             for j in range(4):
                 x0, x1 = d0 + 512 * j, d0 + 512 * j + 512
                 eu = Rf("EU", a + 32 * j, a + 32 * j + 32)
-                if ep[c][j] == "S":
-                    if ge == 512:
+                if ep[c][j] in "SC":
+                    if ep[c][j] == "C":
+                        V("GV", cp(Rf("DE", x0, x1), ind(Xa, eu)))
+                    elif ge == 512:
                         S("GE", act(Rf("DE", x0, x1), ind(Xa, eu), AF.Copy))
                     elif j % 2 == 0:
                         S("GE", act(Rf("DE", x0, x1 + 512), ind(Xa, Rf("EU", a + 32 * j, a + 32 * j + 64)), AF.Copy))
-                    zk = reg(zturn % 2, 0, 4)
+                    zk = reg(bk_["z"][zturn % len(bk_["z"])], 0, 4)
                     zturn += 1
                     PE("psZ", acc([(zk, M("NIB"), z4), (zk, I, Rf("DE", x0, x1))]))
                     S("AE", act(Rf("AE", x0, x1), zk, AF.Abs))
                 else:
-                    V("GE", tt(Rf("DE", x0, x1), ind(Xa, eu), z4, A.subtract))
-                    S("AE", act(Rf("AE", x0, x1), Rf("DE", x0, x1), AF.Abs))
+                    V("GV", tt(Rf("DE", x0, x1), ind(Xa, eu), z4, A.subtract))
+                    if ep[c][j] == "V":
+                        S("AE", act(Rf("AE", x0, x1), Rf("DE", x0, x1), AF.Abs))
+                    else:
+                        V("AV", ts(Rf("AE", x0, x1), Rf("DE", x0, x1), 0.0, A.max, 2.0, A.mult))
             de = reg(4, c)
-            PE("psD", acc([(de, th, M("NIB"))] + hist(de, "N64") + sums(4, c, "AE", "GS")))
+            part = lambda nm, g8, p0, p1: [(Rf("ps4", N * c + ii, N * c + N, 16), Rf(nm, d0 + ii + 16 * p0, d0 + 16 * p1, 16), Rf(g8, 0, 8), [p0, p1]) for ii in range(16)]
+            it = [(de, th, M("NIB"))] + hist(de, "N64")
+            for j in range(4):
+                if ep[c][j] == "R":
+                    it += part("DE", "GN", 32 * j, 32 * j + 32)
+            if opt["dd"][c]:
+                PE("psDa", acc(it + part("AE", "GS", 0, 96), stop=False), opens="ps4")
+                PE("psD", acc(part("AE", "GS", 96, 128), start=False), closes="ps4")
+            else:
+                PE2("psD", it + sums(4, c, "AE", "GS"), first)
             if opt["rho"][c] == "S":
                 S("RP", act(rho, de, AF.Sign, bias=2047.5, scale=-1.0))
                 g1r, n4r = M("G1H"), M("N2")
@@ -382,94 +476,154 @@ def build(opt=None):
                 V("RP", ts(rho, de, 2047.5, A.is_lt, -0.5, A.add))
                 g1r, n4r = M("G1"), M("N4")
             s16, e16 = Rf("S16", a, a + N), Rf("E16", a, a + N)
-            k0, k1, k2 = reg(5, 2 * c), reg(5, 2 * c + 1), reg(6, c)
-            PE("psK0", acc([(k0, s16, I), (k0, M("G1"), r)]))
-            PE("psK1", acc([(k1, e16, I), (k1, M("G1H"), ONE), (k1, M("N4"), r), (k1, g1r, rho)]))
-            it = [(k2, ONE, M("N2"))]
-            for h in range(4):
-                for b in range(2):
-                    for gl in range(2):
-                        x0 = a + 32 * h + 16 * gl
-                        it.append((Rf("ps6", c * N + 2 * h + b, c * N + N, 8), half(b, gl), Rf("ET", x0, x0 + 16)))
-            PE("psK2", acc(it, stop=False), opens="ps6", extra=[shut] if shut is not None else None)
-            PE("psK2", acc([(k2, r, M("N4")), (k2, rho, n4r)], start=False), closes="ps6")
-            w2 = pc("W2")
-            V("W2", ts(w2, k2, -2048.0, A.max))
-            pt = Rf("ps6", 2 * N + 8 * c, 2 * N + 8 * c + 8)
-            w20 = Rf("W2", c * N, c * N + 8)
-            if opt["w"][c] == "S":
-                S("W", act(pc("WF", 2), reg(5, 2 * c, 2), AF.Relu, bias=-2048.0))
-                w0, w1 = Rf("WF", 2 * c * N, 2 * c * N + N), Rf("WF", 2 * c * N + N, 2 * c * N + 2 * N)
-                shut = PE("psT", acc([(pt, I, w20), (pt, w0, Rf("KS32", 0, 8)), (pt, w1, Rf("KS32", 0, 8))]))
-                top, rest, nw = 2048.0, 4096.0, "NI32"
+            kb, kj = bk_["k"][c]
+            k0, k1, k2 = reg(kb, kj), reg(kb, kj + 1), reg(*bk_["k2"][c])
+            i = PE("psK0", acc([(k0, s16, I), (k0, M("G1"), r)]))
+            PE2("psK1", [(k1, e16, I), (k1, M("G1H"), ONE), (k1, M("N4"), r), (k1, g1r, rho)], [i])
+            wq = opt["w"][c]
+            ws = [Rf("WF" if wq[j] == "S" else "WH", (2 * c + j) * N, (2 * c + j + 1) * N) for j in range(2)]
+            for j, n in ((0, 2),) if len(wq) == 3 else ((0, 1), (1, 1)):
+                x0 = (2 * c + j) * N
+                if wq[j] == "S":
+                    S("W" + "ab"[j], act(Rf("WF", x0, x0 + n * N), reg(kb, kj + j, n), AF.Relu, bias=-2048.0))
+                else:
+                    V("W" + "ab"[j], ts(Rf("WH", x0, x0 + n * N), reg(kb, kj + j, n), -4096.0, A.add, -2048.0, A.max))
+            top = 2048.0 * (1 + 16 * wq[:2].count("V"))
+            rest, nw = (4096.0, "NI32") if wq[0] == "S" else (2048.0, "NIB")
+            kept.append((r, rho, q, n4r, s16, e16, ws[0], nw, rest))
+            tops = [(ws[j], Rf("KS32", 0, 8) if wq[j] == "S" else KS) for j in range(2)] + [(I, Rf("W2", c * N, c * N + 8))]
+            mc = opt["mc"]
+            if c == 0 or not mc:
+                n = 1 + mc
+                j0 = k2[1] // N
+                it = [(Rf(k2[0], k2[1], k2[1] + n * N), M("N2"), Rf("ONE", 0, n * N))]
+                for h in range(4):
+                    for b in range(2):
+                        for gl in range(2):
+                            x0 = 32 * h + 16 * gl
+                            it.append((R2(k2[0], j0, j0 + n, 2 * h + b, N, 8), half(b, gl), R2("ET", 2 * t + c, 2 * t + c + n, x0, x0 + 16)))
+                PE("psJ", acc(it, stop=False), opens=k2[0], extra=shut if bk_["k2"][0][0] == bk_["k2"][1][0] else None)
+            if mc and c == 0:
+                inner = PE("psK2", acc([(k2, r, M("N4")), (k2, rho, n4r)], start=False, stop=False), inside=k2[0])
+                tops0 = tops
+                continue
+            PE("psK2", acc([(k2, r, M("N4")), (k2, rho, n4r)], start=False), closes=k2[0], extra=[inner] if mc else None)
+            shut = [V("W2", ts(Rf("W2", (c - mc) * N, c * N + N), Rf(k2[0], k2[1] - mc * N, k2[2]), -2048.0, A.max))]
+            if mc:
+                pts = [Rf(k2[0], 2 * N + 8 * j, 2 * N + 8 * j + 8) for j in range(2)]
+                PE("psT", acc([(pts[0],) + x for x in tops0]) + acc([(pts[1],) + x for x in tops]))
+                V("LST", ts(R2("SU", 2 * t + 2, 2 * t + 4, 0, 8), Rf(k2[0], 2 * N, 2 * N + 16), top, A.add))
             else:
-                V("W", ts(pc("WH", 2), reg(5, 2 * c, 2), -4096.0, A.add, -2048.0, A.max))
-                w0, w1 = Rf("WH", 2 * c * N, 2 * c * N + N), Rf("WH", 2 * c * N + N, 2 * c * N + 2 * N)
-                shut = PE("psT", acc([(pt, I, w20), (pt, w0, KS), (pt, w1, KS)]))
-                top, rest, nw = 2048.0 * 33, 2048.0, "NIB"
+                pt = Rf(k1[0], k1[1], k1[1] + 8)
+                PE("psT", acc([(pt,) + x for x in tops]))
+                V("LST", ts(Rf("SU", a + NA, a + NA + 8), pt, top, A.add))
+        for c in range(2):
+            P["c"] = str(c)
+            a, par, k0, rest = o + c * N, (t % 2) * NA + c * N, reg(*bk_["k"][c]), kept[c][8]
+            z = Rf("Z4", (2 * t + c) * ZW, (2 * t + c) * ZW + N)
             lst = Rf("SU", a + NA, a + NA + 8)
-            V("LST", ts(lst, pt, top, A.add))
             yd, y = Rf("YD", a, a + N), Rf("Y", a, a + N)
-            V("YD", tt(yd, ind(Xa, lst), Rf("F16", a + NA, a + NA + N), A.subtract))
-            S("Y", act(y, yd, AF.Abs, bias=1024.0))
+            fn = Rf(fb, a + NA, a + NA + N)
+            if opt["yd"][c] == "V":
+                V("YD", tt(yd, ind(Xa, lst), fn, A.subtract))
+                S("Y", act(y, yd, AF.Abs, bias=fo))
+            else:
+                xt = Rf("XT", c * N, c * N + N)
+                S("YD", act(xt, ind(Xa, lst), AF.Copy))
+                PE("psB", acc([(k0, M("NIB"), fn), (k0, I, xt)]))
+                S("Y", act(y, k0, AF.Abs, bias=fo))
             if not last:
                 for b in (2 * c, 2 * c + 1):
                     src = Rf("Y", o + NB * b, o + NB * b + NB)
-                    x0 = (2 * t + 2 + c) * 512 + NB * (b % 2)
+                    x0 = (2 * t + 2 + c) * ZW + NB * (b % 2)
                     dst = Rf("Z4", x0, x0 + NB)
                     if (b + t) % 4:
                         i = G("send", [("send", dict(in_=src, to=["Z4", x0], t=t, b=b))], dur=0.3, sem="none")
                         add(P, "N", "recv", [], wr=[dst], dur=EST["net"], sem="za%d%d" % (t + 1, b), inc=0, extra=[i])
                     else:
                         add(P, "Y", "stay", [("copy", dict(out=dst, in_=src))], dur=0.1, sem="za%d%d" % (t + 1, b), inc=16, prio=2.2)
-            xn = reg(3, 2 + c)
+            xn = reg(*bk_["xn"][c])
             PE("psN", acc([(xn, I, z), (xn, I, y)]))
-            V("XN", ts(Rf("XN", a, a + N), xn, 0.5, A.mult, -0.25, A.add))
-            if opt["split"] or c == 1:
-                c0 = c if opt["split"] else 0
+            if opt["xn"][c] == "V":
+                V("XM", ts(Rf("XM", c * N, c * N + N), xn, 0.4995, A.mult, 12582912.0, A.add))
+                V("XN", ts(Rf("XB", a, a + N), Rf("XM", c * N, c * N + N), -12582912.0, A.add))
+            elif opt["xn"][c] == "I":
+                V("XN", ts(Rf("XN", a, a + N), xn, 0.5, A.mult, -0.25, A.add))
+            elif opt["xn"][c] == "J":
+                S("XM", act(Rf("XM", c * N, c * N + N), xn, AF.Identity, bias=12582912.0, scale=0.4995))
+                V("XN", ts(Rf("XN", a, a + N), Rf("XM", c * N, c * N + N), -12582912.0, A.add))
+            else:
+                S("XM", act(Rf("XM", c * N, c * N + N), xn, AF.Identity, bias=12582912.0, scale=0.4995))
+                S("XN", act(Rf("XB", a, a + N), Rf("XM", c * N, c * N + N), AF.Identity, bias=-12582912.0))
+            if split or c == 1:
+                c0 = c if split else 0
                 l0, l1 = 16 * t + 8 * c0, 16 * t + 8 * c + 8
-                py = Rf("ps6", 3 * N + 8 * c0, 3 * N + 8 * c + 8)
-                PE("psY", acc([(py, sel(m), Rf("Y", o + c0 * N + m, a + N, 16)) for m in range(16)]))
+                py = Rf("ps%d" % opt["yb"], 3 * N + 8 * c0, 3 * N + 8 * c + 8)
                 W = lambda nm: Rf(nm, l0, l1)
-                V("PI1", cp(W("PI1"), py))
-                V("PI2", ts(W("PI2"), W("PI1"), 15, A.bitwise_and))
-                V("PI3", tt(W("PI3"), W("PI2"), Rf("BASE", 0, l1 - l0), A.add))
-                V("PLC", cp(W("PLC"), W("PI3")))
-            P["up"] = 0.0
-            sw = Rf("SW", (2 * t + c) * N, (2 * t + c + 1) * N)
-            cn = reg(4, 2 + c)
-            PE("psC", acc([(cn, r, M("N4")), (cn, rho, n4r)]))
-            S("SW", act(sw, cn, AF.Relu, bias=-7.0, scale=1.0 / 4096))
-            if not last:
-                en = Rf("E16", a + NA, a + NA + N)
-                PE("psE", acc([(cn, I, e16), (cn, M("NK4"), sw)]))
-                V("E16", tt(en, w2, cn, A.max))
-                V("EU", ts(Rf("EU", a + NA, a + NA + N), en, 2048.0, A.add))
-            ms = pc("MS")
-            PE("psQ", acc([(reg(7, 0), M("SM"), r), (reg(7, 0), M("Q256"), q)]))
-            S("MS", act(ms, reg(7, 0), AF.Sign, bias=-256.5))
-            PE("psX", acc([(reg(7, 1), s16, I), (reg(7, 1), M("NQ"), ms)]) + acc([(reg(7, 2), e16, I), (reg(7, 2), M("PQ"), ms)]))
-            V("SE", ts(pc("SE", 2), reg(7, 1, 2), -2048.0, A.add, -2048.0, A.max))
-            sx, ex = Rf("SE", 2 * c * N, 2 * c * N + N), Rf("SE", 2 * c * N + N, 2 * c * N + 2 * N)
-            PE("psM", acc([(reg(7, 3), I, sx), (reg(7, 3), I, ex), (reg(7, 3), M("NLI"), r)]))
-            mm_ = pc("MM")
-            V("MM", ts(mm_, reg(7, 3), 2048.0, A.add, -2048.0, A.max))
-            sn, i8 = Rf("ps7", 8, N), Rf("WI", 24, 16 + N)
-            PE("psS", acc([(sn, sx, i8), (sn, ex, i8), (sn, w0, Rf(nw, 8, N)), (sn, mm_, Rf("SHI", 8, N))]))
-            V("SU", ts(Rf("SU", a + NA + 8, a + NA + N), sn, rest, A.add))
-            V("S16", ts(Rf("S16", a + NA, a + NA + N), Rf("SU", a + NA, a + NA + N), -2048.0, A.add))
-            if last:
-                bk = 2 + c
-                it = [(reg(bk, 0), M("PQ"), ONE)]
-                for h in range(4):
-                    for gl in range(2):
-                        for b in range(2):
-                            it.append((Rf("ps%d" % bk, 32 * h + 16 * gl, 32 * h + 16 * gl + 16), half(gl, b), Rf("S16", a + NA + 2 * h + b, a + NA + N, 8)))
-                PE("psO", acc(it))
-                V("YS", tr(pc("YSO"), reg(bk, 0)))
-        for c in range(2) if opt["split"] else (None,):
+                it = [(py, sel(m), Rf("Y", o + c0 * N + m, a + N, 16)) for m in range(16)]
+                if opt["pi"] == 4:
+                    PE("psY", acc(it))
+                    V("PI1", cp(W("PI1"), py))
+                    V("PI2", ts(W("PI2"), W("PI1"), 15, A.bitwise_and))
+                    V("PI3", tt(W("PI3"), W("PI2"), Rf("BASE", 0, l1 - l0), A.add))
+                    V("PLC", cp(W("PLC"), W("PI3")))
+                else:
+                    pz = Rf("ps4", 2 * N, 2 * N + l1 - l0)
+                    i = PE("psY", acc(it))
+                    V("PI1", ts(W("PH"), py, 16392.5, A.add))
+                    PE("psL", acc([(pz, I, Rf("BH", 0, l1 - l0))] + [(pz,) + x[1:] for x in it], stop=False), opens="ps4", extra=[i])
+                    PE("psL", acc([(pz, M("NIB"), W("PH"))], start=False), closes="ps4")
+                    V("PLC", cp(W("PLC"), pz))
+            if c == 1 or not opt["me"]:
+                c0 = 0 if opt["me"] else c
+                cs, n, x0 = range(c0, c + 1), c + 1 - c0, o + NA + c0 * N
+                bank, j0 = opt["cn"][c]
+                sw = Rf("SW", (2 * t + c0) * N, (2 * t + c + 1) * N)
+                PE("psC", [m for j in cs for m in acc([(reg(bank, j0 + j - c0), kept[j][0], M("N4")), (reg(bank, j0 + j - c0), kept[j][1], kept[j][3])])])
+                S("SW", act(sw, reg(bank, j0, n), AF.Relu, bias=-7.0, scale=1.0 / 4096))
+                if not last:
+                    en = Rf("E16", x0, x0 + n * N)
+                    PE("psE", acc([(reg(bank, j0, n), I, Rf("E16", x0 - NA, x0 - NA + n * N)), (reg(bank, j0, n), M("NK4"), sw)]))
+                    V("E16", tt(en, Rf("W2", c0 * N, c * N + N), reg(bank, j0, n), A.max))
+                    V("EU", ts(Rf("EU", x0, x0 + n * N), en, 2048.0, A.add))
+            if c == 1 or not opt["ms"]:
+                c0 = 0 if opt["ms"] else c
+                cs, n, x0 = range(c0, c + 1), c + 1 - c0, o + NA + c0 * N
+                (bq, jq), (bx, jx), (bm, jm), (bs, js) = opt["sb"][c]
+                both = lambda nm, k=1: Rf(nm, k * c0 * N, k * (c + 1) * N)
+                one = lambda nm, j: Rf(nm, j * N, j * N + N)
+                PE("psQ", acc([(reg(bq, jq, n), M("SM"), Rf("RR", par - (c - c0) * N, par + N)), (reg(bq, jq, n), M("Q256"), Rf("QQ", par - (c - c0) * N, par + N))]))
+                S("MS", act(both("MS"), reg(bq, jq, n), AF.Sign, bias=-256.5))
+                ins = []
+                for j in cs:
+                    b1, b2 = reg(bx, jx + 2 * (j - c0)), reg(bx, jx + 2 * (j - c0) + 1)
+                    ins += acc([(b1, kept[j][4], I), (b1, M("NQ"), one("MS", j))]) + acc([(b2, kept[j][5], I), (b2, M("PQ"), one("MS", j))])
+                PE("psX", ins)
+                V("SE", ts(both("SE", 2), reg(bx, jx, 2 * n), -2048.0, A.add, -2048.0, A.max))
+                PE("psM", [m for j in cs for m in acc([(reg(bm, jm + j - c0), I, one("SE", 2 * j)), (reg(bm, jm + j - c0), I, one("SE", 2 * j + 1)),
+                                                      (reg(bm, jm + j - c0), M("NLI"), kept[j][0])])])
+                V("MM", ts(both("MM"), reg(bm, jm, n), 2048.0, A.add, -2048.0, A.max))
+                ins, i8 = [], Rf("WI", 24, 16 + N)
+                for j in cs:
+                    sn = Rf("ps%d" % bs, (js + j - c0) * N + 8, (js + j - c0 + 1) * N)
+                    ins += acc([(sn, one("SE", 2 * j), i8), (sn, one("SE", 2 * j + 1), i8), (sn, kept[j][6], Rf(kept[j][7], 8, N)), (sn, one("MM", j), Rf("SHI", 8, N))])
+                PE("psS", ins)
+                V("SU", ts(R2("SU", 2 * t + 2 + c0, 2 * t + 3 + c, 8, N), R2("ps%d" % bs, js, js + n, 8, N), rest, A.add))
+                V("S16", ts(Rf("S16", x0, x0 + n * N), Rf("SU", x0, x0 + n * N), -2048.0, A.add))
+                if last:
+                    bk = "ps%d" % bk_["o"][c]
+                    it = [(reg(bk_["o"][c], 0, n), M("PQ"), Rf("ONE", 0, n * N))]
+                    for h in range(4):
+                        for gl in range(2):
+                            for b in range(2):
+                                it.append((R2(bk, 0, n, 32 * h + 16 * gl, 32 * h + 16 * gl + 16), half(gl, b), R2("S16", 2 * NT + c0, 2 * NT + c + 1, 2 * h + b, N, 8)))
+                    PE("psO", acc(it))
+                    V("YS", tr(both("YSO"), reg(bk_["o"][c], 0, n)))
+        for c in range(2) if split else (None,):
             lo, hi = (0, 2) if c is None else (c, c + 1)
-            V("SC", cp(ind(Rf("X", lo * L, hi * L), Rf("PLC", 16 * t + 8 * lo, 16 * t + 8 * hi)), Rf("XN", o + lo * N, o + hi * N)))
+            P["c"] = str(hi - 1)
+            V("SC", cp(ind(Rf("X", lo * L, hi * L), Rf("PLC", 16 * t + 8 * lo, 16 * t + 8 * hi)), Rf("XN" if opt["xn"][lo] in "IJ" else "XB", o + lo * N, o + hi * N)))
+    P["c"] = ""
     for lo, hi in ((0, NT - 1), (NT - 1, NT)):
         V("PT", tt(Rf("PT", 16 * lo, 16 * hi), Rf("UH", 16 * lo, 16 * hi), Rf("TC", 16 * lo, 16 * hi), A.add))
         V("PV", tt(Rf("PV", 16 * lo, 16 * hi), Rf("PT", 16 * lo, 16 * hi), R2("SW", 2 * lo, 2 * hi, 0, 8), A.mult))
@@ -482,19 +636,22 @@ def build(opt=None):
     pa = Rf("ps4", 0, 16)
     PE("psP", acc([(pa, M("K4"), R2("SW", 2 * t, 2 * t + 2, 0, 8)) for t in range(NT)]))
     V("YP", tt(Rf("YPO", 0, 16), Rf("PW", 96, 112), pa, A.add))
-    V("YF", ts(Rf("YFO", 0, NA), Rf("F16", NT * NA, NT * NA + NA), -1024.0, A.add))
-    for c in range(16):
-        V("CI", ts(Rf("CI", c * N, c * N + N), I, float(c + 1), A.mult))
+    if fo:
+        V("YF", ts(Rf("FB", NT * NA, NT * NA + NA), Rf("F16", NT * NA, NT * NA + NA), -1024.0, A.add))
     for c in range(2):
+        P["c"] = str(c)
         PE("psV", acc([(reg(c, 0), Rf("CI", k * N, k * N + N), Rf("X", c * L + k, c * L + L, 16)) for k in range(16)]))
         S("YX", act(Rf("YXO", c * N, c * N + N), reg(c, 0), AF.Copy))
-    for k, (o_, b) in enumerate((("yf", "YFO"), ("yp", "YPO"), ("ys", "YSO"), ("yx", "YXO"))):
-        add(P, "Y", "st" + o_, [("store", dict(dst=o_, in_=Rf(b, 0, SCRATCH[b][1][1])))], dur=0.1, sem="ost%d" % k, inc=16, prio=2.0)
+    for k, (o_, b) in enumerate((("yf", Rf("FB", NT * NA, NT * NA + NA)), ("yp", Rf("YPO", 0, 16)), ("ys", Rf("YSO", 0, NA)), ("yx", Rf("YXO", 0, NA)))):
+        add(P, "Y", "st" + o_, [("store", dict(dst=o_, in_=b))], dur=0.1, sem="ost%d" % k, inc=16, prio=2.0)
     return P
 
 
-def schedule(P, e=None):
+def schedule(P, e=None, up=None, turn=None, turn0=None):
     e = e or EST
+    up = UP if up is None else up
+    turn = TURN if turn is None else turn
+    turn0 = TURN0 if turn0 is None else turn0
     T = P["tasks"]
     n = len(T)
     succ = [[] for _ in range(n)]
@@ -516,7 +673,7 @@ def schedule(P, e=None):
     for i in range(n - 1, -1, -1):
         far[i] = T[i]["dur"] + max([lat(i, j, k) + far[j] for j, k in succ[i]] or [T[i]["prio"]])
     for i in range(n):
-        far[i] += 4.0 if T[i]["name"] in HASH else T[i]["up"]
+        far[i] += up.get(T[i]["label"], 0.0)
     ready = [0.0] * n
     left = [len(t["pre"]) for t in T]
     free = {}
@@ -540,30 +697,50 @@ def schedule(P, e=None):
                 if q2 != T[i]["q"] and e2 + e["lat"] > r:
                     r = e2 + e["lat"]
         return r
+    byname, seq = {}, {q: [] for q in free}
+    for t in T:
+        byname.setdefault((t["t"], t["q"], t["label"]), []).append(t["i"])
+    for t in range(NT):
+        for q, names in (turn0 if t == 0 else turn if t < NT - 1 else LAST).items():
+            for nm in names.split():
+                lst = byname.get((t - 1, q, nm[1:]) if nm[0] == "-" else (t, q, nm))
+                if lst:
+                    seq[q].append(lst.pop(0))
+    named = {i for q in seq for i in seq[q]}
+    at = {q: 0 for q in seq}
     while len(order) < n:
         best = None
         for q, lst in avail.items():
+            nxt = seq[q][at[q]] if at[q] < len(seq[q]) else None
+            lst = [j for j in lst if j == nxt or j not in named]
             if not lst:
                 continue
             s = min(er(i) for i in lst)
             if q != "N":
                 s = max(free[q], s)
             if best is None or s < best[0]:
-                best = (s, q)
-        s, q = best
+                best = (s, q, lst)
+        if best is None or best[0] > 1e8:
+            k, q, j = min((seq[q].index(j) - at[q], q, j) for q in avail for j in avail[q] if j in named and er(j) < 1e8)
+            seq[q].remove(j)
+            seq[q].insert(at[q], j)
+            P.setdefault("moved", []).append(T[j]["label"])
+            continue
+        s, q, lst = best
         if q == "N":
             i = min(avail[q], key=lambda j: ready[j])
             s = ready[i]
         else:
-            c = [j for j in avail[q] if er(j) <= s + 0.03]
+            c = [j for j in lst if er(j) <= s + 0.03]
             d = [j for j in c if T[j]["inc"] == 16]
             i = min(d) if d else max(c, key=lambda j: far[j])
             s = max(free[q], er(i))
-        if "opens" in T[i]:
-            opened.add(T[i]["opens"])
         if "closes" in T[i]:
             opened.discard(T[i]["closes"])
+        if "opens" in T[i]:
+            opened.add(T[i]["opens"])
         avail[q].remove(i)
+        at[q] += i in named
         start[i] = s
         end = s + T[i]["dur"]
         for b in T[i]["banks"]:
@@ -605,22 +782,22 @@ def rank_program(g, core, T, topo):
     total = {}
     info = {}
 
-    def ap(v):
+    def ap(v, p0=0, p1=128):
         if not isref(v):
             return v
         if v[0] == "#":
             return ap(v[1]).indirect(ap(v[2]))
         b = T[v[0]]
         if len(v) == 6:
-            return b[:, v[4]:v[5], v[1]:v[2]:v[3]]
+            return b[p0:p1, v[4]:v[5], v[1]:v[2]:v[3]]
         sh = SCRATCH[v[0]][1]
         if len(sh) == 2:
-            return b[:, v[1]:v[2]:v[3]]
+            return b[p0:p1, v[1]:v[2]:v[3]]
         w = sh[2]
         o = v[1] // w
         if v[2] <= o * w + w:
-            return b[:, o, v[1] - o * w:v[2] - o * w:v[3]]
-        return b[:, o:v[2] // w, :]
+            return b[p0:p1, o, v[1] - o * w:v[2] - o * w:v[3]]
+        return b[p0:p1, o:v[2] // w, :]
 
     def lanes(src, dst):
         return topo.engines(src, dst)[::2]
@@ -669,7 +846,7 @@ def rank_program(g, core, T, topo):
             elif m == "copy":
                 h = eng.dma_start(ap(kw["out"]), ap(kw["in_"]))
             else:
-                h = eng.dma_start(T[kw["dst"]][:, 0:kw["in_"][2]], ap(kw["in_"]))
+                h = eng.dma_start(T[kw["dst"]][:, 0:cnt(kw["in_"])], ap(kw["in_"]))
             h.then_inc(T.sem[t["sem"]], 16)
             know = dict(ck)
             know[t["sem"]] = 16
@@ -680,10 +857,12 @@ def rank_program(g, core, T, topo):
         for j, (m, kw) in enumerate(t["ins"]):
             a = {k: ap(v) for k, v in kw.items()}
             if m == "matmul":
-                h = eng.matmul(a["out"], a["lhsT"], a["rhs"], a["start"], a["stop"])
+                h = eng.matmul(ap(kw["out"], *kw["part"]), a["lhsT"], a["rhs"], a["start"], a["stop"])
             elif m == "iota":
                 flag = {} if SCRATCH[kw["out"][0]][2] == "int32" else {"allow_small_or_imprecise_dtypes": True}
                 h = eng.iota(a["out"], a["pattern"], a["base"], a["channel_multiplier"], **flag)
+            elif m == "affine" and "op" in kw:
+                h = eng.affine_select(out=a["out"], in_=a["in_"], pattern=kw["pattern"], compare_op=kw["op"], fill=kw["fill"], base=0, channel_multiplier=-1)
             elif m == "affine":
                 h = eng.affine_select(out=a["out"], in_=a["in_"], pattern=[[0, cnt(kw["in_"])]], compare_op=A.is_gt, fill=0.0, base=1, channel_multiplier=0)
             elif m == "memset":
@@ -704,6 +883,7 @@ def rank_program(g, core, T, topo):
         know = dict(ck)
         know[sem] = total[sem]
         info[i] = (sem, total[sem], know)
-    for sem in sorted(total):
-        g.wait_ge(T.sem[sem], total[sem])
     g.wait_ge(T.sem.lsent, nloc)
+    for sem in sorted(total):
+        if all(ck.get(sem, 0) < total[sem] for ck in clock.values()):
+            g.wait_ge(T.sem[sem], total[sem])

@@ -10,7 +10,7 @@ SCRATCH = {}
 for _nm, _sh, _ty in (
         ("X", [NR], "bfloat16"), ("PL", [NR], "int32"), ("Z4", [2 * NT, ZW], "bfloat16"), ("Y", [NT * NA], "bfloat16"),
         ("DS", [2 * L], "bfloat16"), ("HS", [2 * L], "float16"), ("DE", [2 * L], "bfloat16"), ("AE", [2 * L], "bfloat16"),
-        ("TH", [NA], "int32"), ("S0", [NA], "int32"), ("P0", [16], "int32"), ("FB", [7 * NA], "bfloat16"), ("FM", [NA], "float32"),
+        ("TH", [NA], "int32"), ("S0", [NA], "int32"), ("P0", [16], "int32"), ("FB", [7 * NA], "bfloat16"),
         ("UB", [NT * 16], "bfloat16"), ("UF", [NT * 16], "float32"),
         ("KT", [3 * NA], "float16"), ("TT", [6, N], "float16"), ("THA", [NA], "float16"),
         ("EK", [NT * NA], "float16"), ("ET", [2 * NT, N], "float16"),
@@ -24,17 +24,18 @@ for _nm, _sh, _ty in (
         ("U1", [NT * 16], "int32"), ("U2", [NT * 16], "int32"), ("U3", [NT * 16], "int32"),
         ("U5", [NT * 16], "int32"), ("UH", [NT * 16], "int32"), ("UU", [NT * 16], "uint16"), ("PU", [16], "uint16"),
         ("PT", [NT * 16], "int32"), ("PV", [NT * 16], "int32"), ("PW", [7 * 16], "int32"), ("YPO", [16], "float32"),
-        ("YSO", [NA], "float32"), ("YFO", [NA], "bfloat16"), ("YXO", [NA], "float32"),
+        ("YSO", [NA], "float32"), ("YXO", [NA], "float32"),
         ("IOC", [160], "float32"), ("PC", [1], "float32"), ("PI", [1], "int32"), ("IO8", [N], "int32"), ("BASE", [16], "int32"), ("TC", [NT * 16], "int32"),
         ("IOB", [16], "int32"), ("PG", [1], "int32"), ("PK", [1], "int32"), ("PO", [1], "int32"), ("C15F", [1], "float32"), ("PGF", [1], "float32"),
         ("WK", [1], "float32"), ("K16", [1], "float32"), ("ODC", [1], "float32"), ("EVC", [1], "float32"), ("A8", [N], "int32"),
         ("WI", [160], "bfloat16"), ("EVW", [160], "bfloat16"), ("ODW", [160], "bfloat16"), ("BIG", [144], "bfloat16"), ("BIGW", [144], "bfloat16"),
-        ("GS", [8], "bfloat16"), ("GN", [8], "bfloat16"), ("GH", [8], "bfloat16"), ("O8", [N], "bfloat16"), ("T3", [N], "bfloat16"), ("T4", [N], "bfloat16"),
+        ("GS", [8], "bfloat16"), ("GN", [8], "bfloat16"), ("GH", [8], "bfloat16"), ("O8", [N], "bfloat16"), ("T4", [N], "bfloat16"),
         ("T1", [N], "bfloat16"), ("T2", [N], "bfloat16"), ("ONE", [NA], "bfloat16"), ("NIB", [N], "bfloat16"), ("HI", [N], "bfloat16"), ("I32", [N], "bfloat16"),
         ("N64", [N], "bfloat16"), ("PQ", [N], "bfloat16"), ("NQ", [N], "bfloat16"), ("NK4", [N], "bfloat16"), ("K4", [N], "bfloat16"), ("Q256", [N], "bfloat16"),
         ("G1", [N], "bfloat16"), ("G1H", [N], "bfloat16"), ("N4", [N], "bfloat16"), ("N2", [N], "bfloat16"), ("SM", [N], "bfloat16"),
         ("NLI", [N], "bfloat16"), ("SHI", [N], "bfloat16"), ("CT", [N], "bfloat16"), ("KS32", [8], "float32"), ("NI32", [N], "float32"),
-        ("CI", [L], "bfloat16"), ("CJ", [L], "bfloat16")):
+        ("CI", [L], "bfloat16"), ("MF", [NA], "float32"), ("SH32", [N], "float32"), ("G32", [8], "float32"), ("CU", [N], "bfloat16"),
+        ("HF", [2 * L], "float32"), ("IO16", [N], "float32"), ("OB", [N], "bfloat16"), ("CV", [N], "bfloat16"), ("XH", [N], "float16"), ("YO", [N], "float32")):
     SCRATCH[_nm] = ("sbuf", [128] + _sh, _ty)
 for _k in range(8):
     SCRATCH["ps%d" % _k] = ("psum", [128, 4, N], "float32")
@@ -94,8 +95,21 @@ EST.update(lx=4.5, lpl=9.5)
 TURN0 = {'V': 'ONE PG C15 PK BIG PO WK WI ODC A8 BIGW PQ ODW CT EVC O8 KS KH EVW N4 TT PU U3 PGF TT N2 GH SUs HI S16s THA T1 GN GS0 GS0 GS0 GS1 H0 KE TT UH GS NI0 EUs GS1 RR0 GV0 F160 UU H1 EK ET AV0 NI1 SM KS32 GV1 RR1 E16s NI32 K16 AV1 QQ0 W20 F16 QQ1 LST0 YD0 W21 SE1 LST1 YD1 BASE BH MM1 E161 PI11 EU1 PLC1 SC1', 'S': 'lt lp U1 U2 lf GE1 GE0 GE0 GE0 AE0 AE0 GE1 AE0 GE1 RP0 AE1 AE1 Wa0 AE1 RP1 MS1 Y0 Wa1 Wb1 SW1 XM0 Y1 XM1 XN0 XN1', 'P': 'psU psG psG psA psA psH0 psA psW0 psW0 psW1 psW1 psZ0 psD0 psZ0 psH1 psZ0 psJ0 psZ1 psK00 psF psD0 psZ1 psD1 psK10 psK10 psK01 psK20 psZ1 psJ1 psT0 psK11 psD1 psQ1 psK11 psK21 psX1 psC1 psN0 psT1 psE1 psM1 psN1 psY1 psL1 psL1 psS1', 'G': 'pi ioc pc NIB io8 NIB iob zx1 Q256 zx0 G1 zx0 zx1 G1 zx0 zx1 Q256 NQ NQ SHI NK4 G1H NK4 SM NLI G1H I32 I32 N64 N64 CI K4 SM CI tc send0 K4 send1 send1'}
 
 
-OPT.update(ep0=("SSSR", "SSRR"))
-TURN0 = {'V': 'PG ONE PO ODC EVC WI PK C15 BIG WK PGF KS A8 TT G8 KH TT O8 SUs PU F160 S16s THA GS0 GS0 U3 GS0 GS1 UH H0 KE TT GS1 EUs UU H1 EK NI0 K16 ET GV0 SM AV0 E16s RR0 NI1 F16 RR1 GV1 QQ0 GV1 QQ1 AV1 W20 BH AV1 LST0 YD0 W21 SE1 LST1 YD1 MM1 E161 PI11 EU1 PLC1 SC1', 'S': 'lp lt lf EVW NIB CT PQ ODW BIGW N2 U1 GH U2 NK4 T1 N4 HI GN K4 N64 NQ I32 NI32 Q256 KS32 GE0 GE0 GE0 AE0 AE0 GE1 AE0 GE1 RP0 AE1 Wa0 AE1 MS1 RP1 Y0 Wb1 Wa1 SW1 Y1 XM1 XM0 XN1 XN0', 'P': 'psA psA psU psG psG psH0 psA psW0 psW0 psF psW1 psW1 psZ0 psH1 psZ0 psZ0 psJ0 psK00 psD0 psZ1 psD0 psK01 psK10 psZ1 psK10 psK20 psD1 psQ1 psT0 psK11 psD1 psJ1 psK11 psK21 psX1 psC1 psT1 psN0 psE1 psM1 psN1 psY1 psL1 psL1 psS1', 'G': 'pi pc iob ioc io8 zx0 zx0 zx0 zx1 zx1 G1 zx1 tc G1 G1H G1H SM NLI SHI SM CI CI send0 send1 send1'}
+OPT.update(ep0=("SSSR", "SSRR"), mm="V", h0="VV", fin=0)
+TURN0 = {'V': 'PG ONE PO ODC EVC WI PK C15 BIG WK PGF KS A8 TT G8 KH TT O8 SUs PU F160 S16s THA GS0 GS0 U3 GS0 GS1 UH H0 KE TT GS1 EUs UU H1 EK NI0 K16 ET GV0 SM AV0 E16s RR0 NI1 F16 RR1 GV1 QQ0 GV1 QQ1 AV1 W20 BH AV1 LST0 YD0 W21 SE1 LST1 YD1 MM1 E161 PI11 EU1 PLC1 SC1', 'S': 'lp lt lf EVW NIB CT PQ ODW BIGW N2 U1 GH U2 NK4 T1 N4 HI GN K4 N64 NQ I32 NI32 Q256 KS32 ' + 'CI ' * 16 + 'GE0 GE0 GE0 AE0 AE0 GE1 AE0 GE1 RP0 AE1 Wa0 AE1 MS1 RP1 Y0 Wb1 Wa1 SW1 Y1 XM1 XM0 XN1 XN0', 'P': 'psA psA psU psG psG psH0 psA psW0 psW0 psF psW1 psW1 psZ0 psH1 psZ0 psZ0 psJ0 psK00 psD0 psZ1 psD0 psK01 psK10 psZ1 psK10 psK20 psD1 psQ1 psT0 psK11 psD1 psJ1 psK11 psK21 psX1 psC1 psT1 psN0 psE1 psM1 psN1 psY1 psL1 psL1 psS1', 'G': 'pi pc iob ioc io8 zx0 zx0 zx0 zx1 zx1 G1 zx1 tc G1 G1H G1H SM NLI SHI SM CI CI send0 send1 send1'}
+
+
+OPT.update(h0="SS", fin=1, ms=0, sb=(((2, 0), (0, 1), (0, 3), (0, 0)), ((3, 0), (7, 0), (7, 2), (7, 0))), cn=(None, (1, 0)), w=("VV+", "SS"),
+           bk=dict(OPT["bk"], k1=((5, 1), (5, 3)), k2=((6, 0), (7, 0))), gs=((2, 2, 4, 8), (8, 8)), gs0=((4, 4, 4, 4), (4, 4, 4, 4)), ep0=("SSRR", "SSSR"))
+TURN0 = {'V': 'ONE PG C15 PO PGF WI BIG EVC PK G8 ODC WK KS TT KH TT A8 SUs O8 S16s F160 PU THA GS0 GS0 GS0 GS0 GS1 GS1 GS1 GS1 U3 KE TT UH UU NI0 SM EUs GV0 EK ET GV0 AV0 QQ0 AV0 RR0 NI1 E16s GV1 RR1 AV1 Wa0 F16 W20 QQ1 K16 LST0 YD0 BH SE0 W21 OB MM0 LST1 YD1 E161 SE1 EU1 SU0 PI11 PLC1 SC1 S160', 'S': 'lt lf lp HI EVW ODW PQ GH BIGW G32 NIB NQ T1 CU U1 N2 GN Q256 CI N4 U2 CI NI32 CI CT CI CI CI N64 KS32 NK4 K4 H0 CV CI CI CI I32 H1 GE0 GE0 GE1 AE0 AE0 GE1 AE1 RP0 GE1 AE1 AE1 MS0 CI Wa1 RP1 Y0 Wb1 CI SW1 XM0 MS1 Y1 XN0 CI XM1 XN1 CI CI CI CI', 'P': 'psA psA psU psG psG psW0 psW1 psW0 psF psH0 psW1 psA psH1 psZ0 psZ0 psD0 psJ0 psZ1 psK00 psD0 psK10 psZ1 psK20 psK10 psQ0 psK01 psZ1 psJ1 psT0 psD1 psD1 psX0 psK11 psQ1 psK11 psK21 psC1 psN0 psM0 psT1 psE1 psS0 psX1 psN1 psY1 psL1 psL1 psM1', 'G': 'pc pi ioc io8 iob zx0 zx1 zx0 zx1 NLI SM G1 G1 io16 G1H G1H SHI tc SM send0 send1 send1'}
+TURN = {'V': '-MM1 GS0 GS0 GS0 GS0 U3 H0 -SU1 UH GS1 NI0 UU RR0 EK QQ0 ET GS1 W20 Wa0 H1 F16 LST0 YD0 NI1 -S161 RR1 QQ1 SE0 W21 MM0 LST1 YD1 SU0 E161 SE1 PI11 EU1 S160 PLC1 SC1', 'S': 'GE0 GE0 AE0 U1 GE0 U2 GE0 AE0 GE1 AE0 AE0 GE1 AE1 RP0 GE1 GE1 AE1 AE1 AE1 MS0 Y0 RP1 Wb1 Wa1 SW1 XM0 MS1 Y1 XM1 XN0 XN1', 'P': 'psZ0 psU psG psF psG psW0 psZ0 psZ0 -psS1 psD0 psW0 psZ0 psH0 psZ1 psD0 psK00 psK10 psZ1 psJ0 psK20 psK10 psJ1 psZ1 psW1 psW1 psZ1 psT0 psH1 psQ0 psD1 psD1 psX0 psK01 psK11 psK11 psK21 psC1 psN0 psQ1 psM0 psT1 psS0 psX1 psE1 psN1 psY1 psL1 psL1 psM1', 'G': 'zx0 zx0 zx0 zx1 zx1 zx1 send0 send0 send1 send1'}
+LAST = {'V': '-MM1 GS0 GS0 GS0 GS0 H0 -SU1 U3 UH GS1 NI0 UU RR0 EK -S161 QQ0 ET GS1 W20 Wa0 H1 F16 LST0 YD0 NI1 RR1 SE0 W21 QQ1 PI10 MM0 LST1 PT YD1 SU0 PV PLC0 SE1 S160 PW PI11 SC0 PT MM1 XH1 PLC1 YF PW XD1 YS0 PW SU1 PV S161 PW XP1 PW YX1 PW YS1 YP', 'S': 'GE0 GE0 GE0 GE0 U1 AE0 U2 AE0 GE1 AE0 AE0 GE1 GE1 RP0 AE1 GE1 AE1 AE1 AE1 MS0 YO1 Y0 RP1 Wa1 Wb1 MS1 Y1 XM0 XN0 XM1 XN1 SW1 YX0', 'P': '-psS1 psD0 psZ0 psU psG psZ0 psG psF psW0 psW0 psZ0 psZ0 psH0 psV1 psZ1 psD0 psK00 psD1 psZ1 psJ0 psK10 psK10 psK20 psJ1 psW1 psZ1 psQ0 psT0 psZ1 psW1 psH1 psD1 psX0 psK01 psK11 psK11 psK21 psY0 psM0 psT1 psQ1 psN0 psS0 psL0 psL0 psX1 psY1 psR1 psN1 psL1 psL1 psM1 psC1 psI1 psO0 psI1 psS1 psV0 psO1 psP', 'G': 'zx0 zx0 zx0 zx1 zx1 zx1'}
+
+
+OPT.update(bk=dict(OPT["bk"], k=((5, 0), (6, 1))), w=("VV+", "VS"), h0="SV", ep0=("SSSR", "SSRR"))
+TURN0 = {'V': 'PG PK PGF ONE PO G8 WI ODC A8 WK C15 EVC BIG KS TT KH O8 TT SUs S16s F160 THA GS0 GS0 F16 GS0 U3 PU GS0 GS1 SM GS1 UH KE UU TT GS1 EUs GS1 EK H1 GV0 NI0 E16s RR0 ET QQ0 K16 AV0 NI1 GV1 GV1 AV1 AV1 W20 Wa0 QQ1 RR1 LST0 BH YD0 Wa1 SE0 W21 MM0 LST1 YD1 OB SU0 E161 SE1 PI11 S160 EU1 PLC1 SC1', 'S': 'lf lt lp PQ ODW HI CI EVW N2 NIB NQ G32 T1 CI CU N4 BIGW U1 U2 KS32 CI GN Q256 GH CT NI32 CV CI K4 CI H0 CI CI CI NK4 I32 N64 CI CI GE0 GE0 GE0 AE0 GE1 AE0 AE0 GE1 RP0 AE1 AE1 MS0 RP1 Y0 Wb1 CI CI SW1 MS1 Y1 CI XM0 XM1 XN1 XN0 CI CI CI', 'P': 'psA psA psU psF psG psG psW0 psW0 psW1 psA psH0 psZ0 psW1 psH1 psZ0 psZ0 psK00 psJ0 psQ0 psD0 psZ1 psD0 psK10 psZ1 psK10 psK20 psJ1 psD1 psT0 psD1 psK01 psX0 psK11 psK11 psK21 psC1 psM0 psT1 psN0 psQ1 psS0 psE1 psX1 psN1 psY1 psL1 psL1 psM1', 'G': 'pi ioc pc iob io8 zx0 zx1 zx0 G1 zx1 SHI SM SM G1 NLI tc G1H G1H io16 send0 send1 send1'}
+TURN = {'V': '-MM1 GS0 GS0 GS0 GS0 H0 U3 -SU1 UH GS1 NI0 UU RR0 EK QQ0 ET GS1 W20 Wa0 H1 F16 LST0 -S161 YD0 NI1 RR1 QQ1 SE0 Wa1 W21 MM0 LST1 YD1 SE1 SU0 E161 PI11 S160 EU1 PLC1 SC1', 'S': 'GE0 GE0 GE0 AE0 U1 GE0 U2 AE0 GE1 AE0 AE0 GE1 AE1 RP0 GE1 AE1 GE1 AE1 AE1 MS0 Y0 RP1 Wb1 SW1 MS1 XM0 Y1 XN0 XM1 XN1', 'P': 'psZ0 psU psF psG psW0 psG psZ0 psZ0 -psS1 psD0 psW0 psZ0 psH0 psZ1 psD0 psK00 psK10 psZ1 psJ0 psK20 psK10 psJ1 psZ1 psW1 psD1 psW1 psZ1 psT0 psH1 psQ0 psD1 psX0 psK01 psK11 psK11 psK21 psC1 psM0 psN0 psT1 psQ1 psS0 psX1 psE1 psN1 psY1 psL1 psL1 psM1', 'G': 'zx0 zx0 zx0 zx1 zx1 zx1 send0 send0 send1 send1'}
+LAST = {'V': '-MM1 GS0 GS0 GS0 -SU1 GS0 -S161 H0 U3 GS1 UH NI0 UU RR0 EK QQ0 ET GS1 Wa0 W20 H1 LST0 F16 YD0 NI1 RR1 QQ1 SE0 Wa1 W21 PT PI10 MM0 LST1 PV YD1 PT PW SU0 PLC0 SE1 S160 PI11 SC0 MM1 XH1 PLC1 PW PW SU1 PW S161 PV XD1 PW XP1 PW YF YP YS0 YX1 YS1', 'S': 'GE0 GE0 GE0 AE0 U1 GE0 AE0 U2 GE1 AE0 AE0 GE1 GE1 RP0 AE1 GE1 AE1 MS0 AE1 AE1 Y0 RP1 Wb1 YO1 MS1 Y1 XM0 XN0 XM1 XN1 SW1 YX0', 'P': '-psS1 psD0 psZ0 psZ0 psU psG psZ0 psW0 psW0 psG psF psZ0 psH0 psV1 psZ1 psD0 psD1 psK00 psZ1 psJ0 psK10 psQ0 psK10 psK20 psZ1 psW1 psJ1 psT0 psZ1 psW1 psH1 psD1 psX0 psK01 psK11 psK21 psK11 psY0 psM0 psT1 psQ1 psL0 psN0 psS0 psL0 psX1 psY1 psL1 psM1 psR1 psN1 psL1 psC1 psI1 psS1 psV0 psI1 psP psO0 psO1', 'G': 'zx0 zx0 zx0 zx1 zx1 zx1'}
 
 
 def Rf(buf, lo, hi, st=1):
@@ -336,8 +350,17 @@ def build(opt=None):
     cut("G1H", M("G1H"), M("T2"), A.not_equal, 2048.0)
     cut("NLI", M("NLI"), M("N4"), A.is_ge, 0.0)
     cut("SHI", M("SHI"), Rf("WI", 8, 8 + N), A.not_equal, -1.0)
-    io("CI", Rf("CJ", 0, L), [[1, 16], [0, N]], 0, 1)
-    cut("CI", Rf("CI", 0, L), Rf("CJ", 0, L), A.is_equal, 0.0, 16)
+    if opt["fin"]:
+        io("io16", M("IO16"), [[1, 8], [0, 16]], 0)
+        V("OB", ts(M("OB"), M("IO16"), c1("PGF"), A.is_equal))
+        times("CV", M("CV"), I, 17.0, 128.0)
+    if opt["mm"] == "S":
+        times("SH32", M("SH32"), M("SHI"), 1.0)
+    if "S" in opt["h0"]:
+        times("G32", Rf("G32", 0, 8), Rf("GS", 0, 8), 1.0)
+        times("CU", M("CU"), I, -0.6875, -8.0)
+    for k in range(16):
+        times("CI", Rf("CI", k * N, k * N + N), I, k + 1.0)
     if "S" in "".join(opt["w"]):
         times("KS32", Rf("KS32", 0, 8), Rf("O8", 0, 8), 1.0)
         times("NI32", M("NI32"), I, -1.0)
@@ -374,11 +397,12 @@ def build(opt=None):
         U = lambda nm: Rf(nm, t * 16, t * 16 + 16)
         zb = R2("Z4", 2 * t, 2 * t + 2, 0, N)
         split = opt["split"][last]
+        gs = opt["gs"] if t else opt.get("gs0", opt["gs"])
         P["t"] = t
         for c in range(2):
             P["c"] = str(c)
             z0 = (2 * t + c) * ZW
-            for n in (1, 2, 4)[:2 + (max(opt["gs"][c]) > 4)]:
+            for n in (1, 2, 4)[:2 + (max(gs[c]) > 4)]:
                 G("zx", [("affine", dict(out=Rf("Z4", z0 + n * N, z0 + 2 * n * N), in_=Rf("Z4", z0, z0 + n * N)))])
         P["c"] = ""
         PE("psF", acc([(reg(2, 2, 2), I, Rf(fb, o, o + NA)), (reg(2, 2, 2), I, zb)]))
@@ -408,6 +432,9 @@ def build(opt=None):
         V("ET", tr(Rf("ET", o, o + NA), Rf("EK", o, o + NA)))
         ep = opt["ep0"] if t == 0 else opt["ep"]
         zturn, kept = 0, []
+        if last and opt["fin"]:
+            PE("psV1", acc([(reg(7, 2), Rf("CI", k * N, k * N + N), Rf("X", L + k, 2 * L, 16)) for k in range(16)]))
+            S("YO1", act(Rf("YO", 0, N), reg(7, 2), AF.Copy))
         for c in range(2):
             P["c"] = str(c)
             a, d0 = o + c * N, c * L
@@ -420,16 +447,19 @@ def build(opt=None):
             sums = lambda bank, j, nm, g8: [(Rf("ps%d" % bank, N * j + ii, N * j + N, 16), lane(nm, ii), Rf(g8, 0, 8)) for ii in range(16)]
             first = [len(P["tasks"]) + 1]
             j = 0
-            for n in opt["gs"][c]:
+            for n in gs[c]:
                 V("GS", tt(Rf("DS", d0 + N * j, d0 + N * (j + n)), ind(Xa, Rf("SU", a + 8 * j, a + 8 * (j + n))), Rf("Z4", z[1], z[1] + N * n), A.subtract))
                 j += n
-            hh = opt["hh"][c]
+            hh, hs = opt["hh"][c], t == 0 and opt["h0"][c] == "S"
             for j in range(hh):
                 x0, x1 = d0 + L // hh * j, d0 + L // hh * (j + 1)
-                V("H", ts(Rf("HS", x0, x1), Rf("DS", x0, x1), 127.9375, A.add, 128.0, A.min))
+                if hs:
+                    S("H", act(Rf("HF", x0, x1), Rf("DS", x0, x1), AF.Relu, bias=0.0625, scale=-1.0))
+                else:
+                    V("H", ts(Rf("HS", x0, x1), Rf("DS", x0, x1), 127.9375, A.add, 128.0, A.min))
             bw = bk_["w"][c]
             PE2("psW", [(reg(bw, 0), th, M("HI"))] + hist(reg(bw, 0), "I32") + sums(bw, 0, "DS", "GH"), first)
-            PE("psH", acc([(reg(bw, 1), M("CT"), ONE)] + sums(bw, 1, "HS", "GN")))
+            PE("psH", acc([(reg(bw, 1), M("CU" if hs else "CT"), ONE)] + (sums(bw, 1, "HF", "G32") if hs else sums(bw, 1, "HS", "GN"))))
             ni = pc("NI")
             par = (t % 2) * NA + c * N
             r, rho, q = Rf("RR", par, par + N), Rf("RP", par, par + N), Rf("QQ", par, par + N)
@@ -476,18 +506,18 @@ def build(opt=None):
                 V("RP", ts(rho, de, 2047.5, A.is_lt, -0.5, A.add))
                 g1r, n4r = M("G1"), M("N4")
             s16, e16 = Rf("S16", a, a + N), Rf("E16", a, a + N)
-            kb, kj = bk_["k"][c]
-            k0, k1, k2 = reg(kb, kj), reg(kb, kj + 1), reg(*bk_["k2"][c])
+            k0, k1, k2 = reg(*bk_["k"][c]), reg(*bk_["k1"][c]), reg(*bk_["k2"][c])
             i = PE("psK0", acc([(k0, s16, I), (k0, M("G1"), r)]))
             PE2("psK1", [(k1, e16, I), (k1, M("G1H"), ONE), (k1, M("N4"), r), (k1, g1r, rho)], [i])
             wq = opt["w"][c]
             ws = [Rf("WF" if wq[j] == "S" else "WH", (2 * c + j) * N, (2 * c + j + 1) * N) for j in range(2)]
             for j, n in ((0, 2),) if len(wq) == 3 else ((0, 1), (1, 1)):
-                x0 = (2 * c + j) * N
+                x0, kk = (2 * c + j) * N, (k0, k1)[j]
+                kk = Rf(kk[0], kk[1], kk[1] + n * N)
                 if wq[j] == "S":
-                    S("W" + "ab"[j], act(Rf("WF", x0, x0 + n * N), reg(kb, kj + j, n), AF.Relu, bias=-2048.0))
+                    S("W" + "ab"[j], act(Rf("WF", x0, x0 + n * N), kk, AF.Relu, bias=-2048.0))
                 else:
-                    V("W" + "ab"[j], ts(Rf("WH", x0, x0 + n * N), reg(kb, kj + j, n), -4096.0, A.add, -2048.0, A.max))
+                    V("W" + "ab"[j], ts(Rf("WH", x0, x0 + n * N), kk, -4096.0, A.add, -2048.0, A.max))
             top = 2048.0 * (1 + 16 * wq[:2].count("V"))
             rest, nw = (4096.0, "NI32") if wq[0] == "S" else (2048.0, "NIB")
             kept.append((r, rho, q, n4r, s16, e16, ws[0], nw, rest))
@@ -602,11 +632,16 @@ def build(opt=None):
                 V("SE", ts(both("SE", 2), reg(bx, jx, 2 * n), -2048.0, A.add, -2048.0, A.max))
                 PE("psM", [m for j in cs for m in acc([(reg(bm, jm + j - c0), I, one("SE", 2 * j)), (reg(bm, jm + j - c0), I, one("SE", 2 * j + 1)),
                                                       (reg(bm, jm + j - c0), M("NLI"), kept[j][0])])])
-                V("MM", ts(both("MM"), reg(bm, jm, n), 2048.0, A.add, -2048.0, A.max))
+                if opt["mm"] == "V":
+                    mm_, shi = "MM", "SHI"
+                    V("MM", ts(both("MM"), reg(bm, jm, n), 2048.0, A.add, -2048.0, A.max))
+                else:
+                    mm_, shi = "MF", "SH32"
+                    S("MM", act(both("MF"), reg(bm, jm, n), AF.Relu, bias=4096.0))
                 ins, i8 = [], Rf("WI", 24, 16 + N)
                 for j in cs:
                     sn = Rf("ps%d" % bs, (js + j - c0) * N + 8, (js + j - c0 + 1) * N)
-                    ins += acc([(sn, one("SE", 2 * j), i8), (sn, one("SE", 2 * j + 1), i8), (sn, kept[j][6], Rf(kept[j][7], 8, N)), (sn, one("MM", j), Rf("SHI", 8, N))])
+                    ins += acc([(sn, one("SE", 2 * j), i8), (sn, one("SE", 2 * j + 1), i8), (sn, kept[j][6], Rf(kept[j][7], 8, N)), (sn, one(mm_, j), Rf(shi, 8, N))])
                 PE("psS", ins)
                 V("SU", ts(R2("SU", 2 * t + 2 + c0, 2 * t + 3 + c, 8, N), R2("ps%d" % bs, js, js + n, 8, N), rest, A.add))
                 V("S16", ts(Rf("S16", x0, x0 + n * N), Rf("SU", x0, x0 + n * N), -2048.0, A.add))
@@ -619,7 +654,17 @@ def build(opt=None):
                                 it.append((R2(bk, 0, n, 32 * h + 16 * gl, 32 * h + 16 * gl + 16), half(gl, b), R2("S16", 2 * NT + c0, 2 * NT + c + 1, 2 * h + b, N, 8)))
                     PE("psO", acc(it))
                     V("YS", tr(both("YSO"), reg(bk_["o"][c], 0, n)))
-        for c in range(2) if split else (None,):
+        if last and opt["fin"]:
+            y, pa, pb = Rf("Y", o + N, o + NA), reg(6, 2), reg(5, 0)
+            P["c"] = "1"
+            i = PE("psR", acc([(pa, M("OB"), y)]))
+            V("XH", ts(Rf("XH", 0, N), pa, 16392.5, A.add))
+            PE("psI", acc([(pb, M("CV"), ONE), (pb, M("OB"), y)], stop=False), opens="ps5", extra=[i])
+            PE("psI", acc([(pb, M("NIB"), Rf("XH", 0, N))], start=False), closes="ps5")
+            V("XD", tt(Rf("XT", 0, N), ind(Rf("X", L, 2 * L), Rf("PLC", 16 * t + 8, 16 * t + 16)), Rf("XB", o + N, o + NA), A.subtract))
+            V("XP", tt(Rf("YD", 0, N), Rf("XT", 0, N), pb, A.mult))
+            V("YX", tt(Rf("YXO", N, NA), Rf("YO", 0, N), Rf("YD", 0, N), A.subtract))
+        for c in (range(2 - (last and opt["fin"])) if split else (None,)):
             lo, hi = (0, 2) if c is None else (c, c + 1)
             P["c"] = str(hi - 1)
             V("SC", cp(ind(Rf("X", lo * L, hi * L), Rf("PLC", 16 * t + 8 * lo, 16 * t + 8 * hi)), Rf("XN" if opt["xn"][lo] in "IJ" else "XB", o + lo * N, o + hi * N)))
@@ -638,7 +683,7 @@ def build(opt=None):
     V("YP", tt(Rf("YPO", 0, 16), Rf("PW", 96, 112), pa, A.add))
     if fo:
         V("YF", ts(Rf("FB", NT * NA, NT * NA + NA), Rf("F16", NT * NA, NT * NA + NA), -1024.0, A.add))
-    for c in range(2):
+    for c in range(2 - opt["fin"]):
         P["c"] = str(c)
         PE("psV", acc([(reg(c, 0), Rf("CI", k * N, k * N + N), Rf("X", c * L + k, c * L + L, 16)) for k in range(16)]))
         S("YX", act(Rf("YXO", c * N, c * N + N), reg(c, 0), AF.Copy))

from concourse.mybir import dt, AluOpType, ActivationFunctionType

NT, NA, NR = 6, 256, 4096
N = 128
NB = 64
ZW = 8 * N
L = 16 * N

SCRATCH = {}
for _nm, _sh, _ty in (
        ("X", [NR], "bfloat16"), ("PL", [NR], "int32"), ("Z4", [2 * NT, ZW], "bfloat16"), ("Y", [NT * NA], "bfloat16"),
        ("DS", [2 * L], "bfloat16"), ("HS", [2 * L], "float16"), ("DE", [2 * L], "bfloat16"), ("AE", [2 * L], "bfloat16"),
        ("TH", [NA], "int32"), ("S0", [NA], "int32"), ("P0", [16], "int32"), ("FB", [7 * NA], "bfloat16"),
        ("UB", [NT * 16], "bfloat16"), ("UF", [NT * 16], "float32"),
        ("KT", [3 * NA], "float16"), ("TT", [6, N], "float16"), ("THA", [NA], "float16"),
        ("EK", [NT * NA], "float16"), ("ET", [2 * NT, N], "float16"),
        ("S16", [14, N], "float16"), ("SU", [14, N], "uint16"), ("E16", [7 * NA], "float16"), ("EU", [7 * NA], "uint16"),
        ("F16", [7 * NA], "float16"), ("NI", [NA], "int32"), ("RR", [2 * NA], "bfloat16"), ("RP", [2 * NA], "bfloat16"), ("QQ", [2 * NA], "bfloat16"),
        ("WF", [2 * NA], "float32"), ("WH", [2 * NA], "float16"), ("W2", [NA], "float16"), ("MS", [NA], "bfloat16"),
        ("SE", [2 * NA], "float16"), ("MM", [NA], "float16"), ("SW", [2 * NT, N], "bfloat16"),
        ("YD", [NT * NA], "float32"), ("XN", [NT * NA], "int32"),
        ("PI1", [NT * 16], "int32"), ("PI2", [NT * 16], "int32"), ("PI3", [NT * 16], "int32"), ("PLC", [NT * 16], "uint16"),
        ("PH", [NT * 16], "float16"), ("BH", [16], "float16"), ("XT", [NA], "bfloat16"), ("XM", [NA], "float32"), ("XB", [NT * NA], "bfloat16"),
        ("U1", [NT * 16], "int32"), ("U2", [NT * 16], "int32"), ("U3", [NT * 16], "int32"),
        ("U5", [NT * 16], "int32"), ("UH", [NT * 16], "int32"), ("UU", [NT * 16], "uint16"), ("PU", [16], "uint16"),
        ("PT", [NT * 16], "int32"), ("PV", [NT * 16], "int32"), ("PW", [7 * 16], "int32"), ("YPO", [16], "float32"),
        ("YSO", [NA], "float32"), ("YXO", [NA], "float32"),
        ("IOC", [160], "float32"), ("PC", [1], "float32"), ("PI", [1], "int32"), ("IO8", [N], "int32"), ("BASE", [16], "int32"), ("TC", [NT * 16], "int32"),
        ("IOB", [16], "int32"), ("PG", [1], "int32"), ("PK", [1], "int32"), ("PO", [1], "int32"), ("C15F", [1], "float32"), ("PGF", [1], "float32"),
        ("WK", [1], "float32"), ("K16", [1], "float32"), ("ODC", [1], "float32"), ("EVC", [1], "float32"), ("A8", [N], "int32"),
        ("WI", [160], "bfloat16"), ("EVW", [160], "bfloat16"), ("ODW", [160], "bfloat16"), ("BIG", [144], "bfloat16"), ("BIGW", [144], "bfloat16"),
        ("GS", [8], "bfloat16"), ("GN", [8], "bfloat16"), ("GH", [8], "bfloat16"), ("O8", [N], "bfloat16"), ("T4", [N], "bfloat16"),
        ("T1", [N], "bfloat16"), ("T2", [N], "bfloat16"), ("ONE", [NA], "bfloat16"), ("NIB", [N], "bfloat16"), ("HI", [N], "bfloat16"), ("I32", [N], "bfloat16"),
        ("N64", [N], "bfloat16"), ("PQ", [N], "bfloat16"), ("NQ", [N], "bfloat16"), ("NK4", [N], "bfloat16"), ("K4", [N], "bfloat16"), ("Q256", [N], "bfloat16"),
        ("G1", [N], "bfloat16"), ("G1H", [N], "bfloat16"), ("N4", [N], "bfloat16"), ("N2", [N], "bfloat16"), ("SM", [N], "bfloat16"),
        ("NLI", [N], "bfloat16"), ("SHI", [N], "bfloat16"), ("CT", [N], "bfloat16"), ("KS32", [8], "float32"), ("NI32", [N], "float32"),
        ("CI", [L], "bfloat16"), ("MF", [NA], "float32"), ("SH32", [N], "float32"), ("G32", [8], "float32"), ("CU", [N], "bfloat16"),
        ("HF", [2 * L], "float32"), ("IO16", [N], "float32"), ("OB", [N], "bfloat16"), ("CV", [N], "bfloat16"), ("XH", [N], "float16"), ("YO", [N], "float32")):
    SCRATCH[_nm] = ("sbuf", [128] + _sh, _ty)
for _k in range(8):
    SCRATCH["ps%d" % _k] = ("psum", [128, 4, N], "float32")

LOADS = ["lz", "lx", "ls", "lf", "lp", "lpl", "lt"]
STORES = ["ost%d" % k for k in range(4)]
SEMAPHORES = ["cv", "cs", "ct", "cg", "lsent"] + LOADS + STORES + ["za%d%d" % (t, b) for t in range(1, NT) for b in range(4)]

A = AluOpType
AF = ActivationFunctionType
BYTES2 = {k for k, v in SCRATCH.items() if v[2] in ("bfloat16", "float16", "uint16")}
QS = {"V": "cv", "S": "cs", "P": "ct", "G": "cg"}

EST = dict(g=1.55, sc=3.8, v=0.00083, pe=0.00042, vo=0.035, so=0.06, po=0.0, lat=0.13, self_=0.08, net=2.6, lx=7.0, lpl=16.0)
OPT = dict(ep=("SSSS", "SSSS"), ep0=("SVSR", "SRSV"), w=("VS", "VV"), rho="SS", yd="VV", hh=(1, 1), ge=(512, 512), dd=(0, 0), pi=2, yb=2,
           split=(False, True), cut=dict(psW=16, psD=16), xn="SS", cn=((2, 1), (1, 0)), sb=(7, 0))
UP = {}
TURN0 = dict(
    V="ONE WI PG PO ODC EVC EVW ODW PQ A8 O8 N4 N2 T1 KS TT KH TT PK PGF C15 WK BIG BIGW SUs GH HI THA GN CT GS PU U1 SM U2 F160 U5 K16 U3 BASE UH S16s UU BH F16 KS32 NI32 "
      "GS0 GS0 GS0 GS0 H0 GS1 GS1 NI0 GS1 RR0 QQ0 GS1 Wa0 H1 NI1 RR1 QQ1 KE TT EK ET Wa1 EUs GV0 E16s GV0 AV0 GV1 AV1 GV1 SE0 W20 SE1 MM0 LST0 MM1 YD0 SU0 W21 Wb1 S160 "
      "E160 LST1 YD1 EU0 SU1 E161 S161 EU1 PI11 PLC1 SC1",
    S="lt lp lf MS0 MS1 GE0 GE0 AE0 AE0 GE1 AE0 GE1 RP0 AE1 Wb0 AE1 AE1 SW0 Y0 RP1 XM0 XN0 SW1 Y1 XM1 XN1",
    P="psA psA psU psF psW0 psW0 psH0 psK00 psQ0 psW1 psW1 psH1 psA psK01 psQ1 psJ psZ0 psZ0 psD0 psX0 psX1 psZ1 psD0 psK10 psK20 psZ1 psM0 psT0 psM1 psD1 psC0 psS0 psD1 "
      "psK11 psK21 psE0 psN0 psT1 psC1 psS1 psE1 psY1 psN1 psL1",
    G="pc ioc pi io8 iob zx0 zx0 zx1 zx1 SM G1 G1 SM Q256 Q256 NIB NIB G1H G1H NQ NQ NLI SHI NK4 NK4 I32 I32 N64 N64 K4 K4 tc CI CI send0 send1 send1")
LAST = {}
TURN = dict(
    V="-SU1 GS0 -S161 GS0 GS0 U1 GS0 U2 H0 GS1 U5 GS1 U3 NI0 UH UU RR0 EK GS1 ET GS1 F16 W20 Wa0 H1 LST0 YD0 QQ0 PT NI1 RR1 QQ1 Wa1 PV SE0 Wb1 W21 E160 MM0 LST1 YD1 "
      "PI10 EU0 SU0 PLC0 SE1 S160 SC0 E161 EU1 PI11 MM1 PLC1 SC1 YF PW PW PW PW PT PV PW PW YS0 YP",
    S="GE0 GE0 AE0 GE0 AE0 GE0 AE0 GE1 AE0 GE1 AE1 RP0 GE1 Wb0 AE1 GE1 AE1 AE1 Y0 MS0 RP1 SW0 XM0 XN0 MS1 SW1 Y1 XM1 XN1 YX0 YX1",
    P="psD0 psZ0 psU psZ0 psF psZ0 psW0 psW0 psZ0 psH0 psZ1 psW1 psD0 psD1 psZ1 psK00 psK10 psJ psK20 psZ1 psW1 psT0 psZ1 psH1 psQ0 psD1 psK01 psC0 psN0 psX0 psK11 psK21 "
      "psE0 psM0 psQ1 psT1 psY0 psC1 psS0 psL0 psX1 psE1 psY1 psN1 psM1 psL1 psS1 psP psO0 psV0 psV1 -psO1",
    G="zx0 zx0 zx1 zx1 send0 send0 send1 send1")


OPT.update(bk=dict(w=(2, 3), z=(0, 1), k=((5, 0), (5, 2)), k2=((6, 0), (6, 1)), xn=((3, 2), (3, 3)), pu=3, o=(2, 3)), gs=((1, 1, 1, 1), (1, 1, 1, 1)), pi=4, xn="JI", cut=dict(psW=16, psD=16, psK1=1), ep0=("SRSR", "SRVR"))
TURN0 = {'V': 'WI PG A8 PO EVC HI O8 PQ ONE KS N2 KH EVW PK ODC ODW TT WK PGF TT C15 N4 CT BIG K16 GS PU GN BIGW T1 F160 KS32 BASE SUs GH U1 BH THA U2 NI32 U5 SM U3 F16 UH UU S16s GS0 GS0 GS0 GS0 GS1 GS1 H0 GS1 NI0 GS1 RR0 QQ0 H1 Wa0 KE TT NI1 EK RR1 ET EUs Wa1 GV0 QQ1 GV0 AV0 E16s AV0 GV1 GV1 GV1 AV1 W20 AV1 SE0 LST0 YD0 MM0 W21 Wb1 SE1 LST1 YD1 E160 MM1 SU0 EU0 E161 S160 XN0 PI11 XN1 EU1 PLC1 SC1', 'S': 'lt lp lf GE0 GE0 GE1 AE0 AE0 MS0 AE1 RP0 AE1 Wb0 MS1 Y0 RP1 SW1 SW0 Y1 XM0', 'P': 'psA psA psU psF psW0 psW0 psW1 psH0 psW1 psK00 psH1 psA psK01 psJ psZ0 psQ0 psZ0 psD0 psZ1 psD0 psK10 psQ1 psK20 psK10 psX0 psD1 psT0 psD1 psX1 psM0 psK11 psK21 psK11 psC1 psC0 psT1 psE0 psM1 psE1 psS0 psN0 psY1 psN1 psL1 psS1', 'G': 'ioc pi pc io8 iob zx0 zx0 zx1 zx1 SM G1 G1 SM Q256 Q256 NIB NIB G1H G1H NQ NQ NLI SHI NK4 NK4 I32 I32 N64 N64 K4 K4 tc CI CI send0 send1 send1'}
TURN = {'V': '-SU1 -S161 GS0 GS0 GS0 U1 GS0 U2 U5 H0 U3 GS1 UH GS1 UU NI0 EK RR0 ET GS1 GS1 Wa0 W20 H1 F16 QQ0 LST0 YD0 NI1 RR1 QQ1 Wa1 W21 Wb1 SE0 E160 LST1 YD1 MM0 E161 XN0 SE1 SU0 EU0 S160 PI11 XN1 MM1 PLC1 EU1 SC1', 'S': 'GE0 GE0 GE0 AE0 GE0 AE0 GE1 AE0 AE0 GE1 AE1 RP0 GE1 Wb0 AE1 GE1 AE1 AE1 Y0 SW0 MS0 RP1 SW1 MS1 XM0 Y1', 'P': 'psZ0 psD0 psU psZ0 psF psZ0 psW0 psW0 psZ0 psH0 psZ1 psD0 psD1 psW1 psZ1 psK00 psK10 psK10 psJ psK20 psZ1 psW1 psT0 psZ1 psH1 psQ0 psC0 psD1 psK01 psK11 psX0 psK21 psK11 psC1 psN0 psE0 psQ1 psT1 psE1 psM0 psX1 psS0 psY1 psN1 psM1 psL1 psS1', 'G': 'zx0 zx0 zx1 zx1 send0 send0 send1 send1'}
LAST = {'V': '-SU1 GS0 GS0 GS0 -S161 U1 GS0 U2 U5 H0 GS1 U3 UH NI0 UU EK RR0 GS1 ET GS1 GS1 W20 Wa0 H1 LST0 F16 QQ0 YD0 NI1 RR1 QQ1 SE0 W21 Wb1 Wa1 PI10 XN0 LST1 YD1 PLC0 SE1 MM0 SC0 PI11 XN1 PLC1 SC1 PT SU0 S160 PV MM1 PW SU1 PW PT PW PV S161 PW YS0 YF PW PW YP YS1', 'S': 'GE0 GE0 GE0 AE0 GE0 AE0 GE1 AE0 AE0 GE1 AE1 RP0 GE1 Wb0 AE1 GE1 AE1 AE1 MS0 Y0 RP1 XM0 MS1 SW0 Y1 SW1 YX0 YX1', 'P': 'psD0 psZ0 psU psZ0 psF psZ0 psW0 psW0 psZ0 psH0 psZ1 psD0 psD1 psK00 psZ1 psK10 psK10 psJ psK20 psZ1 psW1 psW1 psT0 psZ1 psH1 psQ0 psD1 psK01 psX0 psK11 psN0 psK21 psK11 psC0 psY0 psQ1 psT1 psL0 psX1 psM0 psY1 psN1 psS0 psL1 psM1 psC1 psP psV1 psS1 psO0 psV0 psO1', 'G': 'zx0 zx0 zx1 zx1'}


OPT.update(xn="SS", u="V", f="V", me=0, ms=0, sb=(((7, 0), (7, 1), (7, 3), (7, 0)), ((0, 0), (0, 1), (0, 3), (0, 0))))
EST.update(pe=0.00036, vo=0.062, so=0.08, self_=0.1)
TURN0 = {'V': 'WI PG PGF A8 O8 C15 PO PQ HI PK EVC ONE KS N4 PU ODC K16 WK TT BASE KH EVW ODW N2 BIG F160 BIGW GH GS TT U1 CT KS32 U2 T1 U5 F16 U3 SUs SM UH UU BH GN S16s THA GS1 GS0 GS0 GS0 GS1 GS0 H0 GS1 GS1 NI0 H1 QQ0 RR0 NI32 Wa0 NI1 KE TT QQ1 EK RR1 ET EUs E16s GV0 GV0 AV0 GV1 AV0 GV1 GV1 AV1 W20 AV1 LST0 Wa1 SE0 YD0 W21 MM0 Wb1 SE1 LST1 YD1 E160 MM1 E161 EU0 PI11 EU1 PI21 SU0 PI31 S160 PLC1 SC1', 'S': 'lf lt lp GE0 GE0 GE1 AE0 AE0 MS0 AE1 RP0 Wb0 AE1 RP1 Y0 MS1 SW0 XM0 SW1 Y1 XM1 XN0 XN1', 'P': 'psU psF psA psA psH0 psW0 psW1 psW0 psW1 psK00 psH1 psA psQ0 psJ0 psK01 psZ0 psZ0 psD0 psK10 psZ1 psD0 psX0 psQ1 psK10 psK20 psD1 psT0 psD1 psK11 psJ1 psK11 psK21 psM0 psX1 psC0 psT1 psC1 psN0 psS0 psE0 psM1 psE1 psY1 psN1 psS1', 'G': 'pc pi ioc io8 zx1 iob zx1 SM zx0 zx0 G1 SM Q256 G1 CI NLI Q256 G1H NQ NQ NIB G1H NIB NK4 NK4 I32 I32 N64 CI SHI N64 tc K4 send0 send1 send1 K4'}
TURN = {'V': '-SU1 GS0 GS0 -S161 GS0 U1 GS0 U2 H0 U5 GS1 U3 GS1 UH NI0 UU EK RR0 ET GS1 GS1 QQ0 W20 H1 Wa0 F16 LST0 YD0 NI1 RR1 QQ1 Wa1 SE0 W21 Wb1 LST1 YD1 MM0 E160 SE1 E161 SU0 EU0 S160 PI11 PI21 EU1 PI31 MM1 PLC1 SC1', 'S': 'GE0 GE0 GE0 AE0 GE0 AE0 AE0 GE1 AE0 GE1 AE1 RP0 GE1 Wb0 GE1 AE1 AE1 AE1 Y0 MS0 RP1 SW0 MS1 SW1 XM0 XN0 Y1 XM1 XN1', 'P': 'psD0 psZ0 psU psZ0 psW0 psZ0 psW0 psF psZ0 psH0 psZ1 psW1 psD0 psD1 psZ1 psK00 psK10 psK10 psJ0 psK20 psZ1 psW1 psJ1 psZ1 psT0 psH1 psQ0 psD1 psK01 psX0 psC0 psK21 psK11 psK11 psQ1 psC1 psN0 psT1 psM0 psE0 psX1 psE1 psS0 psY1 psN1 psM1 psS1', 'G': 'zx0 zx0 zx1 zx1 send0 send0 send1 send1'}
LAST = {'V': 'GS0 -SU1 GS0 GS0 GS0 H0 GS1 U1 U2 U5 -S161 U3 NI0 UH QQ0 UU EK RR0 ET GS1 GS1 W20 GS1 H1 Wa0 F16 LST0 YD0 NI1 RR1 QQ1 SE0 W21 Wb1 Wa1 PI10 PI20 LST1 PI30 YD1 PLC0 SE1 PT SC0 PI11 MM0 PI21 PI31 MM1 PLC1 SC1 PV PW SU0 YF S160 PT PW PV SU1 PW PW PW S161 PW YS0 YP YS1', 'S': 'GE0 GE0 GE0 AE0 GE0 AE0 GE1 AE0 AE0 GE1 AE1 RP0 GE1 GE1 AE1 MS0 Wb0 AE1 AE1 SW0 RP1 Y0 MS1 XM0 XN0 Y1 XM1 XN1 SW1 YX1 YX0', 'P': 'psD0 psZ0 psW0 psU psZ0 psZ0 psW0 psZ0 psF psH0 psZ1 psD0 psD1 psZ1 psK00 psJ0 psQ0 psK20 psW1 psK10 psZ1 psJ1 psK10 psZ1 psC0 psW1 psT0 psH1 psD1 psX0 psK01 psK11 psK21 psK11 psY0 psQ1 psN0 psT1 psM0 psX1 psC1 psY1 psN1 psM1 psS1 psP psS0 psV1 psO0 psV0 psO1', 'G': 'zx0 zx0 zx1 zx1'}


OPT.update(w=("SS+", "SS"), pi=3, u="S", gs=((1, 1, 2), (2, 2)), me=1, cn=(None, (7, 2)), ms=1, sb=(None, ((1, 0), (0, 0), (1, 2), (7, 0))))
TURN0 = {'V': 'ONE WI PG A8 O8 N4 PO PGF PK C15 HI KS EVC PU BIG EVW ODC PQ KH GH K16 WK TT ODW N2 BASE TT T1 KS32 GS BIGW CT F160 SUs GN BH THA F16 SM S16s GS0 GS0 GS1 GS0 GS1 H0 H1 NI32 U3 NI0 UH QQ0 UU RR0 NI1 KE TT EK QQ1 RR1 EUs ET GV0 GV1 GV0 AV0 AV0 E16s GV1 GV1 AV1 W20 AV1 LST0 YD0 W21 SE1 LST1 YD1 E161 EU1 PI11 MM1 PLC1 SC1', 'S': 'lp lf lt U1 U2 GE0 GE0 GE1 AE0 AE0 AE1 RP0 AE1 Wa0 MS1 Wa1 RP1 Y0 Wb1 SW1 XM0 Y1 XM1 XN1 XN0', 'P': 'psA psA psU psG psG psF psW0 psW0 psW1 psW1 psH0 psH1 psA psZ0 psJ0 psZ0 psD0 psZ1 psK00 psD0 psQ1 psK01 psK10 psK10 psK20 psD1 psT0 psD1 psJ1 psK11 psK11 psK21 psX1 psT1 psC1 psN0 psM1 psE1 psN1 psY1 psL1 psL1 psS1', 'G': 'pc ioc pi io8 iob NIB NIB zx0 zx0 SM zx1 zx1 zx0 zx1 G1 G1 SM Q256 Q256 G1H G1H NQ NQ NLI SHI NK4 NK4 I32 I32 N64 N64 K4 K4 tc CI CI send0 send1 send1'}
TURN = {'V': '-SU1 GS0 GS0 GS0 H0 GS1 U3 NI0 UH RR0 -S161 UU EK ET GS1 W20 F16 H1 QQ0 LST0 YD0 NI1 RR1 QQ1 W21 LST1 YD1 SE1 E161 EU1 PI11 MM1 PLC1 SC1', 'S': 'GE0 GE0 GE0 GE0 AE0 AE0 U1 GE1 AE0 U2 AE0 GE1 AE1 GE1 RP0 GE1 AE1 Wa0 AE1 AE1 Y0 RP1 Wa1 Wb1 MS1 XM0 SW1 Y1 XM1 XN0 XN1', 'P': 'psZ0 psD0 psU psW0 psZ0 psG psZ0 psW0 psZ0 psF psG psH0 psZ1 psD0 psK00 psK10 psZ1 psD1 psJ0 psZ1 psK10 psK20 psW1 psW1 psJ1 psZ1 psT0 psH1 psD1 psK01 psK11 psK11 psK21 psC1 psQ1 psN0 psT1 psX1 psE1 psY1 psN1 psM1 psL1 psL1 psS1', 'G': 'zx0 zx0 zx0 zx1 zx1 zx1 send0 send0 send1 send1'}
LAST = {'V': '-SU1 GS0 GS0 GS0 H0 GS1 U3 PT UH -S161 UU NI0 EK RR0 ET GS1 H1 W20 QQ0 F16 NI1 QQ1 RR1 LST0 YD0 W21 LST1 YD1 PI10 SE1 PLC0 PT SC0 PI11 PV MM1 PV PLC1 PW SC1 PW PW SU1 S161 PW YF PW PW YS1 YP', 'S': 'GE0 GE0 GE0 AE0 U1 AE0 GE0 GE1 AE0 U2 AE0 GE1 RP0 GE1 AE1 GE1 AE1 Wa0 AE1 AE1 RP1 Y0 Wb1 Wa1 MS1 XM0 Y1 XN0 SW1 XM1 XN1 YX1 YX0', 'P': 'psZ0 psZ0 psU psD0 psW0 psW0 psG psG psZ0 psZ0 psF psH0 psZ1 psD0 psZ1 psK00 psK10 psJ0 psK20 psD1 psZ1 psW1 psK10 psW1 psZ1 psH1 psJ1 psT0 psD1 psQ1 psK01 psK11 psK11 psK21 psY0 psN0 psT1 psC1 psX1 psL0 psL0 psY1 psN1 psM1 psL1 psL1 psV0 psS1 psV1 psO1 psP', 'G': 'zx0 zx0 zx0 zx1 zx1 zx1'}


OPT.update(ep0=("SSSR", "SSSR"), mc=0, gs=((4, 4, 8), (8, 8)))
EST.update(lx=4.5, lpl=9.5)
TURN0 = {'V': 'ONE PG C15 PK BIG PO WK WI ODC A8 BIGW PQ ODW CT EVC O8 KS KH EVW N4 TT PU U3 PGF TT N2 GH SUs HI S16s THA T1 GN GS0 GS0 GS0 GS1 H0 KE TT UH GS NI0 EUs GS1 RR0 GV0 F160 UU H1 EK ET AV0 NI1 SM KS32 GV1 RR1 E16s NI32 K16 AV1 QQ0 W20 F16 QQ1 LST0 YD0 W21 SE1 LST1 YD1 BASE BH MM1 E161 PI11 EU1 PLC1 SC1', 'S': 'lt lp U1 U2 lf GE1 GE0 GE0 GE0 AE0 AE0 GE1 AE0 GE1 RP0 AE1 AE1 Wa0 AE1 RP1 MS1 Y0 Wa1 Wb1 SW1 XM0 Y1 XM1 XN0 XN1', 'P': 'psU psG psG psA psA psH0 psA psW0 psW0 psW1 psW1 psZ0 psD0 psZ0 psH1 psZ0 psJ0 psZ1 psK00 psF psD0 psZ1 psD1 psK10 psK10 psK01 psK20 psZ1 psJ1 psT0 psK11 psD1 psQ1 psK11 psK21 psX1 psC1 psN0 psT1 psE1 psM1 psN1 psY1 psL1 psL1 psS1', 'G': 'pi ioc pc NIB io8 NIB iob zx1 Q256 zx0 G1 zx0 zx1 G1 zx0 zx1 Q256 NQ NQ SHI NK4 G1H NK4 SM NLI G1H I32 I32 N64 N64 CI K4 SM CI tc send0 K4 send1 send1'}


OPT.update(ep0=("SSSR", "SSRR"), mm="V", h0="VV", fin=0)
TURN0 = {'V': 'PG ONE PO ODC EVC WI PK C15 BIG WK PGF KS A8 TT G8 KH TT O8 SUs PU F160 S16s THA GS0 GS0 U3 GS0 GS1 UH H0 KE TT GS1 EUs UU H1 EK NI0 K16 ET GV0 SM AV0 E16s RR0 NI1 F16 RR1 GV1 QQ0 GV1 QQ1 AV1 W20 BH AV1 LST0 YD0 W21 SE1 LST1 YD1 MM1 E161 PI11 EU1 PLC1 SC1', 'S': 'lp lt lf EVW NIB CT PQ ODW BIGW N2 U1 GH U2 NK4 T1 N4 HI GN K4 N64 NQ I32 NI32 Q256 KS32 ' + 'CI ' * 16 + 'GE0 GE0 GE0 AE0 AE0 GE1 AE0 GE1 RP0 AE1 Wa0 AE1 MS1 RP1 Y0 Wb1 Wa1 SW1 Y1 XM1 XM0 XN1 XN0', 'P': 'psA psA psU psG psG psH0 psA psW0 psW0 psF psW1 psW1 psZ0 psH1 psZ0 psZ0 psJ0 psK00 psD0 psZ1 psD0 psK01 psK10 psZ1 psK10 psK20 psD1 psQ1 psT0 psK11 psD1 psJ1 psK11 psK21 psX1 psC1 psT1 psN0 psE1 psM1 psN1 psY1 psL1 psL1 psS1', 'G': 'pi pc iob ioc io8 zx0 zx0 zx0 zx1 zx1 G1 zx1 tc G1 G1H G1H SM NLI SHI SM CI CI send0 send1 send1'}


OPT.update(h0="SS", fin=1, ms=0, sb=(((2, 0), (0, 1), (0, 3), (0, 0)), ((3, 0), (7, 0), (7, 2), (7, 0))), cn=(None, (1, 0)), w=("VV+", "SS"),
           bk=dict(OPT["bk"], k1=((5, 1), (5, 3)), k2=((6, 0), (7, 0))), gs=((2, 2, 4, 8), (8, 8)), gs0=((4, 4, 4, 4), (4, 4, 4, 4)), ep0=("SSRR", "SSSR"))
TURN0 = {'V': 'ONE PG C15 PO PGF WI BIG EVC PK G8 ODC WK KS TT KH TT A8 SUs O8 S16s F160 PU THA GS0 GS0 GS0 GS0 GS1 GS1 GS1 GS1 U3 KE TT UH UU NI0 SM EUs GV0 EK ET GV0 AV0 QQ0 AV0 RR0 NI1 E16s GV1 RR1 AV1 Wa0 F16 W20 QQ1 K16 LST0 YD0 BH SE0 W21 OB MM0 LST1 YD1 E161 SE1 EU1 SU0 PI11 PLC1 SC1 S160', 'S': 'lt lf lp HI EVW ODW PQ GH BIGW G32 NIB NQ T1 CU U1 N2 GN Q256 CI N4 U2 CI NI32 CI CT CI CI CI N64 KS32 NK4 K4 H0 CV CI CI CI I32 H1 GE0 GE0 GE1 AE0 AE0 GE1 AE1 RP0 GE1 AE1 AE1 MS0 CI Wa1 RP1 Y0 Wb1 CI SW1 XM0 MS1 Y1 XN0 CI XM1 XN1 CI CI CI CI', 'P': 'psA psA psU psG psG psW0 psW1 psW0 psF psH0 psW1 psA psH1 psZ0 psZ0 psD0 psJ0 psZ1 psK00 psD0 psK10 psZ1 psK20 psK10 psQ0 psK01 psZ1 psJ1 psT0 psD1 psD1 psX0 psK11 psQ1 psK11 psK21 psC1 psN0 psM0 psT1 psE1 psS0 psX1 psN1 psY1 psL1 psL1 psM1', 'G': 'pc pi ioc io8 iob zx0 zx1 zx0 zx1 NLI SM G1 G1 io16 G1H G1H SHI tc SM send0 send1 send1'}
TURN = {'V': '-MM1 GS0 GS0 GS0 GS0 U3 H0 -SU1 UH GS1 NI0 UU RR0 EK QQ0 ET GS1 W20 Wa0 H1 F16 LST0 YD0 NI1 -S161 RR1 QQ1 SE0 W21 MM0 LST1 YD1 SU0 E161 SE1 PI11 EU1 S160 PLC1 SC1', 'S': 'GE0 GE0 AE0 U1 GE0 U2 GE0 AE0 GE1 AE0 AE0 GE1 AE1 RP0 GE1 GE1 AE1 AE1 AE1 MS0 Y0 RP1 Wb1 Wa1 SW1 XM0 MS1 Y1 XM1 XN0 XN1', 'P': 'psZ0 psU psG psF psG psW0 psZ0 psZ0 -psS1 psD0 psW0 psZ0 psH0 psZ1 psD0 psK00 psK10 psZ1 psJ0 psK20 psK10 psJ1 psZ1 psW1 psW1 psZ1 psT0 psH1 psQ0 psD1 psD1 psX0 psK01 psK11 psK11 psK21 psC1 psN0 psQ1 psM0 psT1 psS0 psX1 psE1 psN1 psY1 psL1 psL1 psM1', 'G': 'zx0 zx0 zx0 zx1 zx1 zx1 send0 send0 send1 send1'}
LAST = {'V': '-MM1 GS0 GS0 GS0 GS0 H0 -SU1 U3 UH GS1 NI0 UU RR0 EK -S161 QQ0 ET GS1 W20 Wa0 H1 F16 LST0 YD0 NI1 RR1 SE0 W21 QQ1 PI10 MM0 LST1 PT YD1 SU0 PV PLC0 SE1 S160 PW PI11 SC0 PT MM1 XH1 PLC1 YF PW XD1 YS0 PW SU1 PV S161 PW XP1 PW YX1 PW YS1 YP', 'S': 'GE0 GE0 GE0 GE0 U1 AE0 U2 AE0 GE1 AE0 AE0 GE1 GE1 RP0 AE1 GE1 AE1 AE1 AE1 MS0 YO1 Y0 RP1 Wa1 Wb1 MS1 Y1 XM0 XN0 XM1 XN1 SW1 YX0', 'P': '-psS1 psD0 psZ0 psU psG psZ0 psG psF psW0 psW0 psZ0 psZ0 psH0 psV1 psZ1 psD0 psK00 psD1 psZ1 psJ0 psK10 psK10 psK20 psJ1 psW1 psZ1 psQ0 psT0 psZ1 psW1 psH1 psD1 psX0 psK01 psK11 psK11 psK21 psY0 psM0 psT1 psQ1 psN0 psS0 psL0 psL0 psX1 psY1 psR1 psN1 psL1 psL1 psM1 psC1 psI1 psO0 psI1 psS1 psV0 psO1 psP', 'G': 'zx0 zx0 zx0 zx1 zx1 zx1'}


OPT.update(bk=dict(OPT["bk"], k=((5, 0), (6, 1))), w=("VV+", "VS"), h0="SV", ep0=("SSSR", "SSRR"))
TURN0 = {'V': 'PG PK PGF ONE PO G8 WI ODC A8 WK C15 EVC BIG KS TT KH O8 TT SUs S16s F160 THA GS0 GS0 F16 GS0 U3 PU GS0 GS1 SM GS1 UH KE UU TT GS1 EUs GS1 EK H1 GV0 NI0 E16s RR0 ET QQ0 K16 AV0 NI1 GV1 GV1 AV1 AV1 W20 Wa0 QQ1 RR1 LST0 BH YD0 Wa1 SE0 W21 MM0 LST1 YD1 OB SU0 E161 SE1 PI11 S160 EU1 PLC1 SC1', 'S': 'lf lt lp PQ ODW HI CI EVW N2 NIB NQ G32 T1 CI CU N4 BIGW U1 U2 KS32 CI GN Q256 GH CT NI32 CV CI K4 CI H0 CI CI CI NK4 I32 N64 CI CI GE0 GE0 GE0 AE0 GE1 AE0 AE0 GE1 RP0 AE1 AE1 MS0 RP1 Y0 Wb1 CI CI SW1 MS1 Y1 CI XM0 XM1 XN1 XN0 CI CI CI', 'P': 'psA psA psU psF psG psG psW0 psW0 psW1 psA psH0 psZ0 psW1 psH1 psZ0 psZ0 psK00 psJ0 psQ0 psD0 psZ1 psD0 psK10 psZ1 psK10 psK20 psJ1 psD1 psT0 psD1 psK01 psX0 psK11 psK11 psK21 psC1 psM0 psT1 psN0 psQ1 psS0 psE1 psX1 psN1 psY1 psL1 psL1 psM1', 'G': 'pi ioc pc iob io8 zx0 zx1 zx0 G1 zx1 SHI SM SM G1 NLI tc G1H G1H io16 send0 send1 send1'}
TURN = {'V': '-MM1 GS0 GS0 GS0 GS0 H0 U3 -SU1 UH GS1 NI0 UU RR0 EK QQ0 ET GS1 W20 Wa0 H1 F16 LST0 -S161 YD0 NI1 RR1 QQ1 SE0 Wa1 W21 MM0 LST1 YD1 SE1 SU0 E161 PI11 S160 EU1 PLC1 SC1', 'S': 'GE0 GE0 GE0 AE0 U1 GE0 U2 AE0 GE1 AE0 AE0 GE1 AE1 RP0 GE1 AE1 GE1 AE1 AE1 MS0 Y0 RP1 Wb1 SW1 MS1 XM0 Y1 XN0 XM1 XN1', 'P': 'psZ0 psU psF psG psW0 psG psZ0 psZ0 -psS1 psD0 psW0 psZ0 psH0 psZ1 psD0 psK00 psK10 psZ1 psJ0 psK20 psK10 psJ1 psZ1 psW1 psD1 psW1 psZ1 psT0 psH1 psQ0 psD1 psX0 psK01 psK11 psK11 psK21 psC1 psM0 psN0 psT1 psQ1 psS0 psX1 psE1 psN1 psY1 psL1 psL1 psM1', 'G': 'zx0 zx0 zx0 zx1 zx1 zx1 send0 send0 send1 send1'}
LAST = {'V': '-MM1 GS0 GS0 GS0 -SU1 GS0 -S161 H0 U3 GS1 UH NI0 UU RR0 EK QQ0 ET GS1 Wa0 W20 H1 LST0 F16 YD0 NI1 RR1 QQ1 SE0 Wa1 W21 PT PI10 MM0 LST1 PV YD1 PT PW SU0 PLC0 SE1 S160 PI11 SC0 MM1 XH1 PLC1 PW PW SU1 PW S161 PV XD1 PW XP1 PW YF YP YS0 YX1 YS1', 'S': 'GE0 GE0 GE0 AE0 U1 GE0 AE0 U2 GE1 AE0 AE0 GE1 GE1 RP0 AE1 GE1 AE1 MS0 AE1 AE1 Y0 RP1 Wb1 YO1 MS1 Y1 XM0 XN0 XM1 XN1 SW1 YX0', 'P': '-psS1 psD0 psZ0 psZ0 psU psG psZ0 psW0 psW0 psG psF psZ0 psH0 psV1 psZ1 psD0 psD1 psK00 psZ1 psJ0 psK10 psQ0 psK10 psK20 psZ1 psW1 psJ1 psT0 psZ1 psW1 psH1 psD1 psX0 psK01 psK11 psK21 psK11 psY0 psM0 psT1 psQ1 psL0 psN0 psS0 psL0 psX1 psY1 psL1 psM1 psR1 psN1 psL1 psC1 psI1 psS1 psV0 psI1 psP psO0 psO1', 'G': 'zx0 zx0 zx0 zx1 zx1 zx1'}


def Rf(buf, lo, hi, st=1):
    return (buf, lo, hi, st)


def R2(buf, o0, o1, lo, hi, st=1):
    return (buf, lo, hi, st, o0, o1)


def spans(r):
    if len(r) == 4:
        return [r[1:4]]
    w = SCRATCH[r[0]][1][2]
    return [(o * w + r[1], o * w + r[2], r[3]) for o in range(r[4], r[5])]


def cnt(r):
    return sum((hi - lo + st - 1) // st for lo, hi, st in spans(r))


def isref(x):
    return isinstance(x, tuple)


def ind(win, off):
    return ("#", win, off)


def duration(q, ins, e):
    d = 0.0
    for m, kw in ins:
        if m == "matmul":
            d += e["po"] + max(min(64, cnt(kw["lhsT"])), cnt(kw["rhs"])) * e["pe"] * (1 if kw["rhs"][0] in BYTES2 else 4)
            continue
        if m == "iota":
            d += 0.13 + 2 * cnt(kw["out"]) * e["v"]
            continue
        if m == "affine":
            d += 0.17 + 2 * cnt(kw["in_"]) * e["v"]
            continue
        refs = [v for v in kw.values() if isref(v)]
        gat = [k for k, v in kw.items() if isref(v) and v[0] == "#"]
        if gat:
            n = 16 * cnt(kw[gat[0]][2])
            d += 0.06 + n * e["v"] * (e["sc"] if gat[0] == "out" else e["g"])
        elif q == "S":
            d += e["so"] + cnt(kw["out"]) * e["v"]
        else:
            n = cnt(kw.get("out", kw.get("ap")))
            c = 1.0
            if m != "tensor_tensor" and all(v[0] in BYTES2 for v in refs if cnt(v) == n):
                c = 0.5
            if m == "tensor_tensor" and not any(v[0][:2] == "ps" for v in refs):
                c = 2.0
            d += e["vo"] + max(64, n * c) * e["v"]
    return d


def touches(ins):
    rd, wr = [], []
    for m, kw in ins:
        for k, v in kw.items():
            if not isref(v) or k == "src":
                continue
            if v[0] == "#":
                (wr if k == "out" else rd).append(v[1])
                rd.append(v[2])
            elif k in ("out", "ap"):
                wr.append(v)
                if m == "matmul" and not kw["start"]:
                    rd.append(v)
            else:
                rd.append(v)
    return rd, wr


def meet(a, b):
    if not (a[0] < b[1] and b[0] < a[1]):
        return False
    return not (a[2] == b[2] and a[2] > 1 and (a[0] - b[0]) % a[2])


def add(P, q, name, ins, wr=None, dur=None, sem=None, inc=1, extra=None, prio=0.0):
    r, w = touches(ins)
    w += wr or []
    T = {"i": len(P["tasks"]), "q": q, "name": name, "ins": ins, "sem": sem, "inc": inc, "prio": prio,
         "fix": dur, "pre": {}, "banks": [], "label": name + P.get("c", ""), "t": P.get("t", 0)}
    hist = P["last"]
    seen = {}
    for a, lst in (("r", r), ("w", w)):
        for ref in lst:
            for sp in spans(ref):
                seen.setdefault((ref[0],) + tuple(sp), set()).add(a)
    for (buf, lo, hi, st), accs in seen.items():
        if buf[:2] == "ps" and buf not in T["banks"]:
            T["banks"].append(buf)
        for (o, oa, oset) in hist.get(buf, ()):
            if ("w" in accs or "w" in oa) and meet((lo, hi, st), oset):
                T["pre"][o] = "raw"
    for (buf, lo, hi, st), accs in seen.items():
        h = hist.setdefault(buf, [])
        if "w" in accs and st == 1:
            h[:] = [e for e in h if not (lo <= e[2][0] and e[2][1] <= hi)]
    for (buf, lo, hi, st), accs in seen.items():
        hist[buf].append((T["i"], accs, (lo, hi, st)))
    for o in extra or []:
        T["pre"].setdefault(o, "time")
    P["tasks"].append(T)
    return T["i"]


def acc(items, start=True, stop=True):
    k = len(items)
    return [("matmul", dict(out=x[0], lhsT=x[1], rhs=x[2], start=start and i == 0, stop=stop and i == k - 1, part=(x + ([0, 128],))[3]))
            for i, x in enumerate(items)]


def ts(out, in0, s1, op0, s2=None, op1=None):
    kw = dict(out=out, in0=in0, scalar1=s1, scalar2=s2, op0=op0)
    if op1 is not None:
        kw["op1"] = op1
    return [("tensor_scalar", kw)]


def tt(out, in0, in1, op):
    return [("tensor_tensor", dict(out=out, in0=in0, in1=in1, op=op))]


def cp(out, in_):
    return [("tensor_copy", dict(out=out, in_=in_))]


def act(out, in_, f, bias=0.0, scale=1.0):
    return [("activation", dict(out=out, in_=in_, func=f, bias=bias, scale=scale))]


def tr(out, in_):
    return [("vtranspose", dict(out=out, in_=in_))]


def M(name):
    return Rf(name, 0, N)


def sel(m, name="BIG"):
    return Rf(name, 15 - m, 143 - m)


def half(frm, to):
    o = 16 - 16 * (to - frm)
    return Rf("ODW" if frm else "EVW", o, o + N)


def reg(bank, j, n=1):
    return Rf("ps%d" % bank, N * j, N * (j + n))


def build(opt=None):
    opt = opt or OPT
    P = {"tasks": [], "last": {}}
    c1 = lambda n: Rf(n, 0, 1)
    V = lambda nm, ins, **k: add(P, "V", nm, ins, **k)
    S = lambda nm, ins, **k: add(P, "S", nm, ins, **k)
    G = lambda nm, ins, **k: add(P, "G", nm, ins, **k)

    def PE(nm, ins, opens=None, closes=None, inside=None, **k):
        i = add(P, "P", nm, ins, **k)
        if inside:
            opens = closes = inside
        if opens:
            P["tasks"][i]["opens"] = opens
        if closes:
            P["tasks"][i]["closes"] = closes
        return i

    def PE2(nm, items, after):
        k = opt["cut"].get(nm)
        if not k:
            return PE(nm, acc(items))
        PE(nm, acc(items[:-k], stop=False), opens=items[0][0][0], extra=after)
        return PE(nm, acc(items[-k:], start=False), closes=items[0][0][0])

    def load(q, sem, ref, dur, src):
        return add(P, q, sem, [("dma", dict(out=ref, src=src))], dur=0.1, sem=sem, inc=16, prio=dur)
    load("Y", "ls", Rf("S0", 0, NA), 2.2, ("s0", 0, NA))
    load("Y", "lz", R2("Z4", 0, 2, 0, N), 2.2, ("z0", 0, NA))
    load("Y", "lx", Rf("X", 0, NR), EST["lx"], ("x0", 0, NR))
    load("S", "lt", Rf("TH", 0, NA), 2.5, ("th", 0, NA))
    load("S", "lp", Rf("P0", 0, 16), 2.5, ("p0", 0, 16))
    load("S", "lf", Rf("FB", 0, NA), 2.5, ("f0", 0, NA))
    load("Y", "lpl", Rf("PL", 0, NR), EST["lpl"], ("pl", 0, NR))
    io = lambda nm, ref, pat, ch, base=0: G(nm, [("iota", dict(out=ref, pattern=pat, base=base, channel_multiplier=ch))])
    io("pc", c1("PC"), [[1, 1]], 1)
    io("ioc", Rf("IOC", 0, 160), [[1, 160]], 0)
    io("pi", c1("PI"), [[1, 1]], 1)
    io("io8", M("IO8"), [[1, N]], -1, N)
    io("iob", Rf("IOB", 0, 16), [[256, 16]], 0)
    io("tc", Rf("TC", 0, NT * 16), [[4096, NT], [0, 16]], 0, 4096)
    I = Rf("WI", 16, 16 + N)
    ONE = M("ONE")
    V("WI", ts(Rf("WI", 0, 160), Rf("IOC", 0, 160), -16.0, A.add, c1("PC"), A.is_equal))
    V("PG", ts(c1("PG"), c1("PI"), 4, A.arith_shift_right))
    V("PK", ts(c1("PK"), c1("PI"), 15, A.bitwise_and))
    V("PO", ts(c1("PO"), c1("PG"), 1, A.bitwise_and))
    V("ODC", ts(c1("ODC"), c1("PO"), 1.0, A.mult))
    V("EVC", ts(c1("EVC"), c1("PO"), 0.0, A.is_equal))
    times = lambda nm, out, in_, k, b=0.0: S(nm, act(out, in_, AF.Identity, bias=b, scale=k))
    times("EVW", Rf("EVW", 0, 160), Rf("WI", 0, 160), c1("EVC"))
    times("ODW", Rf("ODW", 0, 160), Rf("WI", 0, 160), c1("ODC"))
    V("PGF", ts(c1("PGF"), c1("PG"), 1.0, A.mult))
    V("C15", ts(c1("C15F"), c1("PG"), 16.0, A.mult, 15.0, A.add))
    V("WK", ts(c1("WK"), c1("PK"), 2.0, A.mult, 1.0, A.add))
    V("K16", ts(c1("K16"), c1("PK"), 16.0, A.mult))
    if opt["pi"] == 4:
        V("BASE", ts(Rf("BASE", 0, 16), Rf("IOB", 0, 16), c1("K16"), A.add))
    V("BIG", ts(Rf("BIG", 0, 144), Rf("IOC", 0, 144), c1("C15F"), A.is_equal))
    times("BIGW", Rf("BIGW", 0, 144), Rf("BIG", 0, 144), c1("WK"))
    V("G8", ts(Rf("GS", 0, 8), Rf("IOC", 0, 8), c1("PGF"), A.is_equal))
    times("GN", Rf("GN", 0, 8), Rf("GS", 0, 8), -1.0)
    times("GH", Rf("GH", 0, 8), Rf("GS", 0, 8), -0.5)
    V("ONE", [("memset", dict(ap=Rf("ONE", 0, NA), constant=1.0))])
    V("A8", ts(M("A8"), M("IO8"), 7, A.bitwise_and))
    V("O8", ts(M("O8"), M("A8"), 0.0, A.is_equal))
    for nm, k in (("PQ", 2048.0), ("NIB", -1.0), ("HI", 0.5), ("Q256", 256.0), ("NQ", -2048.0), ("NK4", -4096.0), ("I32", 32.0), ("N64", -64.0), ("K4", 4096.0)):
        times(nm, M(nm), I, k)
    times("CT", M("CT"), I, -0.6875, 8.0)
    for nm, k in (("N4", -4096.0), ("N2", -2048.0), ("T1", 17.0)):
        times(nm, M(nm), M("O8"), k)
    V("BH", ts(Rf("BH", 0, 16), Rf("IOB", 0, 16), c1("K16"), A.add, 16400.0, A.add))
    cut = lambda nm, out, in_, op, fill, k=1: G(nm, [("affine", dict(out=out, in_=in_, op=op, fill=fill, pattern=[[0, k], [1, N]]))])
    cut("G1", M("T2"), M("N4"), A.is_gt, 0.0)
    cut("G1", M("G1"), M("T2"), A.not_equal, 4096.0)
    cut("SM", M("T4"), M("T1"), A.is_gt, 0.0)
    V("SM", tt(M("T1"), M("T4"), M("O8"), A.max))
    cut("SM", M("SM"), M("T1"), A.not_equal, -16.0)
    cut("G1H", M("T2"), M("N2"), A.is_gt, 0.0)
    cut("G1H", M("G1H"), M("T2"), A.not_equal, 2048.0)
    cut("NLI", M("NLI"), M("N4"), A.is_ge, 0.0)
    cut("SHI", M("SHI"), Rf("WI", 8, 8 + N), A.not_equal, -1.0)
    if opt["fin"]:
        io("io16", M("IO16"), [[1, 8], [0, 16]], 0)
        V("OB", ts(M("OB"), M("IO16"), c1("PGF"), A.is_equal))
        times("CV", M("CV"), I, 17.0, 128.0)
    if opt["mm"] == "S":
        times("SH32", M("SH32"), M("SHI"), 1.0)
    if "S" in opt["h0"]:
        times("G32", Rf("G32", 0, 8), Rf("GS", 0, 8), 1.0)
        times("CU", M("CU"), I, -0.6875, -8.0)
    for k in range(16):
        times("CI", Rf("CI", k * N, k * N + N), I, k + 1.0)
    if "S" in "".join(opt["w"]):
        times("KS32", Rf("KS32", 0, 8), Rf("O8", 0, 8), 1.0)
        times("NI32", M("NI32"), I, -1.0)

    def turned(j, bank):
        V("TT", tr(Rf("TT", j * NA, j * NA + NA), Rf("KT", j * NA, j * NA + NA)))
        it = [(reg(bank, 0, 2), M("PQ"), Rf("ONE", 0, NA))]
        for h in range(4):
            for b in range(2):
                for gl in range(2):
                    x0 = 32 * h + 16 * gl
                    it.append((R2("ps%d" % bank, 0, 2, 2 * h + b, N, 8), half(b, gl), R2("TT", 2 * j, 2 * j + 2, x0, x0 + 16)))
        PE("psA", acc(it))
        return reg(bank, 0, 2)
    V("KS", ts(Rf("KT", 0, NA), Rf("S0", 0, NA), -2048.0, A.add))
    V("SUs", cp(Rf("SU", 0, NA), turned(0, 7)))
    V("S16s", ts(Rf("S16", 0, NA), Rf("SU", 0, NA), -2048.0, A.add))
    V("KH", ts(Rf("KT", NA, 2 * NA), Rf("TH", 0, NA), -2048.0, A.add))
    V("THA", ts(Rf("THA", 0, NA), turned(1, 5), -2048.0, A.add))
    fb, fo = ("F16", 1024.0) if opt["f"] == "V" else ("FB", 0.0)
    if fo:
        V("F160", ts(Rf("F16", 0, NA), Rf("FB", 0, NA), 1024.0, A.add))
    V("PU", cp(Rf("PU", 0, 16), Rf("P0", 0, 16)))
    V("KE", ts(Rf("KT", 2 * NA, 3 * NA), ind(Rf("PL", 0, NR), Rf("PU", 0, 16)), -2048.0, A.add))
    V("EUs", cp(Rf("EU", 0, NA), turned(2, 1)))
    V("E16s", ts(Rf("E16", 0, NA), Rf("EU", 0, NA), -2048.0, A.add))
    Xa = Rf("X", 0, NR)
    KS = Rf("O8", 0, 8)
    shut = None
    bk_ = opt["bk"]
    for t in range(NT):
        last = t == NT - 1
        o = t * NA
        U = lambda nm: Rf(nm, t * 16, t * 16 + 16)
        zb = R2("Z4", 2 * t, 2 * t + 2, 0, N)
        split = opt["split"][last]
        gs = opt["gs"] if t else opt.get("gs0", opt["gs"])
        P["t"] = t
        for c in range(2):
            P["c"] = str(c)
            z0 = (2 * t + c) * ZW
            for n in (1, 2, 4)[:2 + (max(gs[c]) > 4)]:
                G("zx", [("affine", dict(out=Rf("Z4", z0 + n * N, z0 + 2 * n * N), in_=Rf("Z4", z0, z0 + n * N)))])
        P["c"] = ""
        PE("psF", acc([(reg(2, 2, 2), I, Rf(fb, o, o + NA)), (reg(2, 2, 2), I, zb)]))
        if opt["f"] == "V":
            V("F16", ts(Rf("F16", o + NA, o + 2 * NA), reg(2, 2, 2), 0.5, A.mult, 511.75, A.add))
        else:
            S("FM", act(Rf("FM", 0, NA), reg(2, 2, 2), AF.Identity, bias=12582912.0, scale=0.4995))
            S("F16", act(Rf("FB", o + NA, o + 2 * NA), Rf("FM", 0, NA), AF.Identity, bias=-12582912.0))
        pu = Rf("ps%d" % bk_["pu"], 2 * N, 2 * N + 16)
        it = [(pu, sel(m, "BIGW"), R2("Z4", 2 * t, 2 * t + 2, m, N, 16)) for m in range(16)]
        i = PE("psU", acc(it))
        if opt["u"] == "V":
            V("U1", cp(U("U1"), pu))
            V("U2", ts(U("U2"), U("U1"), 4095, A.bitwise_and))
            V("U5", ts(U("U5"), U("U2"), 1184.0, A.add))
            V("U3", tt(U("U3"), U("U2"), U("U5"), A.mult))
        else:
            pz = Rf("ps7", 3 * N, 3 * N + 16)
            S("U1", act(U("UB"), pu, AF.Identity, bias=786432.0 - 2047.5))
            PE("psG", acc([(pz,) + x[1:] for x in it], stop=False), opens="ps7", extra=[i])
            PE("psG", acc([(pz, M("NIB"), U("UB"))], start=False), closes="ps7")
            S("U2", act(U("UF"), pz, AF.Square, bias=786432.0 + 592))
            V("U3", ts(U("U3"), U("UF"), -350464.0, A.add))
        V("UH", ts(U("UH"), U("U3"), 5, A.arith_shift_right, 4095, A.bitwise_and))
        V("UU", cp(U("UU"), U("UH")))
        V("EK", ts(Rf("EK", o, o + NA), ind(Rf("PL", 0, NR), U("UU")), -2048.0, A.add))
        V("ET", tr(Rf("ET", o, o + NA), Rf("EK", o, o + NA)))
        ep = opt["ep0"] if t == 0 else opt["ep"]
        zturn, kept = 0, []
        if last and opt["fin"]:
            PE("psV1", acc([(reg(7, 2), Rf("CI", k * N, k * N + N), Rf("X", L + k, 2 * L, 16)) for k in range(16)]))
            S("YO1", act(Rf("YO", 0, N), reg(7, 2), AF.Copy))
        for c in range(2):
            P["c"] = str(c)
            a, d0 = o + c * N, c * L
            z4 = Rf("Z4", (2 * t + c) * ZW, (2 * t + c) * ZW + 512)
            z = Rf("Z4", (2 * t + c) * ZW, (2 * t + c) * ZW + N)
            lane = lambda nm, ii: Rf(nm, d0 + ii, d0 + L, 16)
            pc = lambda nm, k=1: Rf(nm, k * c * N, k * c * N + k * N)
            th = pc("THA")
            hist = lambda out, m: [(out, Rf("SW", (2 * u + c) * N, (2 * u + c + 1) * N), M(m)) for u in range(t)]
            sums = lambda bank, j, nm, g8: [(Rf("ps%d" % bank, N * j + ii, N * j + N, 16), lane(nm, ii), Rf(g8, 0, 8)) for ii in range(16)]
            first = [len(P["tasks"]) + 1]
            j = 0
            for n in gs[c]:
                V("GS", tt(Rf("DS", d0 + N * j, d0 + N * (j + n)), ind(Xa, Rf("SU", a + 8 * j, a + 8 * (j + n))), Rf("Z4", z[1], z[1] + N * n), A.subtract))
                j += n
            hh, hs = opt["hh"][c], t == 0 and opt["h0"][c] == "S"
            for j in range(hh):
                x0, x1 = d0 + L // hh * j, d0 + L // hh * (j + 1)
                if hs:
                    S("H", act(Rf("HF", x0, x1), Rf("DS", x0, x1), AF.Relu, bias=0.0625, scale=-1.0))
                else:
                    V("H", ts(Rf("HS", x0, x1), Rf("DS", x0, x1), 127.9375, A.add, 128.0, A.min))
            bw = bk_["w"][c]
            PE2("psW", [(reg(bw, 0), th, M("HI"))] + hist(reg(bw, 0), "I32") + sums(bw, 0, "DS", "GH"), first)
            PE("psH", acc([(reg(bw, 1), M("CU" if hs else "CT"), ONE)] + (sums(bw, 1, "HF", "G32") if hs else sums(bw, 1, "HS", "GN"))))
            ni = pc("NI")
            par = (t % 2) * NA + c * N
            r, rho, q = Rf("RR", par, par + N), Rf("RP", par, par + N), Rf("QQ", par, par + N)
            V("NI", ts(ni, reg(bw, 1), 0.15625, A.add, -1024.0, A.max))
            V("RR", tt(r, ni, reg(bw, 0), A.is_lt))
            V("QQ", tt(q, ni, reg(bw, 1), A.is_lt))
            ge = opt["ge"][c]
            first = [len(P["tasks"])]
            for j in range(4):
                x0, x1 = d0 + 512 * j, d0 + 512 * j + 512
                eu = Rf("EU", a + 32 * j, a + 32 * j + 32)
                if ep[c][j] in "SC":
                    if ep[c][j] == "C":
                        V("GV", cp(Rf("DE", x0, x1), ind(Xa, eu)))
                    elif ge == 512:
                        S("GE", act(Rf("DE", x0, x1), ind(Xa, eu), AF.Copy))
                    elif j % 2 == 0:
                        S("GE", act(Rf("DE", x0, x1 + 512), ind(Xa, Rf("EU", a + 32 * j, a + 32 * j + 64)), AF.Copy))
                    zk = reg(bk_["z"][zturn % len(bk_["z"])], 0, 4)
                    zturn += 1
                    PE("psZ", acc([(zk, M("NIB"), z4), (zk, I, Rf("DE", x0, x1))]))
                    S("AE", act(Rf("AE", x0, x1), zk, AF.Abs))
                else:
                    V("GV", tt(Rf("DE", x0, x1), ind(Xa, eu), z4, A.subtract))
                    if ep[c][j] == "V":
                        S("AE", act(Rf("AE", x0, x1), Rf("DE", x0, x1), AF.Abs))
                    else:
                        V("AV", ts(Rf("AE", x0, x1), Rf("DE", x0, x1), 0.0, A.max, 2.0, A.mult))
            de = reg(4, c)
            part = lambda nm, g8, p0, p1: [(Rf("ps4", N * c + ii, N * c + N, 16), Rf(nm, d0 + ii + 16 * p0, d0 + 16 * p1, 16), Rf(g8, 0, 8), [p0, p1]) for ii in range(16)]
            it = [(de, th, M("NIB"))] + hist(de, "N64")
            for j in range(4):
                if ep[c][j] == "R":
                    it += part("DE", "GN", 32 * j, 32 * j + 32)
            if opt["dd"][c]:
                PE("psDa", acc(it + part("AE", "GS", 0, 96), stop=False), opens="ps4")
                PE("psD", acc(part("AE", "GS", 96, 128), start=False), closes="ps4")
            else:
                PE2("psD", it + sums(4, c, "AE", "GS"), first)
            if opt["rho"][c] == "S":
                S("RP", act(rho, de, AF.Sign, bias=2047.5, scale=-1.0))
                g1r, n4r = M("G1H"), M("N2")
            else:
                V("RP", ts(rho, de, 2047.5, A.is_lt, -0.5, A.add))
                g1r, n4r = M("G1"), M("N4")
            s16, e16 = Rf("S16", a, a + N), Rf("E16", a, a + N)
            k0, k1, k2 = reg(*bk_["k"][c]), reg(*bk_["k1"][c]), reg(*bk_["k2"][c])
            i = PE("psK0", acc([(k0, s16, I), (k0, M("G1"), r)]))
            PE2("psK1", [(k1, e16, I), (k1, M("G1H"), ONE), (k1, M("N4"), r), (k1, g1r, rho)], [i])
            wq = opt["w"][c]
            ws = [Rf("WF" if wq[j] == "S" else "WH", (2 * c + j) * N, (2 * c + j + 1) * N) for j in range(2)]
            for j, n in ((0, 2),) if len(wq) == 3 else ((0, 1), (1, 1)):
                x0, kk = (2 * c + j) * N, (k0, k1)[j]
                kk = Rf(kk[0], kk[1], kk[1] + n * N)
                if wq[j] == "S":
                    S("W" + "ab"[j], act(Rf("WF", x0, x0 + n * N), kk, AF.Relu, bias=-2048.0))
                else:
                    V("W" + "ab"[j], ts(Rf("WH", x0, x0 + n * N), kk, -4096.0, A.add, -2048.0, A.max))
            top = 2048.0 * (1 + 16 * wq[:2].count("V"))
            rest, nw = (4096.0, "NI32") if wq[0] == "S" else (2048.0, "NIB")
            kept.append((r, rho, q, n4r, s16, e16, ws[0], nw, rest))
            tops = [(ws[j], Rf("KS32", 0, 8) if wq[j] == "S" else KS) for j in range(2)] + [(I, Rf("W2", c * N, c * N + 8))]
            mc = opt["mc"]
            if c == 0 or not mc:
                n = 1 + mc
                j0 = k2[1] // N
                it = [(Rf(k2[0], k2[1], k2[1] + n * N), M("N2"), Rf("ONE", 0, n * N))]
                for h in range(4):
                    for b in range(2):
                        for gl in range(2):
                            x0 = 32 * h + 16 * gl
                            it.append((R2(k2[0], j0, j0 + n, 2 * h + b, N, 8), half(b, gl), R2("ET", 2 * t + c, 2 * t + c + n, x0, x0 + 16)))
                PE("psJ", acc(it, stop=False), opens=k2[0], extra=shut if bk_["k2"][0][0] == bk_["k2"][1][0] else None)
            if mc and c == 0:
                inner = PE("psK2", acc([(k2, r, M("N4")), (k2, rho, n4r)], start=False, stop=False), inside=k2[0])
                tops0 = tops
                continue
            PE("psK2", acc([(k2, r, M("N4")), (k2, rho, n4r)], start=False), closes=k2[0], extra=[inner] if mc else None)
            shut = [V("W2", ts(Rf("W2", (c - mc) * N, c * N + N), Rf(k2[0], k2[1] - mc * N, k2[2]), -2048.0, A.max))]
            if mc:
                pts = [Rf(k2[0], 2 * N + 8 * j, 2 * N + 8 * j + 8) for j in range(2)]
                PE("psT", acc([(pts[0],) + x for x in tops0]) + acc([(pts[1],) + x for x in tops]))
                V("LST", ts(R2("SU", 2 * t + 2, 2 * t + 4, 0, 8), Rf(k2[0], 2 * N, 2 * N + 16), top, A.add))
            else:
                pt = Rf(k1[0], k1[1], k1[1] + 8)
                PE("psT", acc([(pt,) + x for x in tops]))
                V("LST", ts(Rf("SU", a + NA, a + NA + 8), pt, top, A.add))
        for c in range(2):
            P["c"] = str(c)
            a, par, k0, rest = o + c * N, (t % 2) * NA + c * N, reg(*bk_["k"][c]), kept[c][8]
            z = Rf("Z4", (2 * t + c) * ZW, (2 * t + c) * ZW + N)
            lst = Rf("SU", a + NA, a + NA + 8)
            yd, y = Rf("YD", a, a + N), Rf("Y", a, a + N)
            fn = Rf(fb, a + NA, a + NA + N)
            if opt["yd"][c] == "V":
                V("YD", tt(yd, ind(Xa, lst), fn, A.subtract))
                S("Y", act(y, yd, AF.Abs, bias=fo))
            else:
                xt = Rf("XT", c * N, c * N + N)
                S("YD", act(xt, ind(Xa, lst), AF.Copy))
                PE("psB", acc([(k0, M("NIB"), fn), (k0, I, xt)]))
                S("Y", act(y, k0, AF.Abs, bias=fo))
            if not last:
                for b in (2 * c, 2 * c + 1):
                    src = Rf("Y", o + NB * b, o + NB * b + NB)
                    x0 = (2 * t + 2 + c) * ZW + NB * (b % 2)
                    dst = Rf("Z4", x0, x0 + NB)
                    if (b + t) % 4:
                        i = G("send", [("send", dict(in_=src, to=["Z4", x0], t=t, b=b))], dur=0.3, sem="none")
                        add(P, "N", "recv", [], wr=[dst], dur=EST["net"], sem="za%d%d" % (t + 1, b), inc=0, extra=[i])
                    else:
                        add(P, "Y", "stay", [("copy", dict(out=dst, in_=src))], dur=0.1, sem="za%d%d" % (t + 1, b), inc=16, prio=2.2)
            xn = reg(*bk_["xn"][c])
            PE("psN", acc([(xn, I, z), (xn, I, y)]))
            if opt["xn"][c] == "V":
                V("XM", ts(Rf("XM", c * N, c * N + N), xn, 0.4995, A.mult, 12582912.0, A.add))
                V("XN", ts(Rf("XB", a, a + N), Rf("XM", c * N, c * N + N), -12582912.0, A.add))
            elif opt["xn"][c] == "I":
                V("XN", ts(Rf("XN", a, a + N), xn, 0.5, A.mult, -0.25, A.add))
            elif opt["xn"][c] == "J":
                S("XM", act(Rf("XM", c * N, c * N + N), xn, AF.Identity, bias=12582912.0, scale=0.4995))
                V("XN", ts(Rf("XN", a, a + N), Rf("XM", c * N, c * N + N), -12582912.0, A.add))
            else:
                S("XM", act(Rf("XM", c * N, c * N + N), xn, AF.Identity, bias=12582912.0, scale=0.4995))
                S("XN", act(Rf("XB", a, a + N), Rf("XM", c * N, c * N + N), AF.Identity, bias=-12582912.0))
            if split or c == 1:
                c0 = c if split else 0
                l0, l1 = 16 * t + 8 * c0, 16 * t + 8 * c + 8
                py = Rf("ps%d" % opt["yb"], 3 * N + 8 * c0, 3 * N + 8 * c + 8)
                W = lambda nm: Rf(nm, l0, l1)
                it = [(py, sel(m), Rf("Y", o + c0 * N + m, a + N, 16)) for m in range(16)]
                if opt["pi"] == 4:
                    PE("psY", acc(it))
                    V("PI1", cp(W("PI1"), py))
                    V("PI2", ts(W("PI2"), W("PI1"), 15, A.bitwise_and))
                    V("PI3", tt(W("PI3"), W("PI2"), Rf("BASE", 0, l1 - l0), A.add))
                    V("PLC", cp(W("PLC"), W("PI3")))
                else:
                    pz = Rf("ps4", 2 * N, 2 * N + l1 - l0)
                    i = PE("psY", acc(it))
                    V("PI1", ts(W("PH"), py, 16392.5, A.add))
                    PE("psL", acc([(pz, I, Rf("BH", 0, l1 - l0))] + [(pz,) + x[1:] for x in it], stop=False), opens="ps4", extra=[i])
                    PE("psL", acc([(pz, M("NIB"), W("PH"))], start=False), closes="ps4")
                    V("PLC", cp(W("PLC"), pz))
            if c == 1 or not opt["me"]:
                c0 = 0 if opt["me"] else c
                cs, n, x0 = range(c0, c + 1), c + 1 - c0, o + NA + c0 * N
                bank, j0 = opt["cn"][c]
                sw = Rf("SW", (2 * t + c0) * N, (2 * t + c + 1) * N)
                PE("psC", [m for j in cs for m in acc([(reg(bank, j0 + j - c0), kept[j][0], M("N4")), (reg(bank, j0 + j - c0), kept[j][1], kept[j][3])])])
                S("SW", act(sw, reg(bank, j0, n), AF.Relu, bias=-7.0, scale=1.0 / 4096))
                if not last:
                    en = Rf("E16", x0, x0 + n * N)
                    PE("psE", acc([(reg(bank, j0, n), I, Rf("E16", x0 - NA, x0 - NA + n * N)), (reg(bank, j0, n), M("NK4"), sw)]))
                    V("E16", tt(en, Rf("W2", c0 * N, c * N + N), reg(bank, j0, n), A.max))
                    V("EU", ts(Rf("EU", x0, x0 + n * N), en, 2048.0, A.add))
            if c == 1 or not opt["ms"]:
                c0 = 0 if opt["ms"] else c
                cs, n, x0 = range(c0, c + 1), c + 1 - c0, o + NA + c0 * N
                (bq, jq), (bx, jx), (bm, jm), (bs, js) = opt["sb"][c]
                both = lambda nm, k=1: Rf(nm, k * c0 * N, k * (c + 1) * N)
                one = lambda nm, j: Rf(nm, j * N, j * N + N)
                PE("psQ", acc([(reg(bq, jq, n), M("SM"), Rf("RR", par - (c - c0) * N, par + N)), (reg(bq, jq, n), M("Q256"), Rf("QQ", par - (c - c0) * N, par + N))]))
                S("MS", act(both("MS"), reg(bq, jq, n), AF.Sign, bias=-256.5))
                ins = []
                for j in cs:
                    b1, b2 = reg(bx, jx + 2 * (j - c0)), reg(bx, jx + 2 * (j - c0) + 1)
                    ins += acc([(b1, kept[j][4], I), (b1, M("NQ"), one("MS", j))]) + acc([(b2, kept[j][5], I), (b2, M("PQ"), one("MS", j))])
                PE("psX", ins)
                V("SE", ts(both("SE", 2), reg(bx, jx, 2 * n), -2048.0, A.add, -2048.0, A.max))
                PE("psM", [m for j in cs for m in acc([(reg(bm, jm + j - c0), I, one("SE", 2 * j)), (reg(bm, jm + j - c0), I, one("SE", 2 * j + 1)),
                                                      (reg(bm, jm + j - c0), M("NLI"), kept[j][0])])])
                if opt["mm"] == "V":
                    mm_, shi = "MM", "SHI"
                    V("MM", ts(both("MM"), reg(bm, jm, n), 2048.0, A.add, -2048.0, A.max))
                else:
                    mm_, shi = "MF", "SH32"
                    S("MM", act(both("MF"), reg(bm, jm, n), AF.Relu, bias=4096.0))
                ins, i8 = [], Rf("WI", 24, 16 + N)
                for j in cs:
                    sn = Rf("ps%d" % bs, (js + j - c0) * N + 8, (js + j - c0 + 1) * N)
                    ins += acc([(sn, one("SE", 2 * j), i8), (sn, one("SE", 2 * j + 1), i8), (sn, kept[j][6], Rf(kept[j][7], 8, N)), (sn, one(mm_, j), Rf(shi, 8, N))])
                PE("psS", ins)
                V("SU", ts(R2("SU", 2 * t + 2 + c0, 2 * t + 3 + c, 8, N), R2("ps%d" % bs, js, js + n, 8, N), rest, A.add))
                V("S16", ts(Rf("S16", x0, x0 + n * N), Rf("SU", x0, x0 + n * N), -2048.0, A.add))
                if last:
                    bk = "ps%d" % bk_["o"][c]
                    it = [(reg(bk_["o"][c], 0, n), M("PQ"), Rf("ONE", 0, n * N))]
                    for h in range(4):
                        for gl in range(2):
                            for b in range(2):
                                it.append((R2(bk, 0, n, 32 * h + 16 * gl, 32 * h + 16 * gl + 16), half(gl, b), R2("S16", 2 * NT + c0, 2 * NT + c + 1, 2 * h + b, N, 8)))
                    PE("psO", acc(it))
                    V("YS", tr(both("YSO"), reg(bk_["o"][c], 0, n)))
        if last and opt["fin"]:
            y, pa, pb = Rf("Y", o + N, o + NA), reg(6, 2), reg(5, 0)
            P["c"] = "1"
            i = PE("psR", acc([(pa, M("OB"), y)]))
            V("XH", ts(Rf("XH", 0, N), pa, 16392.5, A.add))
            PE("psI", acc([(pb, M("CV"), ONE), (pb, M("OB"), y)], stop=False), opens="ps5", extra=[i])
            PE("psI", acc([(pb, M("NIB"), Rf("XH", 0, N))], start=False), closes="ps5")
            V("XD", tt(Rf("XT", 0, N), ind(Rf("X", L, 2 * L), Rf("PLC", 16 * t + 8, 16 * t + 16)), Rf("XB", o + N, o + NA), A.subtract))
            V("XP", tt(Rf("YD", 0, N), Rf("XT", 0, N), pb, A.mult))
            V("YX", tt(Rf("YXO", N, NA), Rf("YO", 0, N), Rf("YD", 0, N), A.subtract))
        for c in (range(2 - (last and opt["fin"])) if split else (None,)):
            lo, hi = (0, 2) if c is None else (c, c + 1)
            P["c"] = str(hi - 1)
            V("SC", cp(ind(Rf("X", lo * L, hi * L), Rf("PLC", 16 * t + 8 * lo, 16 * t + 8 * hi)), Rf("XN" if opt["xn"][lo] in "IJ" else "XB", o + lo * N, o + hi * N)))
    P["c"] = ""
    for lo, hi in ((0, NT - 1), (NT - 1, NT)):
        V("PT", tt(Rf("PT", 16 * lo, 16 * hi), Rf("UH", 16 * lo, 16 * hi), Rf("TC", 16 * lo, 16 * hi), A.add))
        V("PV", tt(Rf("PV", 16 * lo, 16 * hi), Rf("PT", 16 * lo, 16 * hi), R2("SW", 2 * lo, 2 * hi, 0, 8), A.mult))
    V("PW", tt(Rf("PW", 0, 32), Rf("PV", 0, 32), Rf("PV", 32, 64), A.max))
    V("PW", tt(Rf("PW", 32, 48), Rf("PV", 64, 80), Rf("P0", 0, 16), A.max))
    V("PW", tt(Rf("PW", 48, 64), Rf("PW", 0, 16), Rf("PW", 16, 32), A.max))
    V("PW", tt(Rf("PW", 64, 80), Rf("PW", 32, 48), Rf("PW", 48, 64), A.max))
    V("PW", tt(Rf("PW", 80, 96), Rf("PW", 64, 80), Rf("PV", 80, 96), A.max))
    V("PW", ts(Rf("PW", 96, 112), Rf("PW", 80, 96), 4095, A.bitwise_and))
    pa = Rf("ps4", 0, 16)
    PE("psP", acc([(pa, M("K4"), R2("SW", 2 * t, 2 * t + 2, 0, 8)) for t in range(NT)]))
    V("YP", tt(Rf("YPO", 0, 16), Rf("PW", 96, 112), pa, A.add))
    if fo:
        V("YF", ts(Rf("FB", NT * NA, NT * NA + NA), Rf("F16", NT * NA, NT * NA + NA), -1024.0, A.add))
    for c in range(2 - opt["fin"]):
        P["c"] = str(c)
        PE("psV", acc([(reg(c, 0), Rf("CI", k * N, k * N + N), Rf("X", c * L + k, c * L + L, 16)) for k in range(16)]))
        S("YX", act(Rf("YXO", c * N, c * N + N), reg(c, 0), AF.Copy))
    for k, (o_, b) in enumerate((("yf", Rf("FB", NT * NA, NT * NA + NA)), ("yp", Rf("YPO", 0, 16)), ("ys", Rf("YSO", 0, NA)), ("yx", Rf("YXO", 0, NA)))):
        add(P, "Y", "st" + o_, [("store", dict(dst=o_, in_=b))], dur=0.1, sem="ost%d" % k, inc=16, prio=2.0)
    return P


def schedule(P, e=None, up=None, turn=None, turn0=None):
    e = e or EST
    up = UP if up is None else up
    turn = TURN if turn is None else turn
    turn0 = TURN0 if turn0 is None else turn0
    T = P["tasks"]
    n = len(T)
    succ = [[] for _ in range(n)]
    for t in T:
        t["dur"] = duration(t["q"], t["ins"], e) if t["fix"] is None else t["fix"]
        for o, kind in t["pre"].items():
            succ[o].append((t["i"], kind))

    def lat(o, i, kind):
        a, b = T[o], T[i]
        if kind == "time":
            return 0.0
        if a["inc"] == 16:
            return a["prio"]
        if a["q"] == b["q"]:
            return 0.0 if a["q"] == "P" else e["self_"]
        return e["lat"]
    far = [0.0] * n
    for i in range(n - 1, -1, -1):
        far[i] = T[i]["dur"] + max([lat(i, j, k) + far[j] for j, k in succ[i]] or [T[i]["prio"]])
    for i in range(n):
        far[i] += up.get(T[i]["label"], 0.0)
    ready = [0.0] * n
    left = [len(t["pre"]) for t in T]
    free = {}
    avail = {}
    for t in T:
        free.setdefault(t["q"], 0.0)
        avail.setdefault(t["q"], [])
    for i in range(n):
        if left[i] == 0:
            avail[T[i]["q"]].append(i)
    order, start = [], [0.0] * n
    held = {}
    opened = set()

    def er(i):
        r = ready[i]
        for b in T[i]["banks"]:
            if b in opened and T[i]["q"] == "P" and T[i].get("closes") != b:
                return 1e9
            for q2, (e2, o2) in held.get(b, {}).items():
                if q2 != T[i]["q"] and e2 + e["lat"] > r:
                    r = e2 + e["lat"]
        return r
    byname, seq = {}, {q: [] for q in free}
    for t in T:
        byname.setdefault((t["t"], t["q"], t["label"]), []).append(t["i"])
    for t in range(NT):
        for q, names in (turn0 if t == 0 else turn if t < NT - 1 else LAST).items():
            for nm in names.split():
                lst = byname.get((t - 1, q, nm[1:]) if nm[0] == "-" else (t, q, nm))
                if lst:
                    seq[q].append(lst.pop(0))
    named = {i for q in seq for i in seq[q]}
    at = {q: 0 for q in seq}
    while len(order) < n:
        best = None
        for q, lst in avail.items():
            nxt = seq[q][at[q]] if at[q] < len(seq[q]) else None
            lst = [j for j in lst if j == nxt or j not in named]
            if not lst:
                continue
            s = min(er(i) for i in lst)
            if q != "N":
                s = max(free[q], s)
            if best is None or s < best[0]:
                best = (s, q, lst)
        if best is None or best[0] > 1e8:
            k, q, j = min((seq[q].index(j) - at[q], q, j) for q in avail for j in avail[q] if j in named and er(j) < 1e8)
            seq[q].remove(j)
            seq[q].insert(at[q], j)
            P.setdefault("moved", []).append(T[j]["label"])
            continue
        s, q, lst = best
        if q == "N":
            i = min(avail[q], key=lambda j: ready[j])
            s = ready[i]
        else:
            c = [j for j in lst if er(j) <= s + 0.03]
            d = [j for j in c if T[j]["inc"] == 16]
            i = min(d) if d else max(c, key=lambda j: far[j])
            s = max(free[q], er(i))
        if "closes" in T[i]:
            opened.discard(T[i]["closes"])
        if "opens" in T[i]:
            opened.add(T[i]["opens"])
        avail[q].remove(i)
        at[q] += i in named
        start[i] = s
        end = s + T[i]["dur"]
        for b in T[i]["banks"]:
            for q2, (e2, o2) in held.get(b, {}).items():
                if q2 != q:
                    T[i]["pre"][o2] = "raw"
            held.setdefault(b, {})[q] = (end, i)
        if q != "N":
            free[q] = end
        order.append(i)
        for j, kind in succ[i]:
            x = end + lat(i, j, kind)
            if x > ready[j]:
                ready[j] = x
            left[j] -= 1
            if left[j] == 0:
                avail[T[j]["q"]].append(j)
    return order, start, max(start[i] + T[i]["dur"] + T[i]["prio"] for i in range(n))


CACHE = {}


def plan():
    if "p" not in CACHE:
        P = build()
        CACHE["p"] = (P, schedule(P))
    return CACHE["p"]


def rank_program(g, core, T, topo):
    rank = T.rank_of(core)
    if rank is None:
        return
    P, (order, start, length) = plan()
    tasks = P["tasks"]
    queues = {"V": g.vector, "S": g.scalar, "P": g.tensor, "G": g, "Y": g.sync}
    clock = {q: {} for q in queues}
    total = {}
    info = {}

    def ap(v, p0=0, p1=128):
        if not isref(v):
            return v
        if v[0] == "#":
            return ap(v[1]).indirect(ap(v[2]))
        b = T[v[0]]
        if len(v) == 6:
            return b[p0:p1, v[4]:v[5], v[1]:v[2]:v[3]]
        sh = SCRATCH[v[0]][1]
        if len(sh) == 2:
            return b[p0:p1, v[1]:v[2]:v[3]]
        w = sh[2]
        o = v[1] // w
        if v[2] <= o * w + w:
            return b[p0:p1, o, v[1] - o * w:v[2] - o * w:v[3]]
        return b[p0:p1, o:v[2] // w, :]

    def lanes(src, dst):
        return topo.engines(src, dst)[::2]
    nloc = 0
    for i in order:
        t = tasks[i]
        q = t["q"]
        if q == "N":
            tt_, b = int(t["sem"][2]), int(t["sem"][3])
            e = len(lanes(T.cores[(rank - b - (tt_ - 1)) % 4], core))
            info[i] = (t["sem"], e, {t["sem"]: e})
            total[t["sem"]] = e
            continue
        eng = queues[q]
        ck = clock[q]
        need = {}
        for o, kind in t["pre"].items():
            if kind == "time" or (tasks[o]["q"] == q and q == "P") or o not in info:
                continue
            sem, val, know = info[o]
            if ck.get(sem, 0) < val and need.get(sem, (0,))[0] < val:
                need[sem] = (val, know)
        for sem in sorted(need):
            val, know = need[sem]
            if any(o2 != sem and k2.get(sem, 0) >= val for o2, (v2, k2) in need.items()):
                continue
            eng.wait_ge(T.sem[sem], val)
        for sem, (val, know) in need.items():
            for s2, v2 in know.items():
                if ck.get(s2, 0) < v2:
                    ck[s2] = v2
        if t["name"] == "send":
            kw = t["ins"][0][1]
            dst = T.cores[(rank + kw["b"] + kw["t"]) % 4]
            rid, pid, _s = topo.addr(dst)
            e = lanes(core, dst)
            o = kw["to"][1]
            g.remote_dma(ap(Rf("Z4", o, o + NB)), ap(kw["in_"]), T.sem["za%d%d" % (kw["t"] + 1, kw["b"])], T.sem["lsent"], pid, rid, sum(1 << x for x in e))
            nloc += len(e)
            continue
        if t["inc"] == 16:
            m, kw = t["ins"][0]
            if m == "dma":
                s = kw["src"]
                h = eng.dma_start(ap(kw["out"]), T[s[0]][:, s[1]:s[2]])
            elif m == "copy":
                h = eng.dma_start(ap(kw["out"]), ap(kw["in_"]))
            else:
                h = eng.dma_start(T[kw["dst"]][:, 0:cnt(kw["in_"])], ap(kw["in_"]))
            h.then_inc(T.sem[t["sem"]], 16)
            know = dict(ck)
            know[t["sem"]] = 16
            total[t["sem"]] = 16
            info[i] = (t["sem"], 16, know)
            continue
        sem = QS[q]
        for j, (m, kw) in enumerate(t["ins"]):
            a = {k: ap(v) for k, v in kw.items()}
            if m == "matmul":
                h = eng.matmul(ap(kw["out"], *kw["part"]), a["lhsT"], a["rhs"], a["start"], a["stop"])
            elif m == "iota":
                flag = {} if SCRATCH[kw["out"][0]][2] == "int32" else {"allow_small_or_imprecise_dtypes": True}
                h = eng.iota(a["out"], a["pattern"], a["base"], a["channel_multiplier"], **flag)
            elif m == "affine" and "op" in kw:
                h = eng.affine_select(out=a["out"], in_=a["in_"], pattern=kw["pattern"], compare_op=kw["op"], fill=kw["fill"], base=0, channel_multiplier=-1)
            elif m == "affine":
                h = eng.affine_select(out=a["out"], in_=a["in_"], pattern=[[0, cnt(kw["in_"])]], compare_op=A.is_gt, fill=0.0, base=1, channel_multiplier=0)
            elif m == "memset":
                h = eng.memset(a["ap"], a["constant"])
            elif m == "vtranspose":
                h = eng.transpose(a["out"], a["in_"])
            elif m == "tensor_copy":
                h = eng.tensor_copy(**a)
            elif m == "tensor_tensor":
                h = eng.tensor_tensor(**a)
            elif m == "tensor_scalar":
                h = eng.tensor_scalar(**a)
            else:
                h = eng.activation(**a)
            if j == len(t["ins"]) - 1:
                h.then_inc(T.sem[sem], 1)
        total[sem] = total.get(sem, 0) + 1
        know = dict(ck)
        know[sem] = total[sem]
        info[i] = (sem, total[sem], know)
    g.wait_ge(T.sem.lsent, nloc)
    for sem in sorted(total):
        if all(ck.get(sem, 0) < total[sem] for ck in clock.values()):
            g.wait_ge(T.sem[sem], total[sem])
